import numpy as np, ml_dtypes
CORES = [51,54,179,182]
N = 4
BF = ml_dtypes.bfloat16
def gentries(a):
    return np.ascontiguousarray(a.reshape(8, 16, -1).transpose(0, 2, 1)).reshape(8, -1)
def gtable(e):
    e = np.asarray(e); return np.ascontiguousarray(e.reshape(8, -1, 16).transpose(0, 2, 1)).reshape(128, -1).astype(np.int32)
V, P, XC, B, RO = 256, 512, 4096, 8, 3
E = 16 * V
def place_record(n, a, p, t):
    return ((n * (2 * a + 1) >> 4) + n + 37 * p + 77 * t) & (XC - 1)
def seat(rng, ln, key=None, mix=True, pair=False):
    oc = np.full((N, 8, E), P, np.int64); qs = np.full((N, 8, 16 * P), E, np.int64)
    for r in range(N):
        for g in range(8):
            at = np.flatnonzero((np.arange(16) < ln[r, g][:, None]).reshape(-1))
            if pair and g & 1: at = at[np.argsort(2 * np.minimum(at, at ^ (16 * B)) + (at > (at ^ (16 * B))))]
            s = rng.permutation(16 * P) if key is None else np.argsort(key[r, g].reshape(-1))
            s = s[:len(at)]
            if mix: s = rng.permutation(s)
            oc[r, g, at] = s >> 4; qs[r, g, s] = at
    return oc, qs
def put(oc, qs, r, g, s, n):
    b = int(np.flatnonzero(qs[r, g] == n)[0]); m = int(qs[r, g, s])
    qs[r, g, s] = n; qs[r, g, b] = m; oc[r, g, m] = b >> 4; oc[r, g, n] = s >> 4
def aim(w, y, u):
    i = np.arange(1, 16)[:, None]
    w[0] = (u - np.sum(16 * i * w[1:] + np.minimum(w[1:], y[1:, None]), axis=0)) & (V - 1)
def pack(x, want, oc, qs, th):
    return {"x": np.ascontiguousarray(x.reshape(N, 128, XC)).astype(np.float32).astype(BF), "want": np.stack([want.reshape(128, P)] * N).astype(np.float32).astype(BF),
            "oc": np.stack([gtable(a) for a in oc]), "qs": np.stack([gtable(a) for a in qs]), "th": np.repeat(th, 16, axis=1).reshape(N, 128, 1).astype(np.int32)}
def goods(rng):
    return rng.integers(0, 256, (N, 8, 16, XC)), rng.integers(0, 256, (8, 16, P))
def setup_inputs(rng):
    x, want = goods(rng); oc, qs = seat(rng, rng.integers(8, 17, (N, 8, V)))
    return pack(x, want, oc, qs, rng.integers(450, 901, (N, 8)))
def setup_inputs_alike(rng):
    x, want = goods(rng); ln = rng.choice(np.array([16, 16, 8, 3, 12]), (N, 8, V))
    ln[:, 2] = 16; ln[:, 4] = rng.integers(12, 16, (N, V)); ln[:, 6] = rng.integers(12, 16, (N, V)); ln[:, 6, 1] = 16; ln[N - 1, 6, V - 1] = 15
    key = rng.random((N, 8, P, 1)) + 0.0001 * rng.random((N, 8, P, 16))
    oc, qs = seat(rng, ln, key, False, True)
    want[3] = want[3][:, :1]; x[N - 1, 5] = x[N - 1, 5] >> 1
    key = rng.random((N, 8, P, 16)); one = np.arange(16) == rng.integers(0, 16, (N, P, 1))
    key[:, 4] = np.where(one, -1, np.where(np.roll(one, 1, axis=2), 9, key[:, 4]))
    key[:, 6, 1:N + 1] = 9; key[:, 6, P - 1] = 9; key[N - 1, 6, P - 1, :15] = -1
    for r in range(N): key[r, 6, r + 1, r] = -1
    oc2, qs2 = seat(rng, ln, key)
    oc[:, 2:7:2] = oc2[:, 2:7:2]; qs[:, 2:7:2] = qs2[:, 2:7:2]
    n = np.arange(E); m = n ^ (16 * B)
    for r in range(N):
        a = np.where((n & 15) == 0, n >> 4, np.roll(oc[r, 2], 1)); c = place_record(m, a[m], oc[r, 2], 0)
        y = x[r, 2] >> 1; y[:, c] = y[:, c] | 128; x[r, 2] = y
        put(oc, qs, r, 6, 16 * (r + 1) + r, 128)
    for k in range(15): put(oc, qs, N - 1, 6, 16 * (P - 1) + k, E - 16 + k)
    y = rng.integers(0, 256, 16); y[0] = 255; x[:, 4] = y[:, None]; want[4] = want[4][:, :1]; aim(want[4], y, 0)
    u = 2 + rng.integers(0, V - 3, P); u[1:N + 1] = 1; u[P - 1] = V - 1
    x[:, 6] = 255; aim(want[6], np.full(16, 255), u)
    th = rng.integers(600, 1500, (N, 8)); th[:, 2] = 4080
    return pack(x, want, oc, qs, th)
def setup_inputs_ties(rng):
    x, want = goods(rng); x = 85 * (x >> 6); want = 85 * (want >> 6)
    oc, qs = seat(rng, rng.integers(8, 17, (N, 8, V)))
    for a in (x, oc, qs): a[:, ::2] = a[:1, ::2]
    x[0, 2] = np.minimum(x[0, 2], 170); x[0, 6] = np.minimum(x[0, 6], 170)
    return pack(x, want, oc, qs, 85 * rng.integers(4, 11, (N, 8)) - rng.integers(0, 2, (N, 8)))
def setup_inputs_corners(rng):
    x, want = goods(rng); ln = rng.choice(np.array([0, 1, 15, 16]), (N, 8, V))
    kind = rng.random((N, 8, 1, XC)); x = np.where(kind < 0.4, 255, np.where(kind < 0.5, 0, x))
    cls = rng.integers(0, 4, (8, 1, P)); kind = rng.random((8, 1, P)); many = np.full((8, 16, P), 255); many[:, 1:2] = 255 - cls
    want = np.where(kind < 0.6, many, np.where(kind < 0.7, 0, want))
    want[7, :, ::16] = 255; want[7, 7, ::16] = 254
    for g in range(8):
        x[:g % N, g, 0] = np.minimum(x[:g % N, g, 0], 254)
        for c in range(4): ln[:, g, (16 * 120 * 255 + 4080 - 17 * c) & (V - 1)] = (15, 0, 16, 1)[(g + c) & 3]
    ln[:, 7, V - 1] = 15; ln[:, 0, V - 1] = 16; ln[:, 7, 0] = 16
    c = rng.integers(0, 5, (N, 8, P, 1)); c[:, :, 4::9] = 3
    one = np.arange(16) == rng.integers(0, 16, (N, 8, P, 1))
    key = rng.random((N, 8, P, 1)) + 0.0001 * rng.random((N, 8, P, 16))
    key = key + np.where(c == 0, 0, np.where(c == 1, np.where(one, 3, 0), np.where(c == 2, np.where(one, -3, 3), np.where(c == 3, 6, 1))))
    key[N - 1, 7, 0] = np.where(np.arange(16) < 15, -1, 9)
    oc, qs = seat(rng, ln, key)
    th = rng.choice(np.array([0, 1, 1000, 2000, 4080]), (N, 8)); th[:, ::2] = 4080; th[:, 5] = 4079; th[:, 7] = 4080
    return pack(x, want, oc, qs, th)
def setup_inputs_ends(rng):
    v = np.arange(V); low = np.minimum(v, v ^ B)
    ln = np.where((rng.random((N, 8, V)) < 0.35)[..., low], 16, 0)
    for q in (0, V - 1): ln[..., q] = 16; ln[..., q ^ B] = 16
    who = rng.random((N, 8, P, 1)); who[:, :, 0] = -1; who[:, :, P - 1] = -1
    oc, qs = seat(rng, ln, who + 0.0001 * rng.random((N, 8, P, 16)))
    kind = rng.random((8, 1, P)); want = np.where(kind < 0.25, 255, np.where(kind < 0.4, 0, 255 * rng.integers(0, 2, (8, 16, P))))
    want[:, :, 0] = 255; want[:, :, P - 1] = 255; want[:, :, P // 2] = 0; want[:, :, P - 2] = 0
    kind = rng.random((N, 8, 1, XC)); x = np.where(kind < 0.3, 255, np.where(kind < 0.45, 0, 255 * rng.integers(0, 2, (N, 8, 16, XC))))
    x[..., 0] = 255; x[..., XC - 1] = 255
    for r in range(N):
        for g in range(8):
            put(oc, qs, r, g, 16 * P - 1, E - 1); put(oc, qs, r, g, 0, 0)
            x[r, g, :, int(place_record(E - 1, int(oc[r, g, E - 2]), P - 1, 0))] = 255
    th = np.where(rng.random((N, 8)) < 0.3, 0, 4080); th[:, 0] = 4080; th[:, 1] = 0; th[:, 7] = 4080
    return pack(x, want, oc, qs, th)
def setup_inputs_spread(rng):
    x = np.minimum((np.exp2(8 * rng.random((N, 8, 1, XC))) * rng.random((N, 8, 16, XC))).astype(np.int64), 255)
    want = np.minimum((np.exp2(2 + 6 * rng.random((8, 1, P))) * rng.random((8, 16, P))).astype(np.int64), 255)
    ln = np.minimum((17 * rng.random((N, 8, V)) ** rng.choice(np.array([0.3, 0.6, 1.0, 2.0]), (N, 8, 1))).astype(np.int64), 16)
    oc, qs = seat(rng, ln)
    return pack(x, want, oc, qs, np.minimum(np.exp2(12 * rng.random((N, 8))).astype(np.int64), 4080))
def check_inputs(d):
    bad = []
    for k, hi in (("x", 255), ("want", 255), ("oc", P), ("qs", E), ("th", 4080)):
        a = np.asarray(d[k]).astype(np.float64)
        if not np.all((a >= 0) & (a <= hi)): bad.append("range of " + k)
        elif not np.all(a == np.floor(a)): bad.append("whole numbers of " + k)
    w = np.asarray(d["want"]).astype(np.float32)
    if not np.all(w == w[:1]): bad.append("want alike on all ranks")
    t = np.asarray(d["th"]).reshape(N, 8, 16)
    if not np.all(t == t[:, :, :1]): bad.append("th alike in the rows of a group")
    if "range of oc" in bad or "range of qs" in bad: return bad
    o = np.stack([gentries(a) for a in d["oc"]]).astype(np.int64); q = np.stack([gentries(a) for a in d["qs"]]).astype(np.int64)
    b = (o < P).reshape(N, 8, V, 16)
    if np.any(b[..., 1:] & ~b[..., :-1]): bad.append("queues of oc without gaps")
    ok = True; person = np.arange(16 * P) >> 4
    for r in range(N):
        for g in range(8):
            n = np.bincount(q[r, g], minlength=E + 1)[:E]; back = np.full(E + 1, P, np.int64); back[q[r, g]] = person
            ok = ok and np.array_equal(n, (o[r, g] < P).astype(n.dtype)) and np.array_equal(back[:E], o[r, g])
    if not ok: bad.append("every occupied place of oc in just one slot of qs, of its person")
    return bad
def reference(x, want, oc, qs, th):
    xs = x.astype(np.float32).astype(np.int32).reshape(N, 8, 16, XC); ws = want.astype(np.float32).astype(np.int32).reshape(N, 8, 16, P)
    wp = np.concatenate([ws, np.zeros((N, 8, 16, 1), np.int32)], axis=3); wsum = np.add.reduce(16 * np.arange(16)[:, None] * ws.astype(np.int64), axis=2)
    o = np.stack([gentries(a) for a in oc]).astype(np.int64)
    q = np.stack([gentries(a) for a in qs]).astype(np.int64)
    lim = th.astype(np.int64).reshape(N, 8, 16)[:, :, :1]
    n = np.arange(E); mate = n ^ (16 * B); v = n >> 4; head = (n & 15) == 0; none = np.full((N, 8, 1), E, np.int64)
    for t in range(RO):
        occ = o < P; ahead = np.where(head, v, np.roll(o, 1, axis=2))
        w = np.take_along_axis(wp, o[:, :, None, :], 3)
        own = np.add.reduce(np.minimum(np.take_along_axis(xs, place_record(n, ahead, o, t)[:, :, None, :], 3), w), axis=2).astype(np.int64)
        other = np.add.reduce(np.minimum(np.take_along_axis(xs, place_record(mate, ahead[..., mate], o, t)[:, :, None, :], 3), w), axis=2).astype(np.int64)
        swap = occ & occ[..., mate] & (other + other[..., mate] > own + own[..., mate])
        o2 = np.where(swap, o[..., mate], o); c = np.where(swap, other[..., mate], own)
        qd = np.take_along_axis(np.concatenate([np.where(swap, mate, n), none], axis=2), q, 2)
        best = np.max(np.take_along_axis(np.concatenate([c, np.full((N, 8, 1), -1, np.int64)], axis=2), qd, 2).reshape(N, 8, P, 16), axis=3)
        top = np.max(best, axis=0); holder = np.argmax(best, axis=0)
        tp = np.concatenate([np.broadcast_to(top, (N, 8, P)), np.zeros((N, 8, 1), np.int64)], axis=2)
        go = (c < np.take_along_axis(tp, o2, 2) - lim) | (head & ((v & 7) == t))
        stay = (occ & ~go).astype(np.int64).reshape(N, 8, V, 16)
        to = np.where(stay == 1, 16 * np.arange(V)[:, None] + np.add.accumulate(stay, axis=3) - stay, E).reshape(N, 8, E)
        o = np.full((N, 8, E + 1), P, np.int64); np.put_along_axis(o, to, o2, 2); o = np.ascontiguousarray(o[..., :E])
        q = np.take_along_axis(np.concatenate([to, none], axis=2), qd, 2)
        ln = np.add.reduce(stay, axis=3); empty = q.reshape(N, 8, P, 16) == E; u = (wsum + top) & (V - 1)
        for r in range(N):
            for g in range(8):
                p = np.flatnonzero(np.any(empty[r, g], axis=1) & (top[g] >= 0) & (holder[g] == r)); p = p[ln[r, g, u[r, g, p]] < 16]
                k, i = np.unique(u[r, g, p], return_index=True); p = p[i]; at = 16 * k + ln[r, g, k]
                o[r, g, at] = p; q[r, g, 16 * p + np.argmax(empty[r, g, p], axis=1)] = at
    return {"yoc": np.stack([gtable(a) for a in o]).astype(np.float32), "yq": np.stack([gtable(a) for a in q]).astype(np.float32)}

@@ -1,0 +1,709 @@
+import math
+from concourse.bass import DstId, RemoteDMATransfer
+from concourse.mybir import dt, AluOpType as Op, ActivationFunctionType as Act
+
+LN2 = math.log(2.0)
+BF, F4, FH, I4, U2 = "bfloat16", "float32", "float16", "int32", "uint16"
+WIDTH = {}
+WHERE = {}
+SCRATCH = {}
+
+
+def _decl(dtype, spec):
+    pool, at = "pool_" + dtype, 0
+    for item in spec.split():
+        n, w = item.split(":")
+        WIDTH[n] = int(w)
+        WHERE[n] = (pool, at)
+        at += (int(w) + 15) // 16 * 16
+    SCRATCH[pool] = ("sbuf", [128, at], dtype)
+
+
+_decl(BF, "XT:4096 WT:768 MT:768 T2:528 WG:4096 D0:4096 D1:4096 MG:4096 ZRO:2112 WDS:4112 WDE:4112 GS:8448 GE:8448 "
+          "EZ:144 EZ4:144 EZM:144 EZW:144 INB:128 ULB:32 BO:128 BOP:128 IB:128 IBIG:128 I8K:128 TRI:128 TRQ:128 TRN:128 NLQ:128 NLN:128 "
+          "RS:8 RW:8 CADD:64 FHI:256 FLO:256 EHI:256 ELO:256 CMP:512 TT0:512 TT2:512 AH:4336 B0L:512 BL:1024 G2:256 LV:256 AT:256 "
+          "CQ:256 CN:256")
+_decl(FH, "SH2:128 I16:128 I37:128 IX16:128 C1:256 VF:256 KC0:256 KC1:256 KC2:256 O16:256 O2H:256")
+_decl(I4, "OCP:256 QW:512 THI:16 QI:8 KI:8 B1:8 PI:8 T1:256 TQ:256 H:512 HA:512 W1:512 W2:512 W3:512 W6:512 W7:512 W9:512 WSI:32 WSJ:32 TM:32 UH:32 UL:32 PMI:16 BT:256 BT2:256")
+_decl(U2, "OU:256 HU:512 PU:16 SU:16 OU2:256 WL:512")
+_decl(F4, "IF:128 BOF:128 TA:128 TB:128 TC:128 TD:128 PA:64 PB:64 PG:8 JB:8 BC:8 G0:8 ONE:256 KC:8 KC16:8 KB:8 KW:8 Z0:8 Z1:8 Z4K:8 ODD:8 EVN:8 THF:8 LIM:8 "
+          "JW0:8 JW1:8 JW:8 PHF:8 NV16:256 NPL:256 NQ:256 WV:256 HV:256 ATQ:256 ATN:256 JC:16 JD:16 C1F:256 HM0:256 HM1:256 HM2:256 HBL:256 "
+          "O:256 OE:256 MN:128 TR:128 MC:256 DD:256 PR:128 SW:128 SWD:256 EE:256 E1:256 DE:128 ES:128 E2:256 E3:256 "
+          "F:256 YC:512 SMX:512 PMN:512 RMX:512 RMN:512 R01:512 YN:32 MYK:32 KK:64 K:32 KD:32 KS:512 L4P:32 W4:32 HOLD:32 AP:32 TU:32 LT:128 PEN:128 CK:128 "
+          "RK:128 K1:128 K2:128 KM:128 PM:16 PF:16 DZ:128 ZS:128 DF:128 FS:128 F2:256 FL:256 Y:256 MV:272 EQ:256 AC:256 YO:256 YQ:512 "
+          "LAND0:128 LAND1:128 LAND2:128")
+SCRATCH["OCN"] = ("sbuf", [128, 2, 8, 2, 8], I4)
+SCRATCH["YON"] = ("sbuf", [128, 2, 8, 2, 8], F4)
+for _i in range(8):
+    SCRATCH["P%d" % _i] = ("psum", [128, 512], F4)
+    WIDTH["P%d" % _i] = 512
+    WHERE["P%d" % _i] = ("P%d" % _i, 0)
+SEMAPHORES = (["qv", "qs", "qt", "qg", "sent"] + ["arr%d" % t for t in range(3)] + ["d%d" % i for i in range(30)])
+
+
+def _bank(name):
+    return name[0] == "P" and name[1:].isdigit()
+
+
+def rank_program(g, core, T, topo):
+    rank = T.rank_of(core)
+    if rank is None:
+        return
+    Q = {"v": g.vector, "s": g.scalar, "t": g.tensor, "g": g, "y": g.sync}
+    SEM = {"v": "qv", "s": "qs", "t": "qt", "g": "qg"}
+    cnt = {}
+    known = {q: {} for q in Q}
+    snap = {}
+    hist = {}
+
+    def A(n, lo=0, hi=None, st=1):
+        hi = WIDTH[n] if hi is None else hi
+        buf, c0 = WHERE[n]
+        ap = T[buf][:, c0 + lo:c0 + hi] if st == 1 else T[buf][:, c0 + lo:c0 + hi:st]
+        return (ap, [(n, lo, hi, st)])
+
+    def ROW(n, i, lo, hi):
+        buf, c0 = WHERE[n]
+        return (T[buf][i:128:16, c0 + lo:c0 + hi], [(n, lo, hi, 1)])
+
+    def IND(win, off):
+        return (win[0].indirect(off[0]), win[1] + off[1])
+
+    def clash(a, b):
+        if a[1] <= b[0] or b[1] <= a[0]:
+            return False
+        return (a[0] - b[0]) % math.gcd(a[2], b[2]) == 0
+
+    def need(q, token):
+        sem, n = token
+        if known[q].get(sem, 0) >= n:
+            return
+        Q[q].wait_ge(T.sem[sem], n)
+        for k2, v2 in snap[token].items():
+            if known[q].get(k2, 0) < v2:
+                known[q][k2] = v2
+        known[q][sem] = n
+
+    def deps(q, reads, writes, dma):
+        best = {}
+        for regs, wr in ((reads, False), (writes, True)):
+            for n, lo, hi, st in regs:
+                bank = _bank(n)
+                for (r2, tok, q2, w2, d2) in hist.get(n, []):
+                    if not (bank and q2 != q):
+                        if not clash((lo, hi, st), r2) or not (w2 or wr):
+                            continue
+                        if q == "t" and q2 == q and tok[1] > cnt.get("qt", 0):
+                            continue
+                    best[tok[0]] = max(best.get(tok[0], 0), tok[1])
+        for s in sorted(best):
+            need(q, (s, best[s]))
+
+    def note(q, reads, writes, tok, dma):
+        for n, lo, hi, st in reads:
+            hist.setdefault(n, []).append(((lo, hi, st), tok, q, False, dma))
+        for n, lo, hi, st in writes:
+            keep = []
+            for h in hist.get(n, []):
+                covered = st == 1 and lo <= h[0][0] and h[0][1] <= hi or h[0] == (lo, hi, st)
+                if not (covered or _bank(n) and h[2] != q):
+                    keep.append(h)
+            hist[n] = keep + [((lo, hi, st), tok, q, True, dma)]
+
+    def run(q, call, reads, writes, inc=True):
+        deps(q, reads, writes, False)
+        sem = SEM[q]
+        inst = call()
+        tok = (sem, cnt.get(sem, 0) + 1)
+        if inc:
+            inst.then_inc(T.sem[sem], 1)
+            cnt[sem] = tok[1]
+            s = dict(known[q])
+            s[sem] = tok[1]
+            snap[tok] = s
+        note(q, reads, writes, tok, False)
+
+    def R(*ops):
+        out = []
+        for o in ops:
+            if isinstance(o, tuple):
+                out += o[1]
+        return out
+
+    def val(o):
+        return o[0] if isinstance(o, tuple) else o
+
+    def tt(o, a, b, op):
+        run("v", lambda: g.vector.tensor_tensor(o[0], a[0], b[0], op), R(a, b), o[1])
+
+    def ts(o, a, s1, op0, s2=None, op1=None):
+        if op1 is None:
+            run("v", lambda: g.vector.tensor_scalar(o[0], a[0], val(s1), None, op0), R(a, s1), o[1])
+        else:
+            run("v", lambda: g.vector.tensor_scalar(o[0], a[0], val(s1), val(s2), op0, op1), R(a, s1, s2), o[1])
+
+    def cp(o, a):
+        run("v", lambda: g.vector.tensor_copy(o[0], a[0]), a[1], o[1])
+
+    def scatter(win, off, a):
+        run("v", lambda: g.vector.tensor_copy(win[0].indirect(off[0]), a[0]), R(a, off), win[1])
+
+    def fill(o, c):
+        run("v", lambda: g.vector.memset(o[0], c), [], o[1])
+
+    def scan(o, d0, d1, init, op0, op1):
+        run("v", lambda: g.vector.tensor_tensor_scan(o[0], d0[0], d1[0], init, op0, op1), R(d0, d1), o[1])
+
+    def act(o, a, func=Act.Copy, bias=0.0, scale=1.0):
+        run("s", lambda: g.scalar.activation(o[0], a[0], func, bias=val(bias), scale=val(scale)), R(a, bias, scale), o[1])
+
+    def mm(o, l, r, start=True, stop=True):
+        run("t", lambda: g.tensor.matmul(o[0], l[0], r[0], start, stop), R(l, r), o[1], inc=stop)
+
+    def mms(o, pairs, start=True, stop=True):
+        for i, (l, r) in enumerate(pairs):
+            mm(o, l, r, start and i == 0, stop and i == len(pairs) - 1)
+
+    def iota(o, pattern, base, cm, small=False):
+        if small:
+            run("g", lambda: g.iota(o[0], pattern, base, cm, allow_small_or_imprecise_dtypes=True), [], o[1])
+        else:
+            run("g", lambda: g.iota(o[0], pattern, base, cm), [], o[1])
+
+    def aff(o, a, pattern, op, fillv, base, cm):
+        run("g", lambda: g.affine_select(o[0], a[0], pattern, op, fillv, base, cm), a[1], o[1])
+
+    ndma = [0]
+
+    def dmas(items):
+        sem = "d%d" % ndma[0]
+        ndma[0] += 1
+        tok = (sem, 16 * len(items))
+        allk = {sem: tok[1]}
+        for q, o, a in items:
+            deps(q, a[1], o[1], True)
+            Q[q].dma_start(o[0], a[0]).then_inc(T.sem[sem], 16)
+            for k2, v2 in known[q].items():
+                allk[k2] = max(allk.get(k2, 0), v2)
+        cnt[sem] = tok[1]
+        snap[tok] = allk
+        for q, o, a in items:
+            note(q, a[1], o[1], tok, True)
+
+    def ext(ap, reg=()):
+        return (ap, list(reg))
+
+    def nat(n, ck):
+        return (T[n][:, ck & 1, :, ck >> 1, :], [(n, 0, 1, 1)])
+
+    dmas([("y", (T.OCN[:], [("OCN", 0, 1, 1)]), ext(T.oc[:]))])
+    dmas([("s", A("WT", 256, 768), ext(T.want[:])), ("s", A("THI", 0, 1), ext(T.th[:]))])
+    dmas([("y", A("OCP", 64 * c, 64 * c + 64), nat("OCN", c)) for c in range(4)])
+    dmas([("y", A("XT", 2048 * c, 2048 * c + 2048), ext(T.x[:, 2048 * c:2048 * c + 2048])) for c in range(2)])
+    dmas([("s", A("QW"), ext(T.qs[:]))])
+
+    q1, kc, z0, one = A("QI", 0, 1), A("KC", 0, 1), A("Z0", 0, 1), A("ONE", 0, 128)
+    iota(q1, [[0, 1]], 0, 1)
+    for c in range(4):
+        iota(A("NV16", 64 * c, 64 * c + 64), [[256, 8], [16, 8]], 2048 * (c & 1) + 128 * (c >> 1), 0, True)
+    fill(A("ONE"), 1.0)
+    fill(A("ZRO"), 0.0)
+    for c in range(2):
+        act(A("WDS", 2048 * c, 2048 * c + 2048), A("ZRO", 0, 2048))
+    aff(A("IF"), one, [[-1, 128]], Op.is_equal, 0.0, 0, 1)
+    aff(A("TA"), one, [[-1, 128]], Op.is_equal, 0.0, 1, 1)
+    aff(A("TB"), one, [[-16, 8], [0, 16]], Op.is_ge, 0.0, 0, 1)
+    aff(A("BOF"), A("TB"), [[16, 8], [0, 16]], Op.is_ge, 0.0, 15, -1)
+    aff(A("TD"), A("BOF"), [[1, 128]], Op.is_ge, 0.0, -1, -1)
+    aff(A("PG"), A("ONE", 0, 8), [[0, 8]], Op.is_ge, 0.0, -64, 1)
+    iota(A("CK"), [[64, 2], [0, 16], [128, 4]], 0, 0, True)
+    for c in range(4):
+        iota(A("WV", 64 * c, 64 * c + 64), [[1, 64]], 128 * (c & 1) + 64 * (c >> 1), 0, True)
+    iota(A("JD"), [[16, 16]], 3840, 0, True)
+    iota(A("YC"), [[16, 2], [1, 8], [0, 32]], 0, 0, True)
+    fill(A("WT", 0, 256), 0.0)
+    fill(A("EZ"), 0.0)
+    ts(A("KI", 0, 1), q1, 15, Op.bitwise_and)
+    cp(kc, A("KI", 0, 1))
+    ts(z0, kc, 0.5, Op.is_lt)
+    ts(A("SH2"), A("TA"), 2.0, Op.mult)
+    fill(A("SH2", 0, 128, 16), 0.0)
+    cp(A("I16"), A("IF"))
+    ts(A("I37"), A("IF"), 37.0, Op.mult)
+    ts(A("IX16"), A("IF"), 16.0, Op.mult)
+    ts(A("NPL"), A("NV16"), kc, Op.add)
+    ts(A("C1F"), A("NV16"), 0.125, Op.mult, 512.0, Op.add)
+    ts(A("C1"), A("C1F"), z0, Op.mult, -511.0, Op.add)
+    ts(A("VF"), A("NV16"), 0.0625, Op.mult)
+    ts(A("KC0"), A("ONE"), kc, Op.mult, -1280.0, Op.add)
+    act(A("IB"), A("IF"))
+    ts(A("OE"), A("OCP"), 511.5, Op.is_lt)
+    ts(A("EE"), A("OCP"), 256.0, Op.add)
+    tt(A("O"), A("EE"), A("OE"), Op.mult)
+
+    def ez(n, k):
+        return A(n, 15 - k, 143 - k)
+
+    def persons():
+        cp(A("O16"), A("O"))
+        cp(A("OU"), A("O"))
+
+    def lists(t):
+        mms(A("P2", 0, 256), [(A("SH2"), A("O16")), (A("I16"), A("C1"))])
+        mms(A("P3", 0, 256), [(A("I37"), A("O16")), (A("IX16"), A("VF")), (A("I16"), A("KC%d" % t))])
+        for b in range(2):
+            mms(A("P3", 256 + 128 * b, 384 + 128 * b),
+                [(A("I37"), A("O16", 128 * b, 128 * b + 128)), (A("IX16"), A("VF", 128 - 128 * b, 256 - 128 * b)), (A("I16"), A("KC%d" % t, 0, 128))])
+        tt(A("T1"), A("NPL"), A("P2", 0, 256), Op.mult)
+        ts(A("TQ"), A("T1"), 4, Op.arith_shift_right)
+        tt(A("H", 0, 256), A("TQ"), A("P3", 0, 256), Op.add)
+        ts(A("HA", 0, 256), A("H", 0, 256), 4095, Op.bitwise_and)
+        cp(A("HU", 0, 256), A("HA", 0, 256))
+        for b in range(2):
+            tt(A("H", 256 + 128 * b, 384 + 128 * b), A("TQ", 128 - 128 * b, 256 - 128 * b), A("P3", 256 + 128 * b, 384 + 128 * b), Op.add)
+        ts(A("HA", 256, 512), A("H", 256, 512), 4095, Op.bitwise_and)
+        cp(A("HU", 256, 512), A("HA", 256, 512))
+
+    shared = [3]
+
+    def wants():
+        for c in (0, 2, 1, 3):
+            act(A("WG", 1024 * c, 1024 * c + 1024), IND(A("WT"), A("OU", 64 * c, 64 * c + 64)))
+
+    def minima(c):
+        w = A("WG", 1024 * c, 1024 * c + 1024)
+        for j, n in ((0, "D0"), (1, "D1")):
+            if j and c in shared:
+                continue
+            tt(A(n, 1024 * c, 1024 * c + 1024), IND(A("XT"), A("HU", 256 * j + 64 * c, 256 * j + 64 * c + 64)), w, Op.min)
+        hv, b3 = c & 1, c >> 1
+        for j, n in ((0, "D0"), (1, "D1")):
+            o = A("P%d" % hv, 128 * j + 64 * b3, 128 * j + 64 * b3 + 64)
+            mm(o, A("IB"), A("CADD"), True, False)
+            d = [A(n, 1024 * c + k, 1024 * c + 1024 - 15 + k, 16) for k in range(16)]
+            if j and c in shared:
+                mms(o, [(ez("EZ4", k), A("WG", 1024 * c + k, 1024 * c + 1024 - 15 + k, 16)) for k in range(16)], False, False)
+                mms(o, [(ez("EZM", k), d[k]) for k in range(16)], False, True)
+            else:
+                mms(o, [(ez("EZ4", k), d[k]) for k in range(16)], False, True)
+
+    def shared_gather():
+        for c in shared:
+            act(A("D1", 1024 * c, 1024 * c + 1024), IND(A("XT"), A("HU", 256 + 64 * c, 320 + 64 * c)))
+
+    def shared_clip():
+        for c in shared:
+            for h in range(2):
+                w = (1024 * c + 512 * h, 1024 * c + 512 * h + 512)
+                mms(A("P%d" % (2 + h)), [(A("IB"), A("WG", *w)), (A("INB"), A("D1", *w))])
+                act(A("D1", *w), A("P%d" % (2 + h)), Act.Relu)
+
+    ts(A("PI", 0, 1), q1, 63, Op.bitwise_and)
+    cp(A("JB", 0, 1), A("PI", 0, 1))
+    fill(A("JB", 1, 2), 63.0 * LN2)
+    dmas([("y", A("WDE", 2048 * c, 2048 * c + 2048), A("ZRO", 0, 2048)) for c in range(2)])
+    persons()
+    lists(0)
+    cp(A("EZ", 15, 143, 16), A("BOF", 0, 128, 16))
+    fill(A("CADD"), float(7 - rank))
+    wants()
+    act(A("EZ4"), A("EZ"), scale=4.0)
+    act(A("JW", 0, 1), A("JB", 0, 1), Act.Exp, bias=A("JB", 1, 2), scale=-2.0 * LN2)
+    act(A("EZM"), A("EZ"), scale=-4.0)
+    act(A("INB"), A("IF"), scale=-1.0)
+    shared_gather()
+    ts(A("KB", 0, 1), kc, 1.5, Op.is_lt)
+    for t in (1, 2):
+        ts(A("KC%d" % t), A("ONE"), kc, Op.mult, 77.0 * t - 1280.0, Op.add)
+
+    act(A("BO"), A("BOF"))
+    act(A("BOP"), A("BOF"), scale=A("KB", 0, 1))
+    act(A("TRI"), A("TD"))
+    act(A("TRQ"), A("TD"), scale=-256.0)
+    act(A("TRN"), A("TD"), scale=-1.0)
+    act(A("IBIG"), A("IF"), scale=-33554432.0)
+    act(A("I8K"), A("IF"), scale=8192.0)
+    for c in range(3):
+        w0, w1 = 2048 * c, min(4336, 2048 * c + 2048)
+        act(A("AH", w0, w1), A("ZRO", 0, w1 - w0))
+    for n in ("TT0", "TT2", "KS"):
+        act(A(n), A("ZRO", 0, 512))
+    for t in range(3):
+        act(A("HM%d" % t), A("ZRO", 0, 256))
+    act(A("MV", 256, 272), A("ZRO", 0, 16))
+    act(A("T2", 512, 528), A("ZRO", 0, 16))
+    act(A("WDS", 4096, 4112), A("ZRO", 0, 16))
+    ts(A("Z4K", 0, 1), z0, 4096.0, Op.mult)
+    act(A("WDE", 4096, 4112), A("ONE", 0, 16), scale=A("Z4K", 0, 1))
+    act(A("NLQ"), A("ZRO", 0, 128))
+    act(A("NLN"), A("ZRO", 0, 128))
+    ts(A("RS"), A("BOF", 0, 128, 16), A("KB", 0, 1), Op.mult)
+    fill(A("RMN"), -1.0e6)
+    fill(A("RMN", 0, 512, 16), 1.0e6)
+    act(A("RMX"), A("RMN"), scale=-1.0)
+
+    def slot_windows():
+        q = A("QW")
+        ts(A("H"), q, 256.0, Op.mult)
+        ts(A("W1"), q, 4, Op.arith_shift_right, 0x87, Op.bitwise_and)
+        ts(A("W2"), q, 5, Op.arith_shift_right, 0x38, Op.bitwise_and)
+        ts(A("W3"), q, 1, Op.arith_shift_right, 0x40, Op.bitwise_and)
+        ts(A("HA"), A("H"), 0x100F00, Op.bitwise_and)
+        tt(A("W6"), A("W1"), A("W2"), Op.add)
+        tt(A("W7"), A("W3"), A("HA"), Op.add)
+        tt(A("W9"), A("W6"), A("W7"), Op.add)
+        ts(A("WL"), A("W9"), 4096.0, Op.min)
+
+    def late_constants():
+        ts(A("RW"), A("BOF", 0, 128, 16), kc, Op.mult, 16.0, Op.mult)
+        ts(A("G0"), A("BOF", 0, 128, 16), z0, Op.mult)
+        cp(A("THF", 0, 1), A("THI", 0, 1))
+        ts(A("LIM", 0, 1), A("THF", 0, 1), 4.0, Op.mult, float(rank), Op.add)
+        act(A("TA"), one, scale=A("LIM", 0, 1))
+        for c in range(4):
+            mm(A("P5", 8 * c, 8 * c + 8), A("WT", 256 + 128 * c, 384 + 128 * c), A("RW"))
+        mm(A("P4", 0, 8), A("TA"), A("G0"))
+        for t in range(3):
+            ts(A("HM%d" % t, t, 256, 8), A("ONE", 0, 32), z0, Op.mult, -1.0e6, Op.mult)
+        ts(A("WSI"), A("P5", 0, 32), 255.0, Op.add)
+        for c in range(4):
+            cp(A("L4P", 8 * c, 8 * c + 8), A("P4", 0, 8))
+        ts(A("WSJ"), A("WSI"), 255, Op.bitwise_and)
+        ts(A("W4"), A("WSJ"), 4.0, Op.mult, 32768.0, Op.add)
+        ts(A("KC16", 0, 1), kc, -1.0, Op.mult, 16.0, Op.add)
+        ts(A("Z1", 0, 1), kc, 1.0, Op.is_equal)
+        fill(A("MT", 0, 256), 131072.0)
+        fill(A("R01"), 1.0)
+        fill(A("R01", 0, 512, 16), 0.0)
+        fill(A("RK"), -1.0e6)
+        fill(A("RK", 0, 128, 4), 1.0e6)
+        ts(A("CK"), A("CK"), 31.6, Op.add, 2.0 * LN2, Op.mult)
+        tt(A("JW1", 0, 1), A("JW", 0, 1), A("PG", 0, 1), Op.mult)
+        tt(A("JW0", 0, 1), A("JW", 0, 1), A("JW1", 0, 1), Op.subtract)
+        ts(A("PI", 7, 8), q1, 4, Op.arith_shift_right)
+        ts(A("PHF", 1, 2), A("PI", 7, 8), 16.0, Op.mult)
+        for c in range(4):
+            ts(A("TT2", 128 * c, 128 * c + 128, 16), A("ONE", 0, 8), A("PHF", 1, 2), Op.mult, 256.0 + 128.0 * c, Op.add)
+        ts(A("TT2", 1, 512, 16), A("ONE", 0, 32), kc, Op.mult)
+        ts(A("KW", 0, 1), kc, 2.0, Op.is_equal)
+        ts(A("KW", 1, 2), A("KB", 0, 1), 16.0, Op.mult)
+        tt(A("KW", 2, 3), A("KW", 0, 1), A("KW", 1, 2), Op.add)
+        act(A("EZW"), A("EZ"), scale=A("KW", 2, 3))
+        ts(A("JC"), A("JD"), kc, Op.add)
+        fill(A("BC", 4, 5), -2000.0 * 63.2 * LN2)
+        act(A("NLQ", 0, 128, 16), A("BOF", 0, 128, 16), scale=-256.0)
+        act(A("NLN", 1, 128, 16), A("BOF", 0, 128, 16), scale=-1.0)
+        ts(A("NQ"), A("ONE"), kc, Op.mult, 256.0, Op.mult)
+        tt(A("NQ"), A("NQ"), A("WV"), Op.add)
+        ts(A("CQ"), A("WV"), A("Z1", 0, 1), Op.mult)
+        ts(A("E2"), A("NV16"), -4096.0, Op.add, z0, Op.mult)
+        ts(A("E3"), A("ONE"), A("Z1", 0, 1), Op.mult, 16.0, Op.mult)
+        tt(A("CN"), A("E2"), A("E3"), Op.add)
+        for x in range(16):
+            mm(A("P4", x, 256 - 15 + x, 16), A("IB"), A("CQ", 16 * x, 16 * x + 16))
+        for x in range(16):
+            mm(A("P5", x, 256 - 15 + x, 16), A("IB"), A("CN", 16 * x, 16 * x + 16))
+        act(A("ATQ"), A("P4", 0, 256))
+        act(A("ATN"), A("P5", 0, 256))
+
+    def pair_limits():
+        tt(A("MN"), A("O", 0, 128), A("O", 128, 256), Op.min)
+        ts(A("TR"), A("MN"), 255.5, Op.is_lt, 1.0e6, Op.mult)
+
+    def decide(hv, heads):
+        p = "P%d" % hv
+        w = (128 * hv, 128 * hv + 128)
+        m, d = A("MC", *w), A("DD", *w)
+        cp(m, A(p, 0, 128))
+        tt(d, A(p, 128, 256), m, Op.subtract)
+        pr, tr = A("PR", 64 * hv, 64 * hv + 64), A("TR", 64 * hv, 64 * hv + 64)
+        tt(pr, A("DD", w[0], w[0] + 64), A("DD", w[0] + 64, w[1]), Op.add)
+        sw = A("SW", 64 * hv, 64 * hv + 64)
+        tt(sw, pr, tr, Op.is_gt)
+        for b in range(2):
+            h = (w[0] + 64 * b, w[0] + 64 * b + 64)
+            tt(A("EE", *h), A("DD", *h), sw, Op.mult)
+        f = A("F", *w)
+        tt(f, A("EE", *w), m, Op.add)
+        hi, lo = A("FHI", *w), A("FLO", *w)
+        cp(hi, f)
+        tt(lo, f, hi, Op.subtract)
+        if hv:
+            dmas([("y", ROW("WDS", 0, 0, 4096), A("FHI")), ("y", ROW("WDS", 1, 0, 4096), A("FLO"))])
+            h = A("WDS", heads, 256, 8)
+            act(h, h, scale=-1.0)
+
+    used, plan = [], []
+    for d in sorted([d for d in T.cores if d != core], key=lambda d: len(topo.engines(core, d))):
+        es = [e for e in topo.engines(core, d) if e not in used][:4]
+        used += es
+        plan.append((d, sum(1 << e for e in es), len(es)))
+
+    def send(t):
+        own, reg = A("LAND%d" % t, 32 * rank, 32 * rank + 32)
+        deps("g", reg, [], True)
+        tr = []
+        for d, mask, ne in plan:
+            rid, pid = topo.addr(d, core)
+            tr.append(RemoteDMATransfer(dst_ids=[DstId(rid=rid, pnc=pid)], dma_engine_mask=mask, remote_sem=T.sem["arr%d" % t], src=own, dst=own))
+        g.remote_dma_fused(tr, local_sem=T.sem.sent)
+        n = sum([p[2] for p in plan])
+        cnt["sent"] = cnt.get("sent", 0) + n
+        tok = ("arr%d" % t, n)
+        cnt[tok[0]] = n
+        snap[tok] = {tok[0]: n}
+        for r in range(4):
+            if r != rank:
+                hist.setdefault("LAND%d" % t, []).append(((32 * r, 32 * r + 32, 1), tok, "net", True, True))
+
+    def slot_scores():
+        for c in range(4):
+            for m in (2 * c, 2 * c + 1):
+                o, i = A("GS", 256 + 1024 * m, 1280 + 1024 * m), IND(A("WDS"), A("WL", 64 * m, 64 * m + 64))
+                if m & 1:
+                    cp(o, i)
+                else:
+                    act(o, i)
+            p = "P7" if c & 2 else "P6"
+            for s in range(16):
+                lo = 256 + 2048 * c + s
+                mm(A(p, 128 * (c & 1) + s, 128 * (c & 1) + 128 - 15 + s, 16), A("GS", lo, lo + 2048 - 15, 16), A("RS"))
+        for h, p in ((0, "P6"), (1, "P7")):
+            w = (256 * h, 256 * h + 256)
+            scan(A("PMN", *w), A("RMN", 0, 256), A(p, 0, 256), 0.0, Op.max, Op.min)
+            scan(A("SMX", *w), A("RMX", 0, 256), A(p, 0, 256), 0.0, Op.min, Op.max)
+
+    def roll(t):
+        ts(A("YN"), A("PMN", 15, 512, 16), -1.0, Op.mult)
+        tt(A("LAND%d" % t, 32 * rank, 32 * rank + 32), A("YN"), A("SMX", 15, 512, 16), Op.max)
+        send(t)
+
+    def after_exchange(t):
+        act(A("HBL"), A("HM%d" % t), Act.Identity, bias=A("LIM", 0, 1))
+        for hv in range(2):
+            tt(A("DF", 64 * hv, 64 * hv + 64), A("F", 128 * hv, 128 * hv + 64), A("F", 128 * hv + 64, 128 * hv + 128), Op.subtract)
+        tt(A("DZ"), A("O", 0, 128), A("O", 128, 256), Op.subtract)
+        tt(A("ZS"), A("DZ"), A("SW"), Op.mult)
+        tt(A("FS"), A("DF"), A("SW"), Op.mult)
+        tt(A("O2H", 0, 128), A("O", 0, 128), A("ZS"), Op.subtract)
+        tt(A("O2H", 128, 256), A("O", 128, 256), A("ZS"), Op.add)
+        cp(A("OU2"), A("O2H"))
+        for hv in range(2):
+            tt(A("F2", 64 * hv, 64 * hv + 64), A("F", 128 * hv, 128 * hv + 64), A("FS", 64 * hv, 64 * hv + 64), Op.subtract)
+            tt(A("F2", 128 + 64 * hv, 192 + 64 * hv), A("F", 128 * hv + 64, 128 * hv + 128), A("FS", 64 * hv, 64 * hv + 64), Op.add)
+        tt(A("FL"), A("F2"), A("HBL"), Op.add)
+        ts(A("MYK"), A("LAND%d" % t, 32 * rank, 32 * rank + 32), 0.5, Op.max)
+
+    def place_keys(c, vec):
+        o, i = A("MG", 1024 * c, 1024 * c + 1024), IND(A("MT"), A("OU2", 64 * c, 64 * c + 64))
+        if vec:
+            cp(o, i)
+        else:
+            act(o, i)
+
+    def thresholds(t):
+        ld = "LAND%d" % t
+        tt(A("KK"), A(ld, 0, 64), A(ld, 64, 128), Op.max)
+        tt(A("K"), A("KK", 0, 32), A("KK", 32, 64), Op.max)
+        cp(A("TT0", 0, 512, 16), A("K"))
+        tt(A("TT0", 1, 512, 16), A("K"), A("TT0", 0, 512, 16), Op.subtract)
+        for c in range(4):
+            mm(A("P0", 128 * c, 128 * c + 128), A("TT0", 128 * c, 128 * c + 128), A("IB"))
+        act(A("MT", 256, 768), A("P0"))
+        for c in range(3):
+            place_keys(c, False)
+
+    def applicants():
+        tt(A("KD"), A("K"), A("L4P"), Op.subtract)
+        ts(A("KS", 0, 512, 16), A("KD"), 1.0, Op.max)
+        scan(A("P2"), A("R01"), A("KS"), 0.0, Op.mult, Op.add)
+        tt(A("CMP"), A("PMN"), A("P2"), Op.is_ge)
+        mms(A("P3", 0, 32), [(A("IB"), A("CMP", s, 512 - 15 + s, 16)) for s in range(16)])
+        tt(A("HOLD"), A("K"), A("MYK"), Op.is_equal)
+        tt(A("AP"), A("HOLD"), A("CMP", 15, 512, 16), Op.is_gt)
+        tt(A("TU"), A("K"), A("W4"), Op.add)
+        tt(A("TM"), A("TU"), A("AP"), Op.mult)
+        ts(A("UL"), A("TM"), 2, Op.arith_shift_right, 0x17, Op.bitwise_and)
+        ts(A("UH"), A("TM"), 2, Op.arith_shift_right, 0x20E8, Op.bitwise_and)
+        cp(A("ULB"), A("UL"))
+        for y in range(16):
+            mm(A("P5", 32 * y, 32 * y + 32), A("IB"), A("ULB"))
+        cp(A("TT2", 2, 512, 16), A("P3", 0, 32))
+        for c in range(4):
+            mm(A("P7", 128 * c, 128 * c + 128), A("TT2", 128 * c, 128 * c + 128), A("IB"))
+        place_keys(3, True)
+        for x in range(16):
+            v = 0x2000 + 8 * (x >> 3 & 1) + 128 * (x >> 2 & 1) + 64 * (x >> 1 & 1) + 32 * (x & 1)
+            ts(A("AH", 112 + x, 112 + x + 128 * 31 + 1, 128), A("UH"), float(v), Op.is_equal)
+        tt(A("B0L"), A("P5"), A("YC"), Op.is_equal)
+        for j in range(2):
+            ts(A("BL", 512 * j, 512 * j + 512), A("B0L"), A("JW%d" % j, 0, 1), Op.mult)
+        for c in (0, 3, 1, 2):
+            mms(A("P1", 64 * c, 64 * c + 64), [(ez("EZ", k), A("MG", 1024 * c + k, 1024 * c + 1024 - 15 + k, 16)) for k in range(16)])
+        act(A("T2", 0, 512), A("P7"))
+
+    def leave(t):
+        tt(A("LV"), A("FL"), A("P1", 0, 256), Op.is_lt)
+        mms(A("P3", 0, 256), [(A("TRN" if t == 2 else "TRQ"), A("LV")), (A("I8K"), A("LV"))])
+        for h in range(2):
+            mm(A("P5", 128 * h, 128 * h + 128), A("LV", 128 * h, 128 * h + 128), A("TRI"))
+        for h in range(2):
+            mms(A("P4", 128 * h, 128 * h + 128), [(A("O2H", 128 * h, 128 * h + 128), A("I16")), (A("LV", 128 * h, 128 * h + 128), A("IBIG"))])
+        mm(A("P2", 0, 256), A("BO"), A("LV"))
+        for x in range(16):
+            mm(A("P2", 256 + x, 512 - 15 + x, 16), A("NLN" if t == 2 else "NLQ"), A("LV", 16 * x, 16 * x + 16))
+        for x in range(16):
+            mm(A("P7", 0, 16), ez("EZ", x), A("LV", 16 * x, 16 * x + 16), x == 0, x == 15)
+        tt(A("E1"), A("NPL" if t == 2 else "NQ"), A("P3", 0, 256), Op.add)
+        tt(A("DE"), A("E1", 0, 128), A("E1", 128, 256), Op.subtract)
+        tt(A("ES"), A("DE"), A("SW"), Op.mult)
+        for hv in range(2):
+            es = A("ES", 64 * hv, 64 * hv + 64)
+            tt(A("E2", 128 * hv, 128 * hv + 64), A("E1", 64 * hv, 64 * hv + 64), es, Op.subtract)
+            tt(A("E2", 128 * hv + 64, 128 * hv + 128), A("E1", 128 + 64 * hv, 192 + 64 * hv), es, Op.add)
+        ts(A("E3"), A("E2"), 4096.0, Op.min)
+        act(A("EHI"), A("E3"))
+        ts(A("BT"), A("P5", 0, 256), float(2 ** 23 + 2 ** 19 + 2 ** 15 + 2 ** 11), Op.mult)
+        tt(A("ELO"), A("E3"), A("EHI"), Op.subtract)
+        dmas([("y", ROW("WDE", 0, 0, 4096), A("EHI")), ("y", ROW("WDE", 1, 0, 4096), A("ELO"))])
+        ts(A("BT2"), A("BT"), 2 ** 23 + 2 ** 20 + 2 ** 17 + 2 ** 14, Op.bitwise_and)
+        tt(A("Y"), A("BT2"), A("P4", 0, 256), Op.add)
+
+    def move_slots(chunks, both=False):
+        for m in chunks:
+            o, i = A("GE", 256 + 1024 * m, 1280 + 1024 * m), IND(A("WDE"), A("WL", 64 * m, 64 * m + 64))
+            if both and m > 4:
+                cp(o, i)
+            else:
+                act(o, i)
+
+    def new_entries():
+        scatter(A("GS"), A("SU"), A("AT"))
+
+    def clear_entries():
+        dmas([("y", ROW("GS", i, 256 + 2048 * c, 2304 + 2048 * c), (ROW("ZRO", i, 0, 2048)[0], A("ZRO")[1] + A("KK")[1])) for c in range(4) for i in range(2)])
+
+    def read_slots(n, j, start):
+        mms(A("P%d" % (4 + j), 0, 128), [(ez("EZ", s), A(n, 256 + 2048 * j + s, 2304 + 2048 * j - 15 + s, 16)) for s in range(16)], start, not start)
+
+    def close_up(j):
+        th, d = 2.0 ** (23 - 3 * j), 1 << j
+        ts(A("P5", 0, 256), A("Y"), th, Op.is_lt)
+        ts(A("MV", 0, 256), A("Y"), th, Op.subtract, 0.0, Op.max)
+        tt(A("P5", 256, 512), A("Y"), A("P5", 0, 256), Op.mult)
+        tt(A("Y"), A("P5", 256, 512), A("MV", d, 256 + d), Op.max)
+
+    def logs():
+        for c in range(4):
+            for h in range(8):
+                cg = 8 * c + h
+                w0 = 112 + 128 * cg - 16 * h
+                mm(A("P6", c, 128 - 3 + c, 4), A("AH", w0, w0 + 128), A("BL", cg, 1024 - 31 + cg, 32), h == 0, h == 7)
+        act(A("LT"), A("P6", 0, 128), Act.Ln, bias=2.0 ** -64)
+        act(A("PEN"), A("LT"), Act.Relu, bias=A("BC", 4, 5), scale=-2000.0)
+
+    def winners(t):
+        tt(A("K1"), A("CK"), A("LT"), Op.subtract)
+        tt(A("K2"), A("K1"), A("PEN"), Op.add)
+        scan(A("KM"), A("RK"), A("K2"), 0.0, Op.max, Op.min)
+        tt(A("PM"), A("KM", 3, 64, 4), A("KM", 67, 128, 4), Op.min)
+        ts(A("PF"), A("P7", 0, 16), 0.5, Op.is_lt, 1.0e4, Op.mult)
+        tt(A("PM"), A("PM"), A("PF"), Op.max)
+        ts(A("PMI"), A("PM"), 0.5 / LN2, Op.mult, 512.0, Op.min)
+        cp(A("PU"), A("PMI"))
+        act(A("G2"), IND(A("T2"), A("PU")))
+        for x in range(16):
+            mm(A("P6", 16 * x, 16 * x + 16), A("BOP"), A("G2", x, 256 - 15 + x, 16))
+        for x in range(16):
+            mm(A("P6", 256, 272), ez("EZW", x), A("G2", x, 256 - 15 + x, 16), x == 0, x == 15)
+
+    def settle(t):
+        for h in range(2):
+            mm(A("P1", 128 * h, 128 * h + 128), A("Y", 128 * h, 128 * h + 128), A("IF"))
+        ts(A("EQ"), A("P2", 0, 256), A("KC16", 0, 1), Op.is_equal)
+        tt(A("AC"), A("EQ"), A("P6", 0, 256), Op.mult)
+        tt(A("O"), A("P1", 0, 256), A("AC"), Op.max)
+        if t < 2:
+            persons()
+        tt(A("JD"), A("P6", 256, 272), A("JC"), Op.max)
+        ts(A("SU"), A("JD"), -3840.0, Op.add)
+        tt(A("AT"), A("ATN" if t == 2 else "ATQ"), A("P2", 256, 512), Op.add)
+
+    for t in range(3):
+        if t:
+            lists(t)
+            wants()
+            shared_gather()
+            move_slots(range(3, 6))
+            new_entries()
+            for j in range(4):
+                read_slots("GS", j, True)
+        minima(0)
+        minima(2)
+        shared_clip()
+        if t:
+            move_slots(range(6, 8))
+        pair_limits()
+        minima(1)
+        if t:
+            read_slots("GE", 0, False)
+            read_slots("GE", 1, False)
+        decide(0, t)
+        minima(3)
+        if t:
+            read_slots("GE", 2, False)
+            read_slots("GE", 3, False)
+        else:
+            slot_windows()
+        decide(1, t)
+        if t:
+            for j in range(4):
+                cp(A("WL", 128 * j, 128 * j + 128), A("P%d" % (4 + j), 0, 128))
+        else:
+            late_constants()
+        slot_scores()
+        roll(t)
+        after_exchange(t)
+        thresholds(t)
+        clear_entries()
+        applicants()
+        leave(t)
+        logs()
+        close_up(0)
+        close_up(1)
+        winners(t)
+        close_up(2)
+        close_up(3)
+        settle(t)
+        del shared[:]
+        if t < 2:
+            move_slots(range(3))
+
+    new_entries()
+
+    def read(n, m, start, stop):
+        mms(A("P%d" % m, 0, 64), [(ez("EZ", s), A(n, 256 + 1024 * m + s, 1280 + 1024 * m - 15 + s, 16)) for s in range(16)], start, stop)
+
+    move_slots(range(8), True)
+    early = (0, 1, 2, 3)
+    for m in early:
+        read("GE", m, True, False)
+    for m in range(8):
+        read("GS", m, m not in early, m in early)
+    for m in (5, 4, 6, 7):
+        read("GE", m, False, True)
+    ts(A("OE"), A("O"), 255.5, Op.is_lt, 512.0, Op.mult)
+    ts(A("EE"), A("O"), -256.0, Op.add)
+    tt(A("YO"), A("EE"), A("OE"), Op.max)
+    dmas([("s", nat("YON", c), A("YO", 64 * c, 64 * c + 64)) for c in range(4)])
+    dmas([("s", ext(T.yoc[:]), (T.YON[:], [("YON", 0, 1, 1)]))])
+    for h in range(2):
+        for m in range(4 * h, 4 * h + 4):
+            if m & 1:
+                cp(A("YQ", 64 * m, 64 * m + 64), A("P%d" % m, 0, 64))
+            else:
+                act(A("YQ", 64 * m, 64 * m + 64), A("P%d" % m, 0, 64))
+        dmas([("y", ext(T.yq[:, 256 * h:256 * h + 256]), A("YQ", 256 * h, 256 * h + 256))])
+    for s in sorted(cnt):
+        if known["g"].get(s, 0) < cnt[s]:
+            g.wait_ge(T.sem[s], cnt[s])

@@ -1,6 +1,6 @@
 import math
 from concourse.bass import DstId, RemoteDMATransfer
-from concourse.mybir import dt, AluOpType as Op, ActivationFunctionType as Act
+from concourse.mybir import dt, AluOpType as Op, ActivationFunctionType as Act, AxisListType as Ax
 
 LN2 = math.log(2.0)
 BF, F4, FH, I4, U2 = "bfloat16", "float32", "float16", "int32", "uint16"
@@ -19,26 +19,35 @@ def _decl(dtype, spec):
     SCRATCH[pool] = ("sbuf", [128, at], dtype)
 
 
-_decl(BF, "XT:4096 WT:768 MT:768 T2:528 WG:4096 D0:4096 D1:4096 MG:4096 ZRO:2112 WDS:4112 WDE:4112 GS:8448 GE:8448 "
-          "EZ:144 EZ4:144 EZM:144 EZW:144 INB:128 ULB:32 BO:128 BOP:128 IB:128 IBIG:128 I8K:128 TRI:128 TRQ:128 TRN:128 NLQ:128 NLN:128 "
-          "RS:8 RW:8 CADD:64 FHI:256 FLO:256 EHI:256 ELO:256 CMP:512 TT0:512 TT2:512 AH:4336 B0L:512 BL:1024 G2:256 LV:256 AT:256 "
-          "CQ:256 CN:256")
-_decl(FH, "SH2:128 I16:128 I37:128 IX16:128 C1:256 VF:256 KC0:256 KC1:256 KC2:256 O16:256 O2H:256")
-_decl(I4, "OCP:256 QW:512 THI:16 QI:8 KI:8 B1:8 PI:8 T1:256 TQ:256 H:512 HA:512 W1:512 W2:512 W3:512 W6:512 W7:512 W9:512 WSI:32 WSJ:32 TM:32 UH:32 UL:32 PMI:16 BT:256 BT2:256")
-_decl(U2, "OU:256 HU:512 PU:16 SU:16 OU2:256 WL:512")
-_decl(F4, "IF:128 BOF:128 TA:128 TB:128 TC:128 TD:128 PA:64 PB:64 PG:8 JB:8 BC:8 G0:8 ONE:256 KC:8 KC16:8 KB:8 KW:8 Z0:8 Z1:8 Z4K:8 ODD:8 EVN:8 THF:8 LIM:8 "
-          "JW0:8 JW1:8 JW:8 PHF:8 NV16:256 NPL:256 NQ:256 WV:256 HV:256 ATQ:256 ATN:256 JC:16 JD:16 C1F:256 HM0:256 HM1:256 HM2:256 HBL:256 "
-          "O:256 OE:256 MN:128 TR:128 MC:256 DD:256 PR:128 SW:128 SWD:256 EE:256 E1:256 DE:128 ES:128 E2:256 E3:256 "
-          "F:256 YC:512 SMX:512 PMN:512 RMX:512 RMN:512 R01:512 YN:32 MYK:32 KK:64 K:32 KD:32 KS:512 L4P:32 W4:32 HOLD:32 AP:32 TU:32 LT:128 PEN:128 CK:128 "
-          "RK:128 K1:128 K2:128 KM:128 PM:16 PF:16 DZ:128 ZS:128 DF:128 FS:128 F2:256 FL:256 Y:256 MV:272 EQ:256 AC:256 YO:256 YQ:512 "
-          "LAND0:128 LAND1:128 LAND2:128")
-SCRATCH["OCN"] = ("sbuf", [128, 2, 8, 2, 8], I4)
-SCRATCH["YON"] = ("sbuf", [128, 2, 8, 2, 8], F4)
-for _i in range(8):
-    SCRATCH["P%d" % _i] = ("psum", [128, 512], F4)
-    WIDTH["P%d" % _i] = 512
-    WHERE["P%d" % _i] = ("P%d" % _i, 0)
-SEMAPHORES = (["qv", "qs", "qt", "qg", "sent"] + ["arr%d" % t for t in range(3)] + ["d%d" % i for i in range(30)])
+_decl(BF, "XT:4096 WT:528 MT:528 WG:4096 D0:4096 D1:4096 MG:4096 WD:4112 GS:8192 GE:8192 TT:512 PT:768 AH:1536 ZB:1024 CMP:528 "
+          "EZ4:144 EZM:144 EZP:144 IB:128 INB:128 I8K:128 IN8K:128 I24:128 IN24:128 IPEN:128 I128:128 IM128:128 BO:128 "
+          "RS:8 RS0:8 RS1:8 RS2:8 RE:8 RW:8 CADD:64 R01:256 BIG:16 KILO:64 ONEB:32 CAT:256 CHI:256 CLO:256 "
+          "FHI:256 FLO:256 EHL:512 EM:256 SW:128 GO:256 CN:256 AT:256 B0L:512")
+_decl(FH, "I16:128 IN16:128 I2:128 I37:128 L32:128 C1:256 KC0:256 KC1:256 KC2:256 OP:256 ZS:128 NL:512 YA:256 YB:256 "
+          "IN00:128 IN01:128 IN10:128 IN11:128 OUT00:128 OUT01:128 OUT10:128 OUT11:128")
+_decl(I4, "OCN:256 QW:512 THI:16 QI:8 KI:8 PI:32 H:512 HA:512 TM:32 UH:32 UL:32 SUI:16 BT:256 BT2:256 WSI:32 WSJ:32")
+_decl(U2, "LR:32 LC:32 OU:256 OU2:256 HU:512 SU:16 WL:512")
+_decl(F4, "IF:128 INF:128 BOF:128 I24F:128 IN24F:128 ZF:128 TB:128 TI:128 TJ:128 TK:128 ONE:256 TA:256 TC:16 TD:256 TE:256 TH:256 VV:256 VW:256 "
+          "KC:8 KB:8 KW:16 WR:8 THF:8 LIM:8 JW:8 BC:8 G0:8 RMX:512 RMN:512 RK:128 JC:16 XC:512 YC:512 K1K:256 NPB:256 YP:256 YO:256 YQ:512 "
+          "T1:256 EE:256 FS:128 O2:256 T2:128 SMX:512 PMN:512 MYK:32 KK:64 K:32 KD:32 KD1:32 L4P:32 W4:32 HOLD:32 AP:32 TU:32 "
+          "LT:128 PEN:128 K2:128 KM:128 PF:16 PM:16 PN:16 LZ:16 CV:16 Z1:16 ZW:16 LEN:16 XK:256 Y:272 XS:512 LAND0:128 LAND1:128 LAND2:128")
+SCRATCH["O"] = ("sbuf", [128, 16, 16], FH)
+SCRATCH["O16"] = ("sbuf", [128, 8, 2, 16], FH)
+SCRATCH["OE"] = ("sbuf", [128, 8, 2, 16], FH)
+SCRATCH["BL"] = ("sbuf", [128, 16, 2, 32], BF)
+SCRATCH["P0"] = ("psum", [128, 32, 16], F4)
+SCRATCH["P2"] = ("psum", [128, 16, 2, 16], F4)
+for _n in ("P1", "P3", "P4", "P5", "P6", "P7"):
+    SCRATCH[_n] = ("psum", [128, 512], F4)
+    WIDTH[_n] = 512
+    WHERE[_n] = (_n, 0)
+SEMAPHORES = ["qv", "qs", "qt", "qg", "sent"] + ["arr%d" % t for t in range(3)] + ["d%d" % i for i in range(20)]
+
+CYCLE, PE_CYCLE, GATHER, GATHER2, SCATTER = 0.83, 0.44, 1.05, 1.5, 3.2
+CALL = {"v": 40.0, "s": 220.0, "g": 0.0}
+BANK, PE_OUT = 95.0, 400.0
+HOP, DMA, SEND, REMOTE = 100.0, 1500.0, 2000.0, 1000.0
+SLACK, SECOND = 300.0, 300.0
 
 
 def _bank(name):
@@ -57,22 +66,67 @@ def rank_program(g, core, T, topo):
     hist = {}
 
     def A(n, lo=0, hi=None, st=1):
+        if n == "P0":
+            return (T.P0[:, lo // 16:hi // 16, :], [(n, lo, hi, 1)])
+        if n == "P2":
+            return (T.P2[:, lo // 32:hi // 32], [(n, lo, hi, 1)])
+        if n == "O":
+            hi = 256 if hi is None else hi
+            return (T.O[:, lo // 16:hi // 16, :], [(n, lo, hi, 1)])
         hi = WIDTH[n] if hi is None else hi
         buf, c0 = WHERE[n]
         ap = T[buf][:, c0 + lo:c0 + hi] if st == 1 else T[buf][:, c0 + lo:c0 + hi:st]
         return (ap, [(n, lo, hi, st)])
 
-    def ROW(n, i, lo, hi):
+    def PART(n, p0, p1, ps=1, lo=0, hi=None, st=1):
+        hi = WIDTH[n] if hi is None else hi
         buf, c0 = WHERE[n]
-        return (T[buf][i:128:16, c0 + lo:c0 + hi], [(n, lo, hi, 1)])
+        return (T[buf][p0:p1:ps, c0 + lo:c0 + hi:st], [(n, lo, hi, st)])
+
+    def M(ap, *names):
+        return (ap, [(n, 0, 512, 1) for n in names])
+
+    def whole(o):
+        return M(o[0], o[1][0][0])
 
     def IND(win, off):
-        return (win[0].indirect(off[0]), win[1] + off[1])
+        return (win[0].indirect(off[0]), win[1] + off[1], True)
 
     def clash(a, b):
         if a[1] <= b[0] or b[1] <= a[0]:
             return False
         return (a[0] - b[0]) % math.gcd(a[2], b[2]) == 0
+
+    steps = []
+    seen = {}
+    group = []
+
+    def before(log, q, reads, writes):
+        out = []
+        for regs, wr in ((reads, False), (writes, True)):
+            for n, lo, hi, st in regs:
+                bank = _bank(n)
+                for (r2, tok, q2, w2) in log.get(n, []):
+                    if bank and q2 != q or clash((lo, hi, st), r2) and (w2 or wr):
+                        out.append((tok, q2))
+        return out
+
+    def note(log, q, reads, writes, tok):
+        for n, lo, hi, st in reads:
+            log.setdefault(n, []).append(((lo, hi, st), tok, q, False))
+        for n, lo, hi, st in writes:
+            keep = []
+            for e in log.get(n, []):
+                covered = st == 1 and lo <= e[0][0] and e[0][1] <= hi or e[0] == (lo, hi, st)
+                if not (covered or log is hist and _bank(n) and e[2] != q):
+                    keep.append(e)
+            log[n] = keep + [((lo, hi, st), tok, q, True)]
+
+    def step(queues, time, reads, writes, go, later=0.0):
+        k = len(steps)
+        steps.append({"queues": queues, "time": time, "later": later, "issue": go,
+                      "before": sorted(set(p for p, _ in before(seen, queues, reads, writes)))})
+        note(seen, queues, reads, writes, k)
 
     def need(q, token):
         sem, n = token
@@ -84,34 +138,16 @@ def rank_program(g, core, T, topo):
                 known[q][k2] = v2
         known[q][sem] = n
 
-    def deps(q, reads, writes, dma):
+    def deps(q, reads, writes):
         best = {}
-        for regs, wr in ((reads, False), (writes, True)):
-            for n, lo, hi, st in regs:
-                bank = _bank(n)
-                for (r2, tok, q2, w2, d2) in hist.get(n, []):
-                    if not (bank and q2 != q):
-                        if not clash((lo, hi, st), r2) or not (w2 or wr):
-                            continue
-                        if q == "t" and q2 == q and tok[1] > cnt.get("qt", 0):
-                            continue
-                    best[tok[0]] = max(best.get(tok[0], 0), tok[1])
+        for tok, q2 in before(hist, q, reads, writes):
+            if not (q == "t" and q2 == q and tok[1] > cnt.get("qt", 0)):
+                best[tok[0]] = max(best.get(tok[0], 0), tok[1])
         for s in sorted(best):
             need(q, (s, best[s]))
 
-    def note(q, reads, writes, tok, dma):
-        for n, lo, hi, st in reads:
-            hist.setdefault(n, []).append(((lo, hi, st), tok, q, False, dma))
-        for n, lo, hi, st in writes:
-            keep = []
-            for h in hist.get(n, []):
-                covered = st == 1 and lo <= h[0][0] and h[0][1] <= hi or h[0] == (lo, hi, st)
-                if not (covered or _bank(n) and h[2] != q):
-                    keep.append(h)
-            hist[n] = keep + [((lo, hi, st), tok, q, True, dma)]
-
-    def run(q, call, reads, writes, inc=True):
-        deps(q, reads, writes, False)
+    def issue(q, call, reads, writes, inc=True):
+        deps(q, reads, writes)
         sem = SEM[q]
         inst = call()
         tok = (sem, cnt.get(sem, 0) + 1)
@@ -121,7 +157,11 @@ def rank_program(g, core, T, topo):
             s = dict(known[q])
             s[sem] = tok[1]
             snap[tok] = s
-        note(q, reads, writes, tok, False)
+        note(hist, q, reads, writes, tok)
+
+    def run(q, call, reads, writes, time):
+        time += CALL[q] + (BANK if any(_bank(r[0]) for r in reads + writes) else 0.0)
+        step(q, time, reads, writes, lambda on: issue(on, call, reads, writes))
 
     def R(*ops):
         out = []
@@ -133,305 +173,333 @@ def rank_program(g, core, T, topo):
     def val(o):
         return o[0] if isinstance(o, tuple) else o
 
+    def size(o):
+        return math.prod(o[0].shape[1:])
+
+    def cycles(n, *sides):
+        narrow = all(WHERE.get(o[1][0][0], ("pool_" + FH,))[0][5:] in (BF, FH, U2) and not _bank(o[1][0][0]) for o in sides)
+        return CYCLE * max(64, n / 2 if sides and narrow else n)
+
+    def picked(a):
+        return len(a) == 3
+
     def tt(o, a, b, op):
-        run("v", lambda: g.vector.tensor_tensor(o[0], a[0], b[0], op), R(a, b), o[1])
+        n = size(o)
+        time = GATHER2 * n if picked(a) else cycles(n if _bank(a[1][0][0]) or _bank(b[1][0][0]) else 2 * n)
+        run("v", lambda: g.vector.tensor_tensor(o[0], a[0], b[0], op), R(a, b), o[1], time)
 
     def ts(o, a, s1, op0, s2=None, op1=None):
         if op1 is None:
-            run("v", lambda: g.vector.tensor_scalar(o[0], a[0], val(s1), None, op0), R(a, s1), o[1])
+            run("v", lambda: g.vector.tensor_scalar(o[0], a[0], val(s1), None, op0), R(a, s1), o[1], cycles(size(o), o, a))
         else:
-            run("v", lambda: g.vector.tensor_scalar(o[0], a[0], val(s1), val(s2), op0, op1), R(a, s1, s2), o[1])
+            run("v", lambda: g.vector.tensor_scalar(o[0], a[0], val(s1), val(s2), op0, op1), R(a, s1, s2), o[1], cycles(size(o), o, a))
 
     def cp(o, a):
-        run("v", lambda: g.vector.tensor_copy(o[0], a[0]), a[1], o[1])
+        run("v", lambda: g.vector.tensor_copy(o[0], a[0]), a[1], o[1], cycles(size(o), o, a))
 
     def scatter(win, off, a):
-        run("v", lambda: g.vector.tensor_copy(win[0].indirect(off[0]), a[0]), R(a, off), win[1])
+        run("v", lambda: g.vector.tensor_copy(win[0].indirect(off[0]), a[0]), R(a, off), win[1], SCATTER * size(a))
 
     def fill(o, c):
-        run("v", lambda: g.vector.memset(o[0], c), [], o[1])
+        run("v", lambda: g.vector.memset(o[0], c), [], o[1], cycles(size(o), o))
 
     def scan(o, d0, d1, init, op0, op1):
-        run("v", lambda: g.vector.tensor_tensor_scan(o[0], d0[0], d1[0], init, op0, op1), R(d0, d1), o[1])
+        run("v", lambda: g.vector.tensor_tensor_scan(o[0], d0[0], d1[0], init, op0, op1), R(d0, d1), o[1], cycles(size(o), o, d0, d1))
+
+    def turn(o, a):
+        run("v", lambda: g.vector.transpose(o[0], a[0]), a[1], o[1], cycles(size(o), o, a))
+
+    def total(o, a):
+        run("v", lambda: g.vector.tensor_reduce(o[0], a[0], Ax.X, Op.add), a[1], o[1], cycles(size(a)))
 
     def act(o, a, func=Act.Copy, bias=0.0, scale=1.0):
-        run("s", lambda: g.scalar.activation(o[0], a[0], func, bias=val(bias), scale=val(scale)), R(a, bias, scale), o[1])
+        run("s", lambda: g.scalar.activation(o[0], a[0], func, bias=val(bias), scale=val(scale)), R(a, bias, scale), o[1], cycles(size(o)))
 
-    def mm(o, l, r, start=True, stop=True):
-        run("t", lambda: g.tensor.matmul(o[0], l[0], r[0], start, stop), R(l, r), o[1], inc=stop)
+    def copy(queues, o, a):
+        def go(on):
+            if on == "v":
+                issue(on, lambda: g.vector.tensor_copy(o[0], a[0]), a[1], o[1])
+            else:
+                issue(on, lambda: g.scalar.activation(o[0], a[0], Act.Copy), a[1], o[1])
+        step(queues, 60.0 + GATHER * size(o) if picked(a) else CALL[queues[0]] + cycles(size(o)), a[1], o[1], go)
 
-    def mms(o, pairs, start=True, stop=True):
+    def gather(o, win, off, queues="sv"):
+        copy(queues, o, IND(win, off))
+
+    def mm(o, l, r, start=True, stop=True, more=False, cut=False):
+        wide = WHERE.get(l[1][0][0], ("",))[0] == "pool_" + F4
+        group.append((o, l, r, start, stop, PE_CYCLE * max(min(64, size(l)), size(r)) * (4 if wide else 1)))
+        if stop and not more or cut:
+            mine = list(group)
+            del group[:]
+
+            def go(on):
+                for i, (o, l, r, start, stop, _) in enumerate(mine):
+                    issue(on, lambda: g.tensor.matmul(o[0], l[0], r[0], start, stop), R(l, r), o[1], stop or i == len(mine) - 1)
+            step("t", sum(m[5] for m in mine), sum([R(m[1], m[2]) for m in mine], []), sum([m[0][1] for m in mine], []), go, PE_OUT)
+
+    def mms(o, pairs, start=True, stop=True, more=False, cut=False):
         for i, (l, r) in enumerate(pairs):
-            mm(o, l, r, start and i == 0, stop and i == len(pairs) - 1)
+            last = i == len(pairs) - 1
+            mm(o, l, r, start and i == 0, stop and last, more, cut and last)
 
-    def iota(o, pattern, base, cm, small=False):
+    def iota(o, pattern, base, cm=0, small=True):
+        time = 130.0 + 2 * CYCLE * size(o)
         if small:
-            run("g", lambda: g.iota(o[0], pattern, base, cm, allow_small_or_imprecise_dtypes=True), [], o[1])
+            run("g", lambda: g.iota(o[0], pattern, base, cm, allow_small_or_imprecise_dtypes=True), [], o[1], time)
         else:
-            run("g", lambda: g.iota(o[0], pattern, base, cm), [], o[1])
+            run("g", lambda: g.iota(o[0], pattern, base, cm), [], o[1], time)
 
     def aff(o, a, pattern, op, fillv, base, cm):
-        run("g", lambda: g.affine_select(o[0], a[0], pattern, op, fillv, base, cm), a[1], o[1])
+        run("g", lambda: g.affine_select(o[0], a[0], pattern, op, fillv, base, cm), a[1], o[1], 170.0 + 2 * CYCLE * size(o))
 
     ndma = [0]
 
-    def dmas(items):
-        sem = "d%d" % ndma[0]
-        ndma[0] += 1
-        tok = (sem, 16 * len(items))
-        allk = {sem: tok[1]}
-        for q, o, a in items:
-            deps(q, a[1], o[1], True)
-            Q[q].dma_start(o[0], a[0]).then_inc(T.sem[sem], 16)
-            for k2, v2 in known[q].items():
-                allk[k2] = max(allk.get(k2, 0), v2)
-        cnt[sem] = tok[1]
-        snap[tok] = allk
-        for q, o, a in items:
-            note(q, a[1], o[1], tok, True)
+    def dmas(q, items, later=DMA):
+        def go(on):
+            sem = "d%d" % ndma[0]
+            ndma[0] += 1
+            tok = (sem, 16 * len(items))
+            for o, a in items:
+                deps(on, a[1], o[1])
+                Q[on].dma_start(o[0], a[0]).then_inc(T.sem[sem], 16)
+            cnt[sem] = tok[1]
+            snap[tok] = dict(known[on])
+            snap[tok][sem] = tok[1]
+            for o, a in items:
+                note(hist, on, a[1], o[1], tok)
+        step(q, 50.0 * len(items), sum([a[1] for o, a in items], []), sum([o[1] for o, a in items], []), go, later)
 
-    def ext(ap, reg=()):
-        return (ap, list(reg))
+    def issue_all():
+        n = len(steps)
+        way = [0.0] * n
+        after = [[] for _ in steps]
+        for k, s in enumerate(steps):
+            for p in s["before"]:
+                after[p].append(k)
+        for k in range(n - 1, -1, -1):
+            s = steps[k]
+            way[k] = s["time"] + s["later"] + max([way[x] + (0.0 if steps[x]["queues"] == s["queues"] else HOP) for x in after[k]] + [0.0])
+        way[:loads] = [1.0e9 - k for k in range(loads)]
+        free = {q: 0.0 for q in Q}
+        ends, done, on, left = {}, {}, {}, [len(s["before"]) for s in steps]
+        ready = [k for k in range(n) if not left[k]]
 
-    def nat(n, ck):
-        return (T[n][:, ck & 1, :, ck >> 1, :], [(n, 0, 1, 1)])
+        def start(k, q):
+            return max([free[q]] + [ends[p] if on[p] == q == "t" else done[p] + (0.0 if on[p] == q else HOP) for p in steps[k]["before"]])
 
-    dmas([("y", (T.OCN[:], [("OCN", 0, 1, 1)]), ext(T.oc[:]))])
-    dmas([("s", A("WT", 256, 768), ext(T.want[:])), ("s", A("THI", 0, 1), ext(T.th[:]))])
-    dmas([("y", A("OCP", 64 * c, 64 * c + 64), nat("OCN", c)) for c in range(4)])
-    dmas([("y", A("XT", 2048 * c, 2048 * c + 2048), ext(T.x[:, 2048 * c:2048 * c + 2048])) for c in range(2)])
-    dmas([("s", A("QW"), ext(T.qs[:]))])
+        while ready:
+            can = [(start(k, q) + (SECOND if q != steps[k]["queues"][0] else 0.0), k, q) for k in ready for q in steps[k]["queues"]]
+            first, _, q = min(can)
+            mine = [c for c in can if c[2] == q]
+            best = max([c for c in mine if c[0] <= first + SLACK], key=lambda c: (way[c[1]], -c[1]))
+            fits = [c for c in mine if c[0] + steps[c[1]]["time"] <= best[0]]
+            k = max(fits, key=lambda c: (way[c[1]], -c[1]))[1] if fits else best[1]
+            ends[k] = free[q] = start(k, q) + steps[k]["time"]
+            done[k], on[k] = free[q] + steps[k]["later"], q
+            steps[k]["issue"](q)
+            ready.remove(k)
+            for x in after[k]:
+                left[x] -= 1
+                if not left[x]:
+                    ready.append(x)
 
-    q1, kc, z0, one = A("QI", 0, 1), A("KC", 0, 1), A("Z0", 0, 1), A("ONE", 0, 128)
-    iota(q1, [[0, 1]], 0, 1)
-    for c in range(4):
-        iota(A("NV16", 64 * c, 64 * c + 64), [[256, 8], [16, 8]], 2048 * (c & 1) + 128 * (c >> 1), 0, True)
-    fill(A("ONE"), 1.0)
-    fill(A("ZRO"), 0.0)
-    for c in range(2):
-        act(A("WDS", 2048 * c, 2048 * c + 2048), A("ZRO", 0, 2048))
-    aff(A("IF"), one, [[-1, 128]], Op.is_equal, 0.0, 0, 1)
-    aff(A("TA"), one, [[-1, 128]], Op.is_equal, 0.0, 1, 1)
-    aff(A("TB"), one, [[-16, 8], [0, 16]], Op.is_ge, 0.0, 0, 1)
-    aff(A("BOF"), A("TB"), [[16, 8], [0, 16]], Op.is_ge, 0.0, 15, -1)
-    aff(A("TD"), A("BOF"), [[1, 128]], Op.is_ge, 0.0, -1, -1)
-    aff(A("PG"), A("ONE", 0, 8), [[0, 8]], Op.is_ge, 0.0, -64, 1)
-    iota(A("CK"), [[64, 2], [0, 16], [128, 4]], 0, 0, True)
-    for c in range(4):
-        iota(A("WV", 64 * c, 64 * c + 64), [[1, 64]], 128 * (c & 1) + 64 * (c >> 1), 0, True)
-    iota(A("JD"), [[16, 16]], 3840, 0, True)
-    iota(A("YC"), [[16, 2], [1, 8], [0, 32]], 0, 0, True)
-    fill(A("WT", 0, 256), 0.0)
-    fill(A("EZ"), 0.0)
-    ts(A("KI", 0, 1), q1, 15, Op.bitwise_and)
-    cp(kc, A("KI", 0, 1))
-    ts(z0, kc, 0.5, Op.is_lt)
-    ts(A("SH2"), A("TA"), 2.0, Op.mult)
-    fill(A("SH2", 0, 128, 16), 0.0)
-    cp(A("I16"), A("IF"))
-    ts(A("I37"), A("IF"), 37.0, Op.mult)
-    ts(A("IX16"), A("IF"), 16.0, Op.mult)
-    ts(A("NPL"), A("NV16"), kc, Op.add)
-    ts(A("C1F"), A("NV16"), 0.125, Op.mult, 512.0, Op.add)
-    ts(A("C1"), A("C1F"), z0, Op.mult, -511.0, Op.add)
-    ts(A("VF"), A("NV16"), 0.0625, Op.mult)
-    ts(A("KC0"), A("ONE"), kc, Op.mult, -1280.0, Op.add)
-    act(A("IB"), A("IF"))
-    ts(A("OE"), A("OCP"), 511.5, Op.is_lt)
-    ts(A("EE"), A("OCP"), 256.0, Op.add)
-    tt(A("O"), A("EE"), A("OE"), Op.mult)
+    def ext(ap):
+        return (ap, [])
 
     def ez(n, k):
         return A(n, 15 - k, 143 - k)
 
-    def persons():
-        cp(A("O16"), A("O"))
-        cp(A("OU"), A("O"))
+    def rows(sel, n, lo, width):
+        return [(ez(sel, r), A(n, lo + r, lo + width - 15 + r, 16)) for r in range(16)]
+
+    dmas("y", [(A("OCN"), ext(T.oc[:]))])
+    dmas("s", [(A("WT", 16, 528), ext(T.want[:]))])
+    dmas("y", [(A("XT", 2048 * c, 2048 * c + 2048), ext(T.x[:, 2048 * c:2048 * c + 2048])) for c in range(2)], 4000.0)
+    dmas("y", [(A("QW"), ext(T.qs[:])), (A("THI", 0, 1), ext(T.th[:]))], 5000.0)
+    loads = len(steps)
+
+    q1, kc, one = A("QI", 0, 1), A("KC", 0, 1), A("ONE", 0, 128)
+
+    def constants():
+        iota(q1, [[0, 1]], 0, 1, False)
+        fill(A("ONE"), 1.0)
+        fill(A("ZB"), 0.0)
+        fill(A("ZF"), 0.0)
+        ts(A("KI", 0, 1), q1, 15, Op.bitwise_and)
+        cp(kc, A("KI", 0, 1))
+        for name, v in (("IF", 1.0), ("INF", -1.0), ("I24F", 2.0 ** 24), ("IN24F", -2.0 ** 24), ("IB", 1.0), ("INB", -1.0), ("I8K", 8192.0),
+                        ("IN8K", -8192.0), ("I24", 2.0 ** 24), ("IN24", -2.0 ** 24), ("IPEN", -65536.0), ("I128", 128.0), ("IM128", -128.0),
+                        ("I16", 1.0), ("IN16", -1.0), ("I2", 2.0), ("I37", 37.0)):
+            aff(A(name), A("ZF"), [[-1, 128]], Op.not_equal, v, 0, 1)
+        for h in range(2):
+            for b in range(2):
+                aff(A("IN%d%d" % (h, b)), A("ZF"), [[-32, 4], [1000, 2], [-2, 16]], Op.not_equal, 1.0, -b - 1000 * h, 1)
+                aff(A("OUT%d%d" % (h, b)), A("ZF"), [[-32, 4], [-1, 16], [1000, 2]], Op.not_equal, 1.0, -16 * h - 1000 * b, 1)
+        aff(A("TB"), one, [[-16, 8], [0, 16]], Op.is_ge, 0.0, 0, 1)
+        aff(A("BOF"), A("TB"), [[16, 8], [0, 16]], Op.is_ge, 0.0, 15, -1)
+        aff(A("BO"), A("TB"), [[16, 8], [0, 16]], Op.is_ge, 0.0, 15, -1)
+        for name, v in (("EZ4", 4.0), ("EZM", -4.0), ("EZP", 2.0 ** 24)):
+            fill(A(name), 0.0)
+            ts(A(name, 15, 143, 16), A("BOF", 0, 128, 16), v, Op.mult)
+        fill(PART("L32", 0, 64), 1.0 / 32)
+        for t in range(3):
+            fill(PART("KC%d" % t, 0, 32), 77.0 * t - 1280.0)
+            fill(PART("KC%d" % t, 32, 64), -15.0 / 32)
+        fill(A("CADD"), float(7 - rank))
+        iota(A("TA"), [[1, 256]], 0)
+        iota(A("TC"), [[2, 16]], 17)
+        ts(A("KW", 0, 1), kc, 16.0, Op.mult)
+        ts(A("KW", 1, 2), kc, 32.0, Op.mult)
+        ts(A("NPB"), A("TA"), 0.0625, Op.mult, A("KW", 0, 1), Op.add)
+        fill(A("C1"), -495.0)
+        ts(A("C1", 0, 256, 16), A("TC"), A("KW", 1, 2), Op.add)
+        for y in range(8):
+            ts(A("OP", 32 * y, 32 * y + 32), A("OCN", y, 256, 8), 256.0, Op.add)
+        turn(M(T.O16[:], "O16"), A("OP"))
+        ts(M(T.OE[:], "OE"), M(T.O16[:], "O16"), 767.5, Op.is_ge, -768.0, Op.mult)
+        for b in range(2):
+            mms(A("P1", 128 * b, 128 * b + 128), [(A("IN%d%d" % (h, b)), M(T[n][:, :, h, :], n)) for n in ("O16", "OE") for h in range(2)], more=b < 1)
+        cp(A("O"), A("P1", 0, 256))
+        fill(A("WT", 0, 16), 0.0)
+        cp(A("WL"), A("QW"))
+        ts(A("WR", 0, 1), kc, 4.0, Op.is_equal, 2048.0, Op.mult)
+        for lo in range(0, 4112, 1024):
+            hi = min(lo + 1024, 4112)
+            act(A("WD", lo, hi), A("ZB", 0, hi - lo), Act.Identity, bias=A("WR", 0, 1))
+        ts(A("KB", 0, 1), kc, 1.5, Op.is_lt)
+        ts(A("RS"), A("BOF", 0, 128, 16), A("KB", 0, 1), Op.mult)
+        for t in range(3):
+            ts(A("KB", 1 + t, 2 + t), kc, 5.0 + t, Op.is_equal)
+            ts(A("WR", 1 + t, 2 + t), A("KB", 1 + t, 2 + t), -65536.0, Op.mult, A("WR", 0, 1), Op.add)
+            ts(A("WD", 16 * t, 4096, 128), A("ONE", 0, 32), A("WR", 1 + t, 2 + t), Op.mult)
+            ts(A("KB", 4 + t, 5 + t), A("KB", 1 + t, 2 + t), A("KB", 0, 1), Op.add)
+            ts(A("RS%d" % t), A("BOF", 0, 128, 16), A("KB", 4 + t, 5 + t), Op.mult)
+        iota(A("RMN"), [[0, 512]], -1000000)
+        fill(A("RMN", 0, 512, 16), 1.0e6)
+        iota(A("RMX"), [[0, 512]], 1000000)
+        fill(A("RMX", 0, 512, 16), -1.0e6)
+        iota(A("XC"), [[1, 16], [0, 32]], 512)
+        iota(A("YC"), [[1, 16], [0, 32]], 0)
+        iota(A("K1K"), [[0, 16], [1024, 16]], 0)
+        iota(A("TD"), [[0, 16], [1, 16]], 0)
+        iota(A("CLO"), [[0, 16], [1, 16]], 0)
+        iota(A("VV"), [[16, 16], [256, 16]], -4096)
+        iota(A("VW"), [[-16, 16], [0, 16]], 4096)
+        iota(A("JC"), [[16, 16]], 512)
+        iota(A("PI"), [[1, 32]], 0, 0, False)
+        iota(A("TI", 0, 32), [[0, 16], [16, 2]], 0)
+        iota(A("R01"), [[0, 256]], 1)
+        fill(A("R01", 0, 256, 16), 0.0)
+        fill(A("BIG"), 65536.0)
+        fill(A("KILO"), -1024.0)
+        fill(A("ONEB"), 1.0)
+        ts(A("KW", 2, 3), kc, 2.0, Op.is_equal, -2.0, Op.mult)
+        ts(A("KW", 3, 4), kc, 1.5, Op.is_gt)
+        ts(A("KW", 4, 5), kc, 4.5, Op.is_lt, A("KW", 3, 4), Op.mult)
+        ts(A("KW", 5, 6), A("KW", 2, 3), A("KW", 4, 5), Op.add)
+        ts(A("RE"), A("BOF", 0, 128, 16), A("KW", 5, 6), Op.mult)
+        ts(A("RW"), A("BOF", 0, 128, 16), A("KW", 0, 1), Op.mult)
+        for lo in (0, 1024):
+            iota(A("AH", lo, lo + 512), [[0, 512]], 0)
+        iota(A("PT", 0, 512), [[0, 512]], 0)
+        iota(A("TT"), [[0, 512]], 0)
+        fill(A("MT", 0, 16), 131072.0)
+        fill(A("Y", 256, 272), 2.0 ** 25)
+        fill(A("CMP", 0, 16), 0.0)
+        for j in range(4):
+            fill(A("BC", 1 + j, 2 + j), -2.0 ** (23 - 3 * j))
+        ts(A("KW", 6, 7), kc, -256.0, Op.mult)
+        ts(A("CHI"), A("VW"), A("KW", 6, 7), Op.add)
+        ts(A("KW", 7, 8), kc, 0.5, Op.is_lt, 16.0, Op.mult)
+        ts(A("KW", 8, 9), kc, -1.0, Op.add, A("KW", 7, 8), Op.add)
+        ts(A("TH"), A("TD"), kc, Op.is_equal, 64.0, Op.mult)
+        ts(A("TE"), A("TD"), A("KW", 8, 9), Op.is_equal)
+        tt(A("TE"), A("TE"), A("VV"), Op.mult)
+        tt(A("CAT"), A("TE"), A("TH"), Op.add)
+        ts(A("LR"), A("TI", 0, 32), kc, Op.add)
+        cp(A("LC"), A("PI"))
+        ts(A("JC"), A("JC"), kc, Op.add)
+        fill(A("TI", 64, 128), 0.25)
+        scan(A("TJ", 0, 64), A("TI", 64, 128), A("ZF", 0, 64), 2.0 ** 65, Op.mult, Op.max)
+        for j in range(2):
+            tt(A("TJ", 64, 128), A("TJ", 0, 64), A("IF", 64 * j, 64 * j + 64), Op.mult)
+            total(A("JW", j, j + 1), A("TJ", 64, 128))
+        fill(A("RK"), -128.0 * 2 * LN2)
+        fill(A("RK", 4, 128, 8), 320.0 * 2 * LN2)
+        fill(A("RK", 0, 128, 8), 1.0e6)
+        fill(A("BC", 0, 1), -2000.0 * 63.2 * LN2)
+        ts(A("KW", 9, 10), kc, 0.5, Op.is_lt)
+        cp(A("THF", 0, 1), A("THI", 0, 1))
+        ts(A("LIM", 0, 1), A("THF", 0, 1), 4.0, Op.mult, float(rank), Op.add)
+        ts(A("G0"), A("BOF", 0, 128, 16), A("KW", 9, 10), Op.mult, A("LIM", 0, 1), Op.mult)
+        for c in range(4):
+            mm(A("P6", 8 * c, 8 * c + 8), one, A("G0"), more=True)
+            mm(A("P6", 32 + 8 * c, 40 + 8 * c), A("WT", 16 + 128 * c, 144 + 128 * c), A("RW"), more=c < 3)
+        cp(A("L4P"), A("P6", 0, 32))
+        ts(A("WSI"), A("P6", 32, 64), 255.0, Op.add)
+        ts(A("WSJ"), A("WSI"), 255, Op.bitwise_and)
+        ts(A("W4"), A("WSJ"), 4.0, Op.mult, 32768.0, Op.add)
 
     def lists(t):
-        mms(A("P2", 0, 256), [(A("SH2"), A("O16")), (A("I16"), A("C1"))])
-        mms(A("P3", 0, 256), [(A("I37"), A("O16")), (A("IX16"), A("VF")), (A("I16"), A("KC%d" % t))])
-        for b in range(2):
-            mms(A("P3", 256 + 128 * b, 384 + 128 * b),
-                [(A("I37"), A("O16", 128 * b, 128 * b + 128)), (A("IX16"), A("VF", 128 - 128 * b, 256 - 128 * b)), (A("I16"), A("KC%d" % t, 0, 128))])
-        tt(A("T1"), A("NPL"), A("P2", 0, 256), Op.mult)
-        ts(A("TQ"), A("T1"), 4, Op.arith_shift_right)
-        tt(A("H", 0, 256), A("TQ"), A("P3", 0, 256), Op.add)
+        o = A("O")
+        ts(A("OU"), o, -240.0, Op.add)
+        mm(A("P0", 0, 256), A("I16"), A("C1"), True, False)
+        mm((T.P0[:, 0:16, 1:16], [("P0", 0, 256, 1)]), A("I2"), (T.O[:, :, 0:15], o[1]), False, True, True)
+        mms(A("P0", 256, 512), [(PART("L32", 0, 64), PART("KC%d" % t, 0, 64)), (A("I37"), o)])
+        tt(A("T1"), A("NPB"), A("P0", 0, 256), Op.mult)
+        tt(A("H", 0, 256), A("T1"), A("P0", 256, 512), Op.add)
         ts(A("HA", 0, 256), A("H", 0, 256), 4095, Op.bitwise_and)
         cp(A("HU", 0, 256), A("HA", 0, 256))
         for b in range(2):
-            tt(A("H", 256 + 128 * b, 384 + 128 * b), A("TQ", 128 - 128 * b, 256 - 128 * b), A("P3", 256 + 128 * b, 384 + 128 * b), Op.add)
+            tt(A("H", 256 + 128 * b, 384 + 128 * b), A("T1", 128 - 128 * b, 256 - 128 * b), A("P0", 256 + 128 * b, 384 + 128 * b), Op.add)
         ts(A("HA", 256, 512), A("H", 256, 512), 4095, Op.bitwise_and)
         cp(A("HU", 256, 512), A("HA", 256, 512))
+        ts(A("EM"), o, 255.5, Op.is_lt)
 
-    shared = [3]
-
-    def wants():
-        for c in (0, 2, 1, 3):
-            act(A("WG", 1024 * c, 1024 * c + 1024), IND(A("WT"), A("OU", 64 * c, 64 * c + 64)))
+    def wants(c):
+        gather(A("WG", 1024 * c, 1024 * c + 1024), A("WT"), A("OU", 64 * c, 64 * c + 64))
 
     def minima(c):
-        w = A("WG", 1024 * c, 1024 * c + 1024)
-        for j, n in ((0, "D0"), (1, "D1")):
-            if j and c in shared:
-                continue
-            tt(A(n, 1024 * c, 1024 * c + 1024), IND(A("XT"), A("HU", 256 * j + 64 * c, 256 * j + 64 * c + 64)), w, Op.min)
-        hv, b3 = c & 1, c >> 1
-        for j, n in ((0, "D0"), (1, "D1")):
-            o = A("P%d" % hv, 128 * j + 64 * b3, 128 * j + 64 * b3 + 64)
-            mm(o, A("IB"), A("CADD"), True, False)
-            d = [A(n, 1024 * c + k, 1024 * c + 1024 - 15 + k, 16) for k in range(16)]
-            if j and c in shared:
-                mms(o, [(ez("EZ4", k), A("WG", 1024 * c + k, 1024 * c + 1024 - 15 + k, 16)) for k in range(16)], False, False)
-                mms(o, [(ez("EZM", k), d[k]) for k in range(16)], False, True)
-            else:
-                mms(o, [(ez("EZ4", k), d[k]) for k in range(16)], False, True)
+        w, lo = A("WG", 1024 * c, 1024 * c + 1024), 1024 * c
+        d, pair = whole(A("P2", 64 * c, 64 * c + 64)), whole(A("P3", 64 * (c & 1), 64 * (c & 1) + 64))
+        tt(A("D0", lo, lo + 1024), IND(A("XT"), A("HU", 64 * c, 64 * c + 64)), w, Op.min)
+        mms(A("P1", 64 * c, 64 * c + 64), [(A("IB"), A("CADD"))] + rows("EZ4", "D0", lo, 1024), more=True)
+        mms(d, rows("EZM", "D0", lo, 1024), True, False)
+        mms(pair, [(A("IPEN"), A("EM", 64 * c, 64 * c + 64))] + rows("EZM", "D0", lo, 1024), c < 2, False, cut=True)
+        tt(A("D1", lo, lo + 1024), IND(A("XT"), A("HU", 256 + 64 * c, 320 + 64 * c)), w, Op.min)
+        mms(pair, rows("EZ4", "D1", lo, 1024), False, c > 1, True, cut=True)
+        mms(d, rows("EZ4", "D1", lo, 1024), False, True)
 
-    def shared_gather():
-        for c in shared:
-            act(A("D1", 1024 * c, 1024 * c + 1024), IND(A("XT"), A("HU", 256 + 64 * c, 320 + 64 * c)))
+    def to_window(row, hi, lo):
+        dmas("y", [(PART("WD", row + i, 128, 16, 0, 4096), x) for i, x in enumerate((hi, lo))])
 
-    def shared_clip():
-        for c in shared:
-            for h in range(2):
-                w = (1024 * c + 512 * h, 1024 * c + 512 * h + 512)
-                mms(A("P%d" % (2 + h)), [(A("IB"), A("WG", *w)), (A("INB"), A("D1", *w))])
-                act(A("D1", *w), A("P%d" % (2 + h)), Act.Relu)
-
-    ts(A("PI", 0, 1), q1, 63, Op.bitwise_and)
-    cp(A("JB", 0, 1), A("PI", 0, 1))
-    fill(A("JB", 1, 2), 63.0 * LN2)
-    dmas([("y", A("WDE", 2048 * c, 2048 * c + 2048), A("ZRO", 0, 2048)) for c in range(2)])
-    persons()
-    lists(0)
-    cp(A("EZ", 15, 143, 16), A("BOF", 0, 128, 16))
-    fill(A("CADD"), float(7 - rank))
-    wants()
-    act(A("EZ4"), A("EZ"), scale=4.0)
-    act(A("JW", 0, 1), A("JB", 0, 1), Act.Exp, bias=A("JB", 1, 2), scale=-2.0 * LN2)
-    act(A("EZM"), A("EZ"), scale=-4.0)
-    act(A("INB"), A("IF"), scale=-1.0)
-    shared_gather()
-    ts(A("KB", 0, 1), kc, 1.5, Op.is_lt)
-    for t in (1, 2):
-        ts(A("KC%d" % t), A("ONE"), kc, Op.mult, 77.0 * t - 1280.0, Op.add)
-
-    act(A("BO"), A("BOF"))
-    act(A("BOP"), A("BOF"), scale=A("KB", 0, 1))
-    act(A("TRI"), A("TD"))
-    act(A("TRQ"), A("TD"), scale=-256.0)
-    act(A("TRN"), A("TD"), scale=-1.0)
-    act(A("IBIG"), A("IF"), scale=-33554432.0)
-    act(A("I8K"), A("IF"), scale=8192.0)
-    for c in range(3):
-        w0, w1 = 2048 * c, min(4336, 2048 * c + 2048)
-        act(A("AH", w0, w1), A("ZRO", 0, w1 - w0))
-    for n in ("TT0", "TT2", "KS"):
-        act(A(n), A("ZRO", 0, 512))
-    for t in range(3):
-        act(A("HM%d" % t), A("ZRO", 0, 256))
-    act(A("MV", 256, 272), A("ZRO", 0, 16))
-    act(A("T2", 512, 528), A("ZRO", 0, 16))
-    act(A("WDS", 4096, 4112), A("ZRO", 0, 16))
-    ts(A("Z4K", 0, 1), z0, 4096.0, Op.mult)
-    act(A("WDE", 4096, 4112), A("ONE", 0, 16), scale=A("Z4K", 0, 1))
-    act(A("NLQ"), A("ZRO", 0, 128))
-    act(A("NLN"), A("ZRO", 0, 128))
-    ts(A("RS"), A("BOF", 0, 128, 16), A("KB", 0, 1), Op.mult)
-    fill(A("RMN"), -1.0e6)
-    fill(A("RMN", 0, 512, 16), 1.0e6)
-    act(A("RMX"), A("RMN"), scale=-1.0)
-
-    def slot_windows():
-        q = A("QW")
-        ts(A("H"), q, 256.0, Op.mult)
-        ts(A("W1"), q, 4, Op.arith_shift_right, 0x87, Op.bitwise_and)
-        ts(A("W2"), q, 5, Op.arith_shift_right, 0x38, Op.bitwise_and)
-        ts(A("W3"), q, 1, Op.arith_shift_right, 0x40, Op.bitwise_and)
-        ts(A("HA"), A("H"), 0x100F00, Op.bitwise_and)
-        tt(A("W6"), A("W1"), A("W2"), Op.add)
-        tt(A("W7"), A("W3"), A("HA"), Op.add)
-        tt(A("W9"), A("W6"), A("W7"), Op.add)
-        ts(A("WL"), A("W9"), 4096.0, Op.min)
-
-    def late_constants():
-        ts(A("RW"), A("BOF", 0, 128, 16), kc, Op.mult, 16.0, Op.mult)
-        ts(A("G0"), A("BOF", 0, 128, 16), z0, Op.mult)
-        cp(A("THF", 0, 1), A("THI", 0, 1))
-        ts(A("LIM", 0, 1), A("THF", 0, 1), 4.0, Op.mult, float(rank), Op.add)
-        act(A("TA"), one, scale=A("LIM", 0, 1))
-        for c in range(4):
-            mm(A("P5", 8 * c, 8 * c + 8), A("WT", 256 + 128 * c, 384 + 128 * c), A("RW"))
-        mm(A("P4", 0, 8), A("TA"), A("G0"))
-        for t in range(3):
-            ts(A("HM%d" % t, t, 256, 8), A("ONE", 0, 32), z0, Op.mult, -1.0e6, Op.mult)
-        ts(A("WSI"), A("P5", 0, 32), 255.0, Op.add)
-        for c in range(4):
-            cp(A("L4P", 8 * c, 8 * c + 8), A("P4", 0, 8))
-        ts(A("WSJ"), A("WSI"), 255, Op.bitwise_and)
-        ts(A("W4"), A("WSJ"), 4.0, Op.mult, 32768.0, Op.add)
-        ts(A("KC16", 0, 1), kc, -1.0, Op.mult, 16.0, Op.add)
-        ts(A("Z1", 0, 1), kc, 1.0, Op.is_equal)
-        fill(A("MT", 0, 256), 131072.0)
-        fill(A("R01"), 1.0)
-        fill(A("R01", 0, 512, 16), 0.0)
-        fill(A("RK"), -1.0e6)
-        fill(A("RK", 0, 128, 4), 1.0e6)
-        ts(A("CK"), A("CK"), 31.6, Op.add, 2.0 * LN2, Op.mult)
-        tt(A("JW1", 0, 1), A("JW", 0, 1), A("PG", 0, 1), Op.mult)
-        tt(A("JW0", 0, 1), A("JW", 0, 1), A("JW1", 0, 1), Op.subtract)
-        ts(A("PI", 7, 8), q1, 4, Op.arith_shift_right)
-        ts(A("PHF", 1, 2), A("PI", 7, 8), 16.0, Op.mult)
-        for c in range(4):
-            ts(A("TT2", 128 * c, 128 * c + 128, 16), A("ONE", 0, 8), A("PHF", 1, 2), Op.mult, 256.0 + 128.0 * c, Op.add)
-        ts(A("TT2", 1, 512, 16), A("ONE", 0, 32), kc, Op.mult)
-        ts(A("KW", 0, 1), kc, 2.0, Op.is_equal)
-        ts(A("KW", 1, 2), A("KB", 0, 1), 16.0, Op.mult)
-        tt(A("KW", 2, 3), A("KW", 0, 1), A("KW", 1, 2), Op.add)
-        act(A("EZW"), A("EZ"), scale=A("KW", 2, 3))
-        ts(A("JC"), A("JD"), kc, Op.add)
-        fill(A("BC", 4, 5), -2000.0 * 63.2 * LN2)
-        act(A("NLQ", 0, 128, 16), A("BOF", 0, 128, 16), scale=-256.0)
-        act(A("NLN", 1, 128, 16), A("BOF", 0, 128, 16), scale=-1.0)
-        ts(A("NQ"), A("ONE"), kc, Op.mult, 256.0, Op.mult)
-        tt(A("NQ"), A("NQ"), A("WV"), Op.add)
-        ts(A("CQ"), A("WV"), A("Z1", 0, 1), Op.mult)
-        ts(A("E2"), A("NV16"), -4096.0, Op.add, z0, Op.mult)
-        ts(A("E3"), A("ONE"), A("Z1", 0, 1), Op.mult, 16.0, Op.mult)
-        tt(A("CN"), A("E2"), A("E3"), Op.add)
-        for x in range(16):
-            mm(A("P4", x, 256 - 15 + x, 16), A("IB"), A("CQ", 16 * x, 16 * x + 16))
-        for x in range(16):
-            mm(A("P5", x, 256 - 15 + x, 16), A("IB"), A("CN", 16 * x, 16 * x + 16))
-        act(A("ATQ"), A("P4", 0, 256))
-        act(A("ATN"), A("P5", 0, 256))
-
-    def pair_limits():
-        tt(A("MN"), A("O", 0, 128), A("O", 128, 256), Op.min)
-        ts(A("TR"), A("MN"), 255.5, Op.is_lt, 1.0e6, Op.mult)
-
-    def decide(hv, heads):
-        p = "P%d" % hv
-        w = (128 * hv, 128 * hv + 128)
-        m, d = A("MC", *w), A("DD", *w)
-        cp(m, A(p, 0, 128))
-        tt(d, A(p, 128, 256), m, Op.subtract)
-        pr, tr = A("PR", 64 * hv, 64 * hv + 64), A("TR", 64 * hv, 64 * hv + 64)
-        tt(pr, A("DD", w[0], w[0] + 64), A("DD", w[0] + 64, w[1]), Op.add)
-        sw = A("SW", 64 * hv, 64 * hv + 64)
-        tt(sw, pr, tr, Op.is_gt)
+    def decide():
+        f = A("P1", 256, 512)
+        ts(A("SW"), A("P3", 0, 128), 0.0, Op.is_gt)
         for b in range(2):
-            h = (w[0] + 64 * b, w[0] + 64 * b + 64)
-            tt(A("EE", *h), A("DD", *h), sw, Op.mult)
-        f = A("F", *w)
-        tt(f, A("EE", *w), m, Op.add)
-        hi, lo = A("FHI", *w), A("FLO", *w)
-        cp(hi, f)
-        tt(lo, f, hi, Op.subtract)
-        if hv:
-            dmas([("y", ROW("WDS", 0, 0, 4096), A("FHI")), ("y", ROW("WDS", 1, 0, 4096), A("FLO"))])
-            h = A("WDS", heads, 256, 8)
-            act(h, h, scale=-1.0)
+            tt(A("EE", 128 * b, 128 * b + 128), A("P2", 128 * b, 128 * b + 128), A("SW"), Op.mult)
+        tt(f, A("EE"), A("P1", 0, 256), Op.add)
+        cp(A("FHI"), f)
+        tt(A("FLO"), f, A("FHI"), Op.subtract)
+        to_window(0, A("FHI"), A("FLO"))
+
+    def exchange():
+        mms(A("P0", 0, 128), [(A("I16"), A("O", 0, 128)), (A("IN16"), A("O", 128, 256))], more=True)
+        mms(A("P2", 256, 384), [(A(l), A(n, lo, lo + 128)) for l, lo in (("IB", 0), ("INB", 128)) for n in ("FHI", "FLO")])
+        tt(A("ZS"), A("P0", 0, 128), A("SW"), Op.mult)
+        tt(A("FS"), A("P2", 256, 384), A("SW"), Op.mult)
+        for b, l in enumerate(("IN16", "I16")):
+            mms(A("P0", 256 + 128 * b, 384 + 128 * b), [(A("I16"), A("O", 128 * b, 128 * b + 128)), (A(l), A("ZS"))], more=b < 1)
+        ts(A("OU2"), A("P0", 256, 512), -240.0, Op.add)
+        act(A("O2"), A("P0", 256, 512))
+
+    def by_slot(n, m):
+        gather(A(n, 1024 * m, 1024 * m + 1024), A("WD"), A("WL", 64 * m, 64 * m + 64))
+
+    def read(bank, n, sel, c):
+        for s in range(16):
+            mm(A(bank, 128 * c + s, 128 * c + 128 - 15 + s, 16), A(n, 2048 * c + s, 2048 * c + 2048 - 15 + s, 16), A(sel), more=s < 15)
 
     used, plan = [], []
     for d in sorted([d for d in T.cores if d != core], key=lambda d: len(topo.engines(core, d))):
@@ -439,271 +507,175 @@ def rank_program(g, core, T, topo):
         used += es
         plan.append((d, sum(1 << e for e in es), len(es)))
 
-    def send(t):
-        own, reg = A("LAND%d" % t, 32 * rank, 32 * rank + 32)
-        deps("g", reg, [], True)
-        tr = []
-        for d, mask, ne in plan:
-            rid, pid = topo.addr(d, core)
-            tr.append(RemoteDMATransfer(dst_ids=[DstId(rid=rid, pnc=pid)], dma_engine_mask=mask, remote_sem=T.sem["arr%d" % t], src=own, dst=own))
-        g.remote_dma_fused(tr, local_sem=T.sem.sent)
-        n = sum([p[2] for p in plan])
-        cnt["sent"] = cnt.get("sent", 0) + n
-        tok = ("arr%d" % t, n)
-        cnt[tok[0]] = n
-        snap[tok] = {tok[0]: n}
-        for r in range(4):
-            if r != rank:
-                hist.setdefault("LAND%d" % t, []).append(((32 * r, 32 * r + 32, 1), tok, "net", True, True))
-
-    def slot_scores():
-        for c in range(4):
-            for m in (2 * c, 2 * c + 1):
-                o, i = A("GS", 256 + 1024 * m, 1280 + 1024 * m), IND(A("WDS"), A("WL", 64 * m, 64 * m + 64))
-                if m & 1:
-                    cp(o, i)
-                else:
-                    act(o, i)
-            p = "P7" if c & 2 else "P6"
-            for s in range(16):
-                lo = 256 + 2048 * c + s
-                mm(A(p, 128 * (c & 1) + s, 128 * (c & 1) + 128 - 15 + s, 16), A("GS", lo, lo + 2048 - 15, 16), A("RS"))
-        for h, p in ((0, "P6"), (1, "P7")):
-            w = (256 * h, 256 * h + 256)
-            scan(A("PMN", *w), A("RMN", 0, 256), A(p, 0, 256), 0.0, Op.max, Op.min)
-            scan(A("SMX", *w), A("RMX", 0, 256), A(p, 0, 256), 0.0, Op.min, Op.max)
-
     def roll(t):
-        ts(A("YN"), A("PMN", 15, 512, 16), -1.0, Op.mult)
-        tt(A("LAND%d" % t, 32 * rank, 32 * rank + 32), A("YN"), A("SMX", 15, 512, 16), Op.max)
-        send(t)
+        land = "LAND%d" % t
+        own = A(land, 32 * rank, 32 * rank + 32)
+        scan(A("SMX"), A("RMX"), A("P4"), 0.0, Op.min, Op.max)
+        cp(own, A("SMX", 15, 512, 16))
+        others = [(land, 32 * r, 32 * r + 32, 1) for r in range(4) if r != rank]
 
-    def after_exchange(t):
-        act(A("HBL"), A("HM%d" % t), Act.Identity, bias=A("LIM", 0, 1))
-        for hv in range(2):
-            tt(A("DF", 64 * hv, 64 * hv + 64), A("F", 128 * hv, 128 * hv + 64), A("F", 128 * hv + 64, 128 * hv + 128), Op.subtract)
-        tt(A("DZ"), A("O", 0, 128), A("O", 128, 256), Op.subtract)
-        tt(A("ZS"), A("DZ"), A("SW"), Op.mult)
-        tt(A("FS"), A("DF"), A("SW"), Op.mult)
-        tt(A("O2H", 0, 128), A("O", 0, 128), A("ZS"), Op.subtract)
-        tt(A("O2H", 128, 256), A("O", 128, 256), A("ZS"), Op.add)
-        cp(A("OU2"), A("O2H"))
-        for hv in range(2):
-            tt(A("F2", 64 * hv, 64 * hv + 64), A("F", 128 * hv, 128 * hv + 64), A("FS", 64 * hv, 64 * hv + 64), Op.subtract)
-            tt(A("F2", 128 + 64 * hv, 192 + 64 * hv), A("F", 128 * hv + 64, 128 * hv + 128), A("FS", 64 * hv, 64 * hv + 64), Op.add)
-        tt(A("FL"), A("F2"), A("HBL"), Op.add)
-        ts(A("MYK"), A("LAND%d" % t, 32 * rank, 32 * rank + 32), 0.5, Op.max)
-
-    def place_keys(c, vec):
-        o, i = A("MG", 1024 * c, 1024 * c + 1024), IND(A("MT"), A("OU2", 64 * c, 64 * c + 64))
-        if vec:
-            cp(o, i)
-        else:
-            act(o, i)
+        def go(on):
+            deps(on, own[1], [])
+            tr = []
+            tok = ("arr%d" % t, sum([p[2] for p in plan]))
+            for d, mask, ne in plan:
+                rid, pid = topo.addr(d, core)
+                tr.append(RemoteDMATransfer(dst_ids=[DstId(rid=rid, pnc=pid)], dma_engine_mask=mask, remote_sem=T.sem[tok[0]], src=own[0], dst=own[0]))
+            g.remote_dma_fused(tr, local_sem=T.sem.sent)
+            cnt["sent"] = cnt.get("sent", 0) + tok[1]
+            cnt[tok[0]] = tok[1]
+            snap[tok] = {tok[0]: tok[1]}
+            note(hist, "net", [], others, tok)
+        step("g", SEND, own[1], others, go, REMOTE)
+        scan(A("PMN"), A("RMN"), A("P5"), 0.0, Op.max, Op.min)
+        ts(A("MYK"), own, 0.5, Op.max)
 
     def thresholds(t):
-        ld = "LAND%d" % t
-        tt(A("KK"), A(ld, 0, 64), A(ld, 64, 128), Op.max)
+        land = "LAND%d" % t
+        tt(A("KK"), A(land, 0, 64), A(land, 64, 128), Op.max)
         tt(A("K"), A("KK", 0, 32), A("KK", 32, 64), Op.max)
-        cp(A("TT0", 0, 512, 16), A("K"))
-        tt(A("TT0", 1, 512, 16), A("K"), A("TT0", 0, 512, 16), Op.subtract)
+        tt(A("KD"), A("K"), A("L4P"), Op.subtract)
+        cp(A("TT", 0, 512, 16), A("KD"))
+        tt(A("TT", 1, 512, 16), A("KD"), A("TT", 0, 512, 16), Op.subtract)
         for c in range(4):
-            mm(A("P0", 128 * c, 128 * c + 128), A("TT0", 128 * c, 128 * c + 128), A("IB"))
-        act(A("MT", 256, 768), A("P0"))
-        for c in range(3):
-            place_keys(c, False)
+            mm(A("P3", 128 * c, 128 * c + 128), A("TT", 128 * c, 128 * c + 128), A("IB"), more=c < 3)
+        act(A("MT", 16, 528), A("P3"))
+
+    def limits(t, c):
+        w, f = (64 * c, 64 * c + 64), 64 * (c & 1)
+        gather(A("MG", 1024 * c, 1024 * c + 1024), A("MT"), A("OU2", *w))
+        o = A("P3", *w)
+        mms(o, [(A("IN24"), A("FHI", *w)), (A("IN24"), A("FLO", *w)), (A("IN24F" if c > 1 else "I24F"), A("FS", f, f + 64))], True, False)
+        if not c & 1:
+            mm(A("P3", 64 * c + 16 * t, 64 * c + 16 * t + 1), A("I24"), A("BIG", 0, 1), False, False)
+        mms(o, rows("EZP", "MG", 1024 * c, 1024) + [(A("IB"), A("KILO"))], False, True)
 
     def applicants():
-        tt(A("KD"), A("K"), A("L4P"), Op.subtract)
-        ts(A("KS", 0, 512, 16), A("KD"), 1.0, Op.max)
-        scan(A("P2"), A("R01"), A("KS"), 0.0, Op.mult, Op.add)
-        tt(A("CMP"), A("PMN"), A("P2"), Op.is_ge)
-        mms(A("P3", 0, 32), [(A("IB"), A("CMP", s, 512 - 15 + s, 16)) for s in range(16)])
+        ts(A("KD1"), A("KD"), 1.0, Op.max)
         tt(A("HOLD"), A("K"), A("MYK"), Op.is_equal)
-        tt(A("AP"), A("HOLD"), A("CMP", 15, 512, 16), Op.is_gt)
         tt(A("TU"), A("K"), A("W4"), Op.add)
+        tt(A("CMP", 16, 528), IND(A("KD1"), A("LC")), A("PMN"), Op.is_le)
+        tt(A("AP"), A("HOLD"), A("CMP", 31, 528, 16), Op.is_gt)
         tt(A("TM"), A("TU"), A("AP"), Op.mult)
-        ts(A("UL"), A("TM"), 2, Op.arith_shift_right, 0x17, Op.bitwise_and)
-        ts(A("UH"), A("TM"), 2, Op.arith_shift_right, 0x20E8, Op.bitwise_and)
-        cp(A("ULB"), A("UL"))
-        for y in range(16):
-            mm(A("P5", 32 * y, 32 * y + 32), A("IB"), A("ULB"))
-        cp(A("TT2", 2, 512, 16), A("P3", 0, 32))
-        for c in range(4):
-            mm(A("P7", 128 * c, 128 * c + 128), A("TT2", 128 * c, 128 * c + 128), A("IB"))
-        place_keys(3, True)
-        for x in range(16):
-            v = 0x2000 + 8 * (x >> 3 & 1) + 128 * (x >> 2 & 1) + 64 * (x >> 1 & 1) + 32 * (x & 1)
-            ts(A("AH", 112 + x, 112 + x + 128 * 31 + 1, 128), A("UH"), float(v), Op.is_equal)
-        tt(A("B0L"), A("P5"), A("YC"), Op.is_equal)
+        ts(A("UL"), A("TM"), 2, Op.arith_shift_right, 15, Op.bitwise_and)
+        ts(A("UH"), A("TM"), 6, Op.arith_shift_right, 0x20F, Op.bitwise_and)
+        tt(A("B0L"), IND(A("UL"), A("LR")), A("YC"), Op.is_equal)
+        tt(A("AH", 512, 1024), IND(A("UH"), A("LR")), A("XC"), Op.is_equal)
         for j in range(2):
-            ts(A("BL", 512 * j, 512 * j + 512), A("B0L"), A("JW%d" % j, 0, 1), Op.mult)
-        for c in (0, 3, 1, 2):
-            mms(A("P1", 64 * c, 64 * c + 64), [(ez("EZ", k), A("MG", 1024 * c + k, 1024 * c + 1024 - 15 + k, 16)) for k in range(16)])
-        act(A("T2", 0, 512), A("P7"))
+            ts(M(T.BL[:, :, j, :], "BL%d" % j), A("B0L"), A("JW", j, j + 1), Op.mult)
+        for c in range(4):
+            for x in range(8):
+                w0, a = 512 - 512 * (x & 1) + 8 * c + x, 32 * (x >> 1)
+                mm(PART("P4", a, a + 32, 1, c, 128 - 3 + c, 4), A("AH", w0, w0 + 1024 - 31, 32), M(T.BL[:, :, :, 8 * c + x], "BL0", "BL1"),
+                   not x & 1, bool(x & 1), 8 * c + x < 31)
+        act(A("LT"), A("P4", 0, 128), Act.Ln, bias=2.0 ** -64)
+        act(A("PEN"), A("LT"), Act.Relu, bias=A("BC", 0, 1), scale=-2000.0)
 
-    def leave(t):
-        tt(A("LV"), A("FL"), A("P1", 0, 256), Op.is_lt)
-        mms(A("P3", 0, 256), [(A("TRN" if t == 2 else "TRQ"), A("LV")), (A("I8K"), A("LV"))])
-        for h in range(2):
-            mm(A("P5", 128 * h, 128 * h + 128), A("LV", 128 * h, 128 * h + 128), A("TRI"))
-        for h in range(2):
-            mms(A("P4", 128 * h, 128 * h + 128), [(A("O2H", 128 * h, 128 * h + 128), A("I16")), (A("LV", 128 * h, 128 * h + 128), A("IBIG"))])
-        mm(A("P2", 0, 256), A("BO"), A("LV"))
-        for x in range(16):
-            mm(A("P2", 256 + x, 512 - 15 + x, 16), A("NLN" if t == 2 else "NLQ"), A("LV", 16 * x, 16 * x + 16))
-        for x in range(16):
-            mm(A("P7", 0, 16), ez("EZ", x), A("LV", 16 * x, 16 * x + 16), x == 0, x == 15)
-        tt(A("E1"), A("NPL" if t == 2 else "NQ"), A("P3", 0, 256), Op.add)
-        tt(A("DE"), A("E1", 0, 128), A("E1", 128, 256), Op.subtract)
-        tt(A("ES"), A("DE"), A("SW"), Op.mult)
-        for hv in range(2):
-            es = A("ES", 64 * hv, 64 * hv + 64)
-            tt(A("E2", 128 * hv, 128 * hv + 64), A("E1", 64 * hv, 64 * hv + 64), es, Op.subtract)
-            tt(A("E2", 128 * hv + 64, 128 * hv + 128), A("E1", 128 + 64 * hv, 192 + 64 * hv), es, Op.add)
-        ts(A("E3"), A("E2"), 4096.0, Op.min)
-        act(A("EHI"), A("E3"))
-        ts(A("BT"), A("P5", 0, 256), float(2 ** 23 + 2 ** 19 + 2 ** 15 + 2 ** 11), Op.mult)
-        tt(A("ELO"), A("E3"), A("EHI"), Op.subtract)
-        dmas([("y", ROW("WDE", 0, 0, 4096), A("EHI")), ("y", ROW("WDE", 1, 0, 4096), A("ELO"))])
+    def leave():
+        ts(A("GO"), A("P3", 0, 256), 0.0, Op.is_gt)
+        tt(A("P3", 256, 512), A("O2"), A("P3", 0, 256), Op.max)
+        scan(A("CN"), A("R01"), A("GO"), 0.0, Op.mult, Op.add)
+        ts(A("BT"), A("CN"), float(2 ** 23 + 2 ** 19 + 2 ** 15 + 2 ** 11), Op.mult)
         ts(A("BT2"), A("BT"), 2 ** 23 + 2 ** 20 + 2 ** 17 + 2 ** 14, Op.bitwise_and)
-        tt(A("Y"), A("BT2"), A("P4", 0, 256), Op.add)
+        tt(A("Y", 0, 256), A("BT2"), A("P3", 256, 512), Op.add)
 
-    def move_slots(chunks, both=False):
-        for m in chunks:
-            o, i = A("GE", 256 + 1024 * m, 1280 + 1024 * m), IND(A("WDE"), A("WL", 64 * m, 64 * m + 64))
-            if both and m > 4:
-                cp(o, i)
-            else:
-                act(o, i)
-
-    def new_entries():
-        scatter(A("GS"), A("SU"), A("AT"))
-
-    def clear_entries():
-        dmas([("y", ROW("GS", i, 256 + 2048 * c, 2304 + 2048 * c), (ROW("ZRO", i, 0, 2048)[0], A("ZRO")[1] + A("KK")[1])) for c in range(4) for i in range(2)])
-
-    def read_slots(n, j, start):
-        mms(A("P%d" % (4 + j), 0, 128), [(ez("EZ", s), A(n, 256 + 2048 * j + s, 2304 + 2048 * j - 15 + s, 16)) for s in range(16)], start, not start)
+    def new_places():
+        mms(A("P2", 384, 512), [(A("IB"), A("CN", 0, 128)), (A("INB"), A("CN", 128, 256)), (A("IN8K"), A("GO", 0, 128)), (A("I8K"), A("GO", 128, 256))], more=True)
+        mm(A("P0", 0, 256), A("IB"), A("CHI"), True, False)
+        mm(A("P0", 0, 128), A("IM128"), A("SW"), False, False)
+        mm(A("P0", 128, 256), A("I128"), A("SW"), False, True)
+        tt(A("T2"), A("P2", 384, 512), A("SW"), Op.mult)
+        mms(A("P0", 256, 512), [(A("IB"), A("CLO")), (A("INB"), A("CN")), (A("I8K"), A("GO"))], True, False)
+        mm(A("P0", 256, 384), A("IF"), A("T2"), False, False)
+        mm(A("P0", 384, 512), A("INF"), A("T2"), False, True)
+        act(A("EHL"), A("P0", 0, 512))
+        to_window(2, A("EHL", 0, 256), A("EHL", 256, 512))
 
     def close_up(j):
-        th, d = 2.0 ** (23 - 3 * j), 1 << j
-        ts(A("P5", 0, 256), A("Y"), th, Op.is_lt)
-        ts(A("MV", 0, 256), A("Y"), th, Op.subtract, 0.0, Op.max)
-        tt(A("P5", 256, 512), A("Y"), A("P5", 0, 256), Op.mult)
-        tt(A("Y"), A("P5", 256, 512), A("MV", d, 256 + d), Op.max)
+        act(A("P1", 0, 272), A("Y"), Act.Abs, bias=A("BC", 1 + j, 2 + j))
+        tt(A("Y", 0, 256), A("Y", 0, 256), A("P1", 1 << j, 256 + (1 << j)), Op.min)
 
-    def logs():
+    def winners():
+        left = A("CN", 15, 256, 16)
+        tt(A("K2"), A("PEN"), A("LT"), Op.subtract)
+        ts(A("PF"), left, 0.5, Op.is_lt, 1.0e4, Op.mult)
+        scan(A("KM"), A("RK"), A("K2"), 0.0, Op.add, Op.min)
+        ts(A("LZ"), left, -1024.0, Op.mult, 256.0 + 16384.0, Op.add)
+        tt(A("PM"), A("KM", 7, 128, 8), A("PF"), Op.add)
+        ts(A("PN"), A("PM"), 0.5 / LN2, Op.mult, 479.6, Op.add)
+        tt(A("SUI"), A("PN"), A("JC"), Op.min)
+        ts(A("CV"), A("SUI"), 511.5, Op.is_ge, -768.0, Op.mult)
+        tt(A("Z1"), A("SUI"), A("LZ"), Op.add)
+        tt(A("ZW"), A("Z1"), A("CV"), Op.add)
+        tt(A("XK"), IND(A("ZW"), A("LC", 0, 16)), A("K1K"), Op.subtract)
+
+    def append():
+        tt(A("O"), A("Y", 0, 256), A("XK"), Op.min)
+
+    def new_entries():
+        ts(A("LEN"), A("CN", 15, 256, 16), -1.0, Op.mult, 16.0, Op.add)
+        cp(A("SU"), A("SUI"))
+        tt(A("AT"), IND(A("LEN"), A("LC", 0, 16)), A("CAT"), Op.min)
+        scatter(A("PT"), A("SU"), A("AT"))
+        mms(A("P7"), [(A("I8K"), A("CMP", 16, 528)), (A("IN8K"), A("CMP", 15, 527))], True, False)
+        mms(A("P7", 0, 512, 16), [(A("I8K"), A("CMP", 15, 527, 16)), (A("IN8K"), A("ONEB"))], False, False)
         for c in range(4):
-            for h in range(8):
-                cg = 8 * c + h
-                w0 = 112 + 128 * cg - 16 * h
-                mm(A("P6", c, 128 - 3 + c, 4), A("AH", w0, w0 + 128), A("BL", cg, 1024 - 31 + cg, 32), h == 0, h == 7)
-        act(A("LT"), A("P6", 0, 128), Act.Ln, bias=2.0 ** -64)
-        act(A("PEN"), A("LT"), Act.Relu, bias=A("BC", 4, 5), scale=-2000.0)
+            mm(A("P7", 128 * c, 128 * c + 128), A("PT", 128 * c, 128 * c + 128), A("BO"), False, c == 3)
+        act(A("XS"), A("P7"), bias=8192.0 + 2048.0)
 
-    def winners(t):
-        tt(A("K1"), A("CK"), A("LT"), Op.subtract)
-        tt(A("K2"), A("K1"), A("PEN"), Op.add)
-        scan(A("KM"), A("RK"), A("K2"), 0.0, Op.max, Op.min)
-        tt(A("PM"), A("KM", 3, 64, 4), A("KM", 67, 128, 4), Op.min)
-        ts(A("PF"), A("P7", 0, 16), 0.5, Op.is_lt, 1.0e4, Op.mult)
-        tt(A("PM"), A("PM"), A("PF"), Op.max)
-        ts(A("PMI"), A("PM"), 0.5 / LN2, Op.mult, 512.0, Op.min)
-        cp(A("PU"), A("PMI"))
-        act(A("G2"), IND(A("T2"), A("PU")))
-        for x in range(16):
-            mm(A("P6", 16 * x, 16 * x + 16), A("BOP"), A("G2", x, 256 - 15 + x, 16))
-        for x in range(16):
-            mm(A("P6", 256, 272), ez("EZW", x), A("G2", x, 256 - 15 + x, 16), x == 0, x == 15)
+    def new_slots(out, lo, hi):
+        tt(A("NL", lo, hi), A("P6", lo, hi), A("XS", lo, hi), Op.min)
+        for c in range(lo, hi, 128):
+            mm(A("P5", c, c + 128), A("NL", c, c + 128), A("I16"), more=c + 128 < hi)
+        ts(A(out, lo, hi), A("P5", lo, hi), 2048.0, Op.add, 4096.0, Op.min)
 
-    def settle(t):
-        for h in range(2):
-            mm(A("P1", 128 * h, 128 * h + 128), A("Y", 128 * h, 128 * h + 128), A("IF"))
-        ts(A("EQ"), A("P2", 0, 256), A("KC16", 0, 1), Op.is_equal)
-        tt(A("AC"), A("EQ"), A("P6", 0, 256), Op.mult)
-        tt(A("O"), A("P1", 0, 256), A("AC"), Op.max)
-        if t < 2:
-            persons()
-        tt(A("JD"), A("P6", 256, 272), A("JC"), Op.max)
-        ts(A("SU"), A("JD"), -3840.0, Op.add)
-        tt(A("AT"), A("ATN" if t == 2 else "ATQ"), A("P2", 256, 512), Op.add)
-
+    constants()
     for t in range(3):
+        lists(t)
+        for c in (0, 2, 1, 3):
+            wants(c)
+            minima(c)
+        decide()
+        exchange()
         if t:
-            lists(t)
-            wants()
-            shared_gather()
-            move_slots(range(3, 6))
-            new_entries()
-            for j in range(4):
-                read_slots("GS", j, True)
-        minima(0)
-        minima(2)
-        shared_clip()
-        if t:
-            move_slots(range(6, 8))
-        pair_limits()
-        minima(1)
-        if t:
-            read_slots("GE", 0, False)
-            read_slots("GE", 1, False)
-        decide(0, t)
-        minima(3)
-        if t:
-            read_slots("GE", 2, False)
-            read_slots("GE", 3, False)
-        else:
-            slot_windows()
-        decide(1, t)
-        if t:
-            for j in range(4):
-                cp(A("WL", 128 * j, 128 * j + 128), A("P%d" % (4 + j), 0, 128))
-        else:
-            late_constants()
-        slot_scores()
+            new_slots("WL", 0, 512)
+        for c in range(4):
+            by_slot("GS", 2 * c)
+            by_slot("GS", 2 * c + 1)
+            read("P4", "GS", "RS", c)
+            read("P5", "GS", "RS%d" % t, c)
         roll(t)
-        after_exchange(t)
         thresholds(t)
-        clear_entries()
+        for c in range(4):
+            limits(t, c)
         applicants()
-        leave(t)
-        logs()
-        close_up(0)
-        close_up(1)
-        winners(t)
-        close_up(2)
-        close_up(3)
-        settle(t)
-        del shared[:]
+        leave()
+        new_places()
+        winners()
+        for j in range(4):
+            close_up(j)
+        append()
+        new_entries()
         if t < 2:
-            move_slots(range(3))
+            iota(A("PT", 0, 512), [[0, 512]], 0)
+        for c in range(4):
+            by_slot("GE", 2 * c)
+            by_slot("GE", 2 * c + 1)
+            read("P6", "GE", "RE", c)
 
-    new_entries()
-
-    def read(n, m, start, stop):
-        mms(A("P%d" % m, 0, 64), [(ez("EZ", s), A(n, 256 + 1024 * m + s, 1280 + 1024 * m - 15 + s, 16)) for s in range(16)], start, stop)
-
-    move_slots(range(8), True)
-    early = (0, 1, 2, 3)
-    for m in early:
-        read("GE", m, True, False)
-    for m in range(8):
-        read("GS", m, m not in early, m in early)
-    for m in (5, 4, 6, 7):
-        read("GE", m, False, True)
-    ts(A("OE"), A("O"), 255.5, Op.is_lt, 512.0, Op.mult)
-    ts(A("EE"), A("O"), -256.0, Op.add)
-    tt(A("YO"), A("EE"), A("OE"), Op.max)
-    dmas([("s", nat("YON", c), A("YO", 64 * c, 64 * c + 64)) for c in range(4)])
-    dmas([("s", ext(T.yoc[:]), (T.YON[:], [("YON", 0, 1, 1)]))])
+    ts(A("YA"), A("O"), 255.5, Op.is_lt, 512.0, Op.mult)
+    ts(A("YB"), A("O"), -256.0, Op.add, 0.0, Op.max)
     for h in range(2):
-        for m in range(4 * h, 4 * h + 4):
-            if m & 1:
-                cp(A("YQ", 64 * m, 64 * m + 64), A("P%d" % m, 0, 64))
-            else:
-                act(A("YQ", 64 * m, 64 * m + 64), A("P%d" % m, 0, 64))
-        dmas([("y", ext(T.yq[:, 256 * h:256 * h + 256]), A("YQ", 256 * h, 256 * h + 256))])
+        mms((T.P2[:, 0:8, h, :], [("P2", 0, 256, 1)]),
+            [(A("OUT%d%d" % (h, b)), A(n, 128 * b, 128 * b + 128)) for n in ("YA", "YB") for b in range(2)], more=h < 1)
+    turn(A("YP"), A("P2", 0, 256))
+    for y in range(8):
+        copy("vs", A("YO", y, 256, 8), A("YP", 32 * y, 32 * y + 32))
+    dmas("y", [(ext(T.yoc[:]), A("YO"))])
+    for lo in (0, 256):
+        new_slots("YQ", lo, lo + 256)
+        dmas("y", [(ext(T.yq[:, lo:lo + 256]), A("YQ", lo, lo + 256))])
+    issue_all()
     for s in sorted(cnt):
         if known["g"].get(s, 0) < cnt[s]:
             g.wait_ge(T.sem[s], cnt[s])

@@ -21,20 +21,19 @@ def _decl(dtype, spec):
 
 _decl(BF, "XT:4096 WT:528 MT:528 WG:4096 D0:4096 D1:4096 MG:4096 WD:4112 GS:8192 GE:8192 TT:512 PT:768 AH:1536 ZB:1024 CMP:528 "
           "EZ4:144 EZM:144 EZP:144 IB:128 INB:128 I8K:128 IN8K:128 I24:128 IN24:128 IPEN:128 I128:128 IM128:128 BO:128 "
-          "RS:8 RS0:8 RS1:8 RS2:8 RE:8 RW:8 CADD:64 R01:256 BIG:16 KILO:64 ONEB:32 CAT:256 CHI:256 CLO:256 "
-          "FHI:256 FLO:256 EHL:512 EM:256 SW:128 GO:256 CN:256 AT:256 B0L:512")
-_decl(FH, "I16:128 IN16:128 I2:128 I37:128 L32:128 C1:256 KC0:256 KC1:256 KC2:256 OP:256 ZS:128 NL:512 YA:256 YB:256 "
+          "RS:8 RS0:8 RS1:8 RS2:8 RE:8 RW:8 CADD:64 R01:256 BIG:16 KILO:256 ONEB:32 CAT:256 CHI:256 CLO:256 "
+          "FHI:256 FLO:256 EHL:512 EM:256 SW:128 GO:256 CN:256 AT:256 BL:512 YC:512")
+_decl(FH, "UF:64 I16:128 IN16:128 I2:128 I37:128 L32:128 C1:256 KC0:256 KC1:256 KC2:256 OP:256 ZS:128 NL:512 YA:256 YB:256 "
           "IN00:128 IN01:128 IN10:128 IN11:128 OUT00:128 OUT01:128 OUT10:128 OUT11:128")
-_decl(I4, "OCN:256 QW:512 THI:16 QI:8 KI:8 PI:32 H:512 HA:512 TM:32 UH:32 UL:32 SUI:16 BT:256 BT2:256 WSI:32 WSJ:32")
-_decl(U2, "LR:32 LC:32 OU:256 OU2:256 HU:512 SU:16 WL:512")
+_decl(I4, "OCN:256 QW:512 THI:16 QI:8 KI:8 PI:32 H:512 HA:512 TM:32 UU:64 SUI:16 BT:256 BT2:256 WSI:32 WSJ:32")
+_decl(U2, "LC:32 OU:256 OU2:256 HU:512 SU:16 WL:512")
 _decl(F4, "IF:128 INF:128 BOF:128 I24F:128 IN24F:128 ZF:128 TB:128 TI:128 TJ:128 TK:128 ONE:256 TA:256 TC:16 TD:256 TE:256 TH:256 VV:256 VW:256 "
-          "KC:8 KB:8 KW:16 WR:8 THF:8 LIM:8 JW:8 BC:8 G0:8 RMX:512 RMN:512 RK:128 JC:16 XC:512 YC:512 K1K:256 NPB:256 YP:256 YO:256 YQ:512 "
+          "KC:8 KB:8 KW:16 WR:8 THF:8 LIM:8 JW:8 BC:8 G0:8 RMX:512 RMN:512 RK:128 JC:16 XC:512 K1K:256 NPB:256 YP:256 YO:256 YQ:512 "
           "T1:256 EE:256 FS:128 O2:256 T2:128 SMX:512 PMN:512 MYK:32 KK:64 K:32 KD:32 KD1:32 L4P:32 W4:32 HOLD:32 AP:32 TU:32 "
           "LT:128 PEN:128 K2:128 KM:128 PF:16 PM:16 PN:16 LZ:16 CV:16 Z1:16 ZW:16 LEN:16 XK:256 Y:272 XS:512 LAND0:128 LAND1:128 LAND2:128")
 SCRATCH["O"] = ("sbuf", [128, 16, 16], FH)
 SCRATCH["O16"] = ("sbuf", [128, 8, 2, 16], FH)
 SCRATCH["OE"] = ("sbuf", [128, 8, 2, 16], FH)
-SCRATCH["BL"] = ("sbuf", [128, 16, 2, 32], BF)
 SCRATCH["P0"] = ("psum", [128, 32, 16], F4)
 SCRATCH["P2"] = ("psum", [128, 16, 2, 16], F4)
 for _n in ("P1", "P3", "P4", "P5", "P6", "P7"):
@@ -46,8 +45,10 @@ SEMAPHORES = ["qv", "qs", "qt", "qg", "sent"] + ["arr%d" % t for t in range(3)] 
 CYCLE, PE_CYCLE, GATHER, GATHER2, SCATTER = 0.83, 0.44, 1.05, 1.5, 3.2
 CALL = {"v": 40.0, "s": 220.0, "g": 0.0}
 BANK, PE_OUT = 95.0, 400.0
-HOP, DMA, SEND, REMOTE = 100.0, 1500.0, 2000.0, 1000.0
-SLACK, SECOND = 300.0, 300.0
+HOP, DMA, SEND, REMOTE = 200.0, 1500.0, 2000.0, 1000.0
+
+
+SHARED = ((2,), (), ())
 
 
 def _bank(name):
@@ -86,8 +87,8 @@ def rank_program(g, core, T, topo):
     def M(ap, *names):
         return (ap, [(n, 0, 512, 1) for n in names])
 
-    def whole(o):
-        return M(o[0], o[1][0][0])
+    def whole(o, c=3):
+        return (o[0], o[1] + [("open" + o[1][0][0], 0 if c == 3 else c, c + 1, 1)])
 
     def IND(win, off):
         return (win[0].indirect(off[0]), win[1] + off[1], True)
@@ -124,7 +125,7 @@ def rank_program(g, core, T, topo):
 
     def step(queues, time, reads, writes, go, later=0.0):
         k = len(steps)
-        steps.append({"queues": queues, "time": time, "later": later, "issue": go,
+        steps.append({"queue": queues, "time": time, "later": later, "issue": go,
                       "before": sorted(set(p for p, _ in before(seen, queues, reads, writes)))})
         note(seen, queues, reads, writes, k)
 
@@ -138,16 +139,16 @@ def rank_program(g, core, T, topo):
                 known[q][k2] = v2
         known[q][sem] = n
 
-    def deps(q, reads, writes):
+    def deps(q, reads, writes, adds=False):
         best = {}
         for tok, q2 in before(hist, q, reads, writes):
-            if not (q == "t" and q2 == q and tok[1] > cnt.get("qt", 0)):
+            if not (q2 == q == "t" and (adds or tok[1] > cnt.get("qt", 0))):
                 best[tok[0]] = max(best.get(tok[0], 0), tok[1])
         for s in sorted(best):
             need(q, (s, best[s]))
 
-    def issue(q, call, reads, writes, inc=True):
-        deps(q, reads, writes)
+    def issue(q, call, reads, writes, inc=True, adds=False):
+        deps(q, reads, writes, adds)
         sem = SEM[q]
         inst = call()
         tok = (sem, cnt.get(sem, 0) + 1)
@@ -159,9 +160,9 @@ def rank_program(g, core, T, topo):
             snap[tok] = s
         note(hist, q, reads, writes, tok)
 
-    def run(q, call, reads, writes, time):
+    def run(q, call, reads, writes, time, line=()):
         time += CALL[q] + (BANK if any(_bank(r[0]) for r in reads + writes) else 0.0)
-        step(q, time, reads, writes, lambda on: issue(on, call, reads, writes))
+        step(q, time, reads, writes + list(line), lambda on: issue(on, call, reads, writes))
 
     def R(*ops):
         out = []
@@ -186,7 +187,7 @@ def rank_program(g, core, T, topo):
     def tt(o, a, b, op):
         n = size(o)
         time = GATHER2 * n if picked(a) else cycles(n if _bank(a[1][0][0]) or _bank(b[1][0][0]) else 2 * n)
-        run("v", lambda: g.vector.tensor_tensor(o[0], a[0], b[0], op), R(a, b), o[1], time)
+        run("v", lambda: g.vector.tensor_tensor(o[0], a[0], b[0], op), R(a, b), o[1], time, [("lineD", 0, 1, 1)] if n == 1024 else [])
 
     def ts(o, a, s1, op0, s2=None, op1=None):
         if op1 is None:
@@ -221,7 +222,8 @@ def rank_program(g, core, T, topo):
                 issue(on, lambda: g.vector.tensor_copy(o[0], a[0]), a[1], o[1])
             else:
                 issue(on, lambda: g.scalar.activation(o[0], a[0], Act.Copy), a[1], o[1])
-        step(queues, 60.0 + GATHER * size(o) if picked(a) else CALL[queues[0]] + cycles(size(o)), a[1], o[1], go)
+        step(queues, 60.0 + GATHER * size(o) if picked(a) else CALL[queues[0]] + cycles(size(o)), a[1],
+             o[1] + ([("line" + queues + o[1][0][0], 0, 1, 1)] if picked(a) else []), go)
 
     def gather(o, win, off, queues="sv"):
         copy(queues, o, IND(win, off))
@@ -235,7 +237,7 @@ def rank_program(g, core, T, topo):
 
             def go(on):
                 for i, (o, l, r, start, stop, _) in enumerate(mine):
-                    issue(on, lambda: g.tensor.matmul(o[0], l[0], r[0], start, stop), R(l, r), o[1], stop or i == len(mine) - 1)
+                    issue(on, lambda: g.tensor.matmul(o[0], l[0], r[0], start, stop), R(l, r), o[1][:1], stop or i == len(mine) - 1, not start)
             step("t", sum(m[5] for m in mine), sum([R(m[1], m[2]) for m in mine], []), sum([m[0][1] for m in mine], []), go, PE_OUT)
 
     def mms(o, pairs, start=True, stop=True, more=False, cut=False):
@@ -272,37 +274,37 @@ def rank_program(g, core, T, topo):
 
     def issue_all():
         n = len(steps)
-        way = [0.0] * n
         after = [[] for _ in steps]
         for k, s in enumerate(steps):
             for p in s["before"]:
                 after[p].append(k)
+
+        def gap(p, k):
+            same = steps[p]["queue"] == steps[k]["queue"]
+            return 0.0 if same and steps[p]["queue"] == "t" else steps[p]["later"] + (0.0 if same else HOP)
+
+        way = [0.0] * n
         for k in range(n - 1, -1, -1):
-            s = steps[k]
-            way[k] = s["time"] + s["later"] + max([way[x] + (0.0 if steps[x]["queues"] == s["queues"] else HOP) for x in after[k]] + [0.0])
+            way[k] = steps[k]["time"] + max([way[x] + gap(k, x) for x in after[k]] + [steps[k]["later"]])
         way[:loads] = [1.0e9 - k for k in range(loads)]
-        free = {q: 0.0 for q in Q}
-        ends, done, on, left = {}, {}, {}, [len(s["before"]) for s in steps]
+        at, busy, left = {}, {q: [] for q in Q}, [len(s["before"]) for s in steps]
         ready = [k for k in range(n) if not left[k]]
-
-        def start(k, q):
-            return max([free[q]] + [ends[p] if on[p] == q == "t" else done[p] + (0.0 if on[p] == q else HOP) for p in steps[k]["before"]])
-
         while ready:
-            can = [(start(k, q) + (SECOND if q != steps[k]["queues"][0] else 0.0), k, q) for k in ready for q in steps[k]["queues"]]
-            first, _, q = min(can)
-            mine = [c for c in can if c[2] == q]
-            best = max([c for c in mine if c[0] <= first + SLACK], key=lambda c: (way[c[1]], -c[1]))
-            fits = [c for c in mine if c[0] + steps[c[1]]["time"] <= best[0]]
-            k = max(fits, key=lambda c: (way[c[1]], -c[1]))[1] if fits else best[1]
-            ends[k] = free[q] = start(k, q) + steps[k]["time"]
-            done[k], on[k] = free[q] + steps[k]["later"], q
-            steps[k]["issue"](q)
+            k = min(ready, key=lambda x: (-way[x], x))
             ready.remove(k)
+            time, line, i = steps[k]["time"], busy[steps[k]["queue"]], 0
+            t = max([0.0] + [at[p] + steps[p]["time"] + gap(p, k) for p in steps[k]["before"]])
+            while i < len(line) and line[i][0] < t + time:
+                t = max(t, line[i][1])
+                i += 1
+            line.insert(i, (t, t + time))
+            at[k] = t
             for x in after[k]:
                 left[x] -= 1
                 if not left[x]:
                     ready.append(x)
+        for k in sorted(range(n), key=lambda x: (at[x], x)):
+            steps[k]["issue"](steps[k]["queue"])
 
     def ext(ap):
         return (ap, [])
@@ -364,9 +366,10 @@ def rank_program(g, core, T, topo):
         fill(A("WT", 0, 16), 0.0)
         cp(A("WL"), A("QW"))
         ts(A("WR", 0, 1), kc, 4.0, Op.is_equal, 2048.0, Op.mult)
-        for lo in range(0, 4112, 1024):
-            hi = min(lo + 1024, 4112)
-            act(A("WD", lo, hi), A("ZB", 0, hi - lo), Act.Identity, bias=A("WR", 0, 1))
+        for lo in range(0, 4096, 1024):
+            act(A("WD", lo, lo + 1024), A("ZB"), Act.Identity, bias=A("WR", 0, 1))
+        ts(A("WR", 4, 5), kc, 4.5, Op.is_gt, -65536.0, Op.mult)
+        ts(A("WD", 4096, 4112), A("ZB", 0, 16), A("WR", 4, 5), Op.add, A("WR", 0, 1), Op.add)
         ts(A("KB", 0, 1), kc, 1.5, Op.is_lt)
         ts(A("RS"), A("BOF", 0, 128, 16), A("KB", 0, 1), Op.mult)
         for t in range(3):
@@ -388,7 +391,6 @@ def rank_program(g, core, T, topo):
         iota(A("VW"), [[-16, 16], [0, 16]], 4096)
         iota(A("JC"), [[16, 16]], 512)
         iota(A("PI"), [[1, 32]], 0, 0, False)
-        iota(A("TI", 0, 32), [[0, 16], [16, 2]], 0)
         iota(A("R01"), [[0, 256]], 1)
         fill(A("R01", 0, 256, 16), 0.0)
         fill(A("BIG"), 65536.0)
@@ -417,14 +419,13 @@ def rank_program(g, core, T, topo):
         ts(A("TE"), A("TD"), A("KW", 8, 9), Op.is_equal)
         tt(A("TE"), A("TE"), A("VV"), Op.mult)
         tt(A("CAT"), A("TE"), A("TH"), Op.add)
-        ts(A("LR"), A("TI", 0, 32), kc, Op.add)
         cp(A("LC"), A("PI"))
         ts(A("JC"), A("JC"), kc, Op.add)
         fill(A("TI", 64, 128), 0.25)
         scan(A("TJ", 0, 64), A("TI", 64, 128), A("ZF", 0, 64), 2.0 ** 65, Op.mult, Op.max)
-        for j in range(2):
-            tt(A("TJ", 64, 128), A("TJ", 0, 64), A("IF", 64 * j, 64 * j + 64), Op.mult)
-            total(A("JW", j, j + 1), A("TJ", 64, 128))
+        tt(A("TK", 0, 64), A("IF", 0, 64), A("IF", 64, 128), Op.add)
+        tt(A("TJ", 64, 128), A("TJ", 0, 64), A("TK", 0, 64), Op.mult)
+        total(A("JW", 0, 1), A("TJ", 64, 128))
         fill(A("RK"), -128.0 * 2 * LN2)
         fill(A("RK", 4, 128, 8), 320.0 * 2 * LN2)
         fill(A("RK", 0, 128, 8), 1.0e6)
@@ -458,18 +459,30 @@ def rank_program(g, core, T, topo):
         ts(A("EM"), o, 255.5, Op.is_lt)
 
     def wants(c):
-        gather(A("WG", 1024 * c, 1024 * c + 1024), A("WT"), A("OU", 64 * c, 64 * c + 64))
+        gather(A("WG", 1024 * c, 1024 * c + 1024), A("WT"), A("OU", 64 * c, 64 * c + 64), "s")
 
-    def minima(c):
+    def minima(c, shared):
         w, lo = A("WG", 1024 * c, 1024 * c + 1024), 1024 * c
-        d, pair = whole(A("P2", 64 * c, 64 * c + 64)), whole(A("P3", 64 * (c & 1), 64 * (c & 1) + 64))
+        d, pair = whole(A("P2", 64 * c, 64 * c + 64), c), whole(A("P3", 64 * (c & 1), 64 * (c & 1) + 64))
         tt(A("D0", lo, lo + 1024), IND(A("XT"), A("HU", 64 * c, 64 * c + 64)), w, Op.min)
-        mms(A("P1", 64 * c, 64 * c + 64), [(A("IB"), A("CADD"))] + rows("EZ4", "D0", lo, 1024), more=True)
-        mms(d, rows("EZM", "D0", lo, 1024), True, False)
+        mms(A("P1", 64 * c, 64 * c + 64), [(A("IB"), A("CADD"))] + rows("EZ4", "D0", lo, 1024))
         mms(pair, [(A("IPEN"), A("EM", 64 * c, 64 * c + 64))] + rows("EZM", "D0", lo, 1024), c < 2, False, cut=True)
-        tt(A("D1", lo, lo + 1024), IND(A("XT"), A("HU", 256 + 64 * c, 320 + 64 * c)), w, Op.min)
-        mms(pair, rows("EZ4", "D1", lo, 1024), False, c > 1, True, cut=True)
-        mms(d, rows("EZ4", "D1", lo, 1024), False, True)
+        early = rows("EZM", "D0", lo, 1024)
+        if c == 3:
+            mms(d, early, True, False, cut=True)
+            early = []
+        if c in shared:
+            gather(A("D1", lo, lo + 1024), A("XT"), A("HU", 256 + 64 * c, 320 + 64 * c), "s")
+            for b, bank in enumerate(("P4", "P5")):
+                part = (lo + 512 * b, lo + 512 * b + 512)
+                mms(A(bank), [(A("IB"), A("WG", *part)), (A("INB"), A("D1", *part))])
+                act(A("D1", *part), A(bank), Act.Relu)
+            late = rows("EZ4", "WG", lo, 1024) + rows("EZM", "D1", lo, 1024)
+        else:
+            tt(A("D1", lo, lo + 1024), IND(A("XT"), A("HU", 256 + 64 * c, 320 + 64 * c)), w, Op.min)
+            late = rows("EZ4", "D1", lo, 1024)
+        mms(pair, late, False, c > 1, True, cut=True)
+        mms(d, early + late, c < 3, True)
 
     def to_window(row, hi, lo):
         dmas("y", [(PART("WD", row + i, 128, 16, 0, 4096), x) for i, x in enumerate((hi, lo))])
@@ -494,8 +507,8 @@ def rank_program(g, core, T, topo):
         ts(A("OU2"), A("P0", 256, 512), -240.0, Op.add)
         act(A("O2"), A("P0", 256, 512))
 
-    def by_slot(n, m):
-        gather(A(n, 1024 * m, 1024 * m + 1024), A("WD"), A("WL", 64 * m, 64 * m + 64))
+    def by_slot(n, m, both):
+        gather(A(n, 1024 * m, 1024 * m + 1024), A("WD"), A("WL", 64 * m, 64 * m + 64), "sv"[m & 1] if both else "s")
 
     def read(bank, n, sel, c):
         for s in range(16):
@@ -542,42 +555,51 @@ def rank_program(g, core, T, topo):
         act(A("MT", 16, 528), A("P3"))
 
     def limits(t, c):
-        w, f = (64 * c, 64 * c + 64), 64 * (c & 1)
-        gather(A("MG", 1024 * c, 1024 * c + 1024), A("MT"), A("OU2", *w))
-        o = A("P3", *w)
-        mms(o, [(A("IN24"), A("FHI", *w)), (A("IN24"), A("FLO", *w)), (A("IN24F" if c > 1 else "I24F"), A("FS", f, f + 64))], True, False)
-        if not c & 1:
-            mm(A("P3", 64 * c + 16 * t, 64 * c + 16 * t + 1), A("I24"), A("BIG", 0, 1), False, False)
-        mms(o, rows("EZP", "MG", 1024 * c, 1024) + [(A("IB"), A("KILO"))], False, True)
+        w = (64 * c, 64 * c + 64)
+        gather(A("MG", 1024 * c, 1024 * c + 1024), A("MT"), A("OU2", *w), "sv"[c & 1])
+        if c == 0:
+            mms(whole(A("P1", 0, 256)), [(A("IN24"), A("FHI")), (A("IN24"), A("FLO"))], True, False)
+            for b, l in enumerate(("I24F", "IN24F")):
+                mm(whole(A("P1", 128 * b, 128 * b + 128)), A(l), A("FS"), False, False)
+            mm(whole(A("P1", 16 * t, 256, 128)), A("I24"), A("BIG", 0, 2), False, False, cut=True)
+        mms(whole(A("P1", *w)), rows("EZP", "MG", 1024 * c, 1024), False, False, cut=c < 3)
+        if c == 3:
+            mm(whole(A("P1", 0, 256)), A("IB"), A("KILO"), False, True)
 
     def applicants():
-        ts(A("KD1"), A("KD"), 1.0, Op.max)
         tt(A("HOLD"), A("K"), A("MYK"), Op.is_equal)
         tt(A("TU"), A("K"), A("W4"), Op.add)
-        tt(A("CMP", 16, 528), IND(A("KD1"), A("LC")), A("PMN"), Op.is_le)
+        tt(A("CMP", 16, 528), IND(A("KD"), A("LC")), A("PMN"), Op.is_le)
         tt(A("AP"), A("HOLD"), A("CMP", 31, 528, 16), Op.is_gt)
         tt(A("TM"), A("TU"), A("AP"), Op.mult)
-        ts(A("UL"), A("TM"), 2, Op.arith_shift_right, 15, Op.bitwise_and)
-        ts(A("UH"), A("TM"), 6, Op.arith_shift_right, 0x20F, Op.bitwise_and)
-        tt(A("B0L"), IND(A("UL"), A("LR")), A("YC"), Op.is_equal)
-        tt(A("AH", 512, 1024), IND(A("UH"), A("LR")), A("XC"), Op.is_equal)
+        ts(A("UU", 0, 32), A("TM"), 6, Op.arith_shift_right, 0x20F, Op.bitwise_and)
+        ts(A("UU", 32, 64), A("TM"), 2, Op.arith_shift_right, 15, Op.bitwise_and)
+        cp(A("UF"), A("UU"))
+        for x in range(16):
+            mm(A("P6", 32 * x, 32 * x + 32), A("I16"), A("UF", 0, 32), more=x < 15)
+        mm(A("P7"), A("INB"), A("YC"), True, False)
+        for y in range(16):
+            mm(A("P7", 32 * y, 32 * y + 32), A("I16"), A("UF", 32, 64), False, y == 15)
+        tt(A("AH", 512, 1024), A("P6"), A("XC"), Op.is_equal)
+        ts(A("BL"), A("P7"), 0.0, Op.is_equal, A("JW", 0, 1), Op.mult)
         for j in range(2):
-            ts(M(T.BL[:, :, j, :], "BL%d" % j), A("B0L"), A("JW", j, j + 1), Op.mult)
-        for c in range(4):
-            for x in range(8):
-                w0, a = 512 - 512 * (x & 1) + 8 * c + x, 32 * (x >> 1)
-                mm(PART("P4", a, a + 32, 1, c, 128 - 3 + c, 4), A("AH", w0, w0 + 1024 - 31, 32), M(T.BL[:, :, :, 8 * c + x], "BL0", "BL1"),
-                   not x & 1, bool(x & 1), 8 * c + x < 31)
+            for c in range(4):
+                for x in range(8):
+                    w0, a, col = 512 - 512 * (x & 1) + 8 * c + x, 32 * (x >> 1), 4 * j + c
+                    reg = ("P4", 512, 640, 1) if (j, c, x) == (1, 0, 0) else ("P4", 512 + 128 * j + a + col, 513 + 128 * j + a + col, 1)
+                    mm((PART("P4", a, a + 32, 1, col, 128 - 7 + col, 8)[0], [reg]),
+                       PART("AH", 64 * j, 64 * j + 64, 1, w0, w0 + 1024 - 31, 32), PART("BL", 64 * j, 64 * j + 64, 1, 8 * c + x, 512, 32),
+                       not x & 1, bool(x & 1), 32 * j + 8 * c + x < 63)
         act(A("LT"), A("P4", 0, 128), Act.Ln, bias=2.0 ** -64)
         act(A("PEN"), A("LT"), Act.Relu, bias=A("BC", 0, 1), scale=-2000.0)
 
     def leave():
-        ts(A("GO"), A("P3", 0, 256), 0.0, Op.is_gt)
-        tt(A("P3", 256, 512), A("O2"), A("P3", 0, 256), Op.max)
+        ts(A("GO"), A("P1", 0, 256), 0.0, Op.is_gt)
+        tt(A("P1", 256, 512), A("O2"), A("P1", 0, 256), Op.max)
         scan(A("CN"), A("R01"), A("GO"), 0.0, Op.mult, Op.add)
         ts(A("BT"), A("CN"), float(2 ** 23 + 2 ** 19 + 2 ** 15 + 2 ** 11), Op.mult)
         ts(A("BT2"), A("BT"), 2 ** 23 + 2 ** 20 + 2 ** 17 + 2 ** 14, Op.bitwise_and)
-        tt(A("Y", 0, 256), A("BT2"), A("P3", 256, 512), Op.add)
+        tt(A("Y", 0, 256), A("BT2"), A("P1", 256, 512), Op.add)
 
     def new_places():
         mms(A("P2", 384, 512), [(A("IB"), A("CN", 0, 128)), (A("INB"), A("CN", 128, 256)), (A("IN8K"), A("GO", 0, 128)), (A("I8K"), A("GO", 128, 256))], more=True)
@@ -592,8 +614,8 @@ def rank_program(g, core, T, topo):
         to_window(2, A("EHL", 0, 256), A("EHL", 256, 512))
 
     def close_up(j):
-        act(A("P1", 0, 272), A("Y"), Act.Abs, bias=A("BC", 1 + j, 2 + j))
-        tt(A("Y", 0, 256), A("Y", 0, 256), A("P1", 1 << j, 256 + (1 << j)), Op.min)
+        act(A("P3", 0, 272), A("Y"), Act.Abs, bias=A("BC", 1 + j, 2 + j))
+        tt(A("Y", 0, 256), A("Y", 0, 256), A("P3", 1 << j, 256 + (1 << j)), Op.min)
 
     def winners():
         left = A("CN", 15, 256, 16)
@@ -634,14 +656,14 @@ def rank_program(g, core, T, topo):
         lists(t)
         for c in (0, 2, 1, 3):
             wants(c)
-            minima(c)
+            minima(c, SHARED[t])
         decide()
         exchange()
         if t:
             new_slots("WL", 0, 512)
         for c in range(4):
-            by_slot("GS", 2 * c)
-            by_slot("GS", 2 * c + 1)
+            by_slot("GS", 2 * c, True)
+            by_slot("GS", 2 * c + 1, True)
             read("P4", "GS", "RS", c)
             read("P5", "GS", "RS%d" % t, c)
         roll(t)
@@ -659,8 +681,8 @@ def rank_program(g, core, T, topo):
         if t < 2:
             iota(A("PT", 0, 512), [[0, 512]], 0)
         for c in range(4):
-            by_slot("GE", 2 * c)
-            by_slot("GE", 2 * c + 1)
+            by_slot("GE", 2 * c, t == 2)
+            by_slot("GE", 2 * c + 1, t == 2)
             read("P6", "GE", "RE", c)
 
     ts(A("YA"), A("O"), 255.5, Op.is_lt, 512.0, Op.mult)
@@ -670,7 +692,7 @@ def rank_program(g, core, T, topo):
             [(A("OUT%d%d" % (h, b)), A(n, 128 * b, 128 * b + 128)) for n in ("YA", "YB") for b in range(2)], more=h < 1)
     turn(A("YP"), A("P2", 0, 256))
     for y in range(8):
-        copy("vs", A("YO", y, 256, 8), A("YP", 32 * y, 32 * y + 32))
+        copy("v", A("YO", y, 256, 8), A("YP", 32 * y, 32 * y + 32))
     dmas("y", [(ext(T.yoc[:]), A("YO"))])
     for lo in (0, 256):
         new_slots("YQ", lo, lo + 256)

@@ -19,19 +19,21 @@ def _decl(dtype, spec):
     SCRATCH[pool] = ("sbuf", [128, at], dtype)
 
 
-_decl(BF, "XT:4096 WT:528 MT:528 WG:4096 D0:4096 D1:4096 MG:4096 WD:4112 GS:8192 GE:8192 TT:512 PT:768 AH:1536 ZB:1024 CMP:528 "
-          "EZ4:144 EZM:144 EZP:144 IB:128 INB:128 I8K:128 IN8K:128 I24:128 IN24:128 IPEN:128 I128:128 IM128:128 BO:128 "
-          "RS:8 RS0:8 RS1:8 RS2:8 RE:8 RW:8 CADD:64 R01:256 BIG:16 KILO:256 ONEB:32 CAT:256 CHI:256 CLO:256 "
-          "FHI:256 FLO:256 EHL:512 EM:256 SW:128 GO:256 CN:256 AT:256 BL:512 YC:512")
-_decl(FH, "UF:64 I16:128 IN16:128 I2:128 I37:128 L32:128 C1:256 KC0:256 KC1:256 KC2:256 OP:256 ZS:128 NL:512 YA:256 YB:256 "
+_decl(BF, "XT:4096 WT:528 MT:528 WG:4096 D0:4096 D1:4096 MG:4096 WD:4112 GS:8192 GE:8192 TT:512 PT:768 AH:1536 CMP:528 "
+          "EZ4:432 IB:128 INB:128 I8K:128 IN8K:128 I24:128 IN24:128 IPEN:128 I128:128 IM128:128 BO:128 "
+          "RS:8 RS0:8 RS1:8 RS2:8 RE:8 RW:8 CADD:64 R01:256 BIG:16 ONEB:32 CAT:256 CHI:256 CLO:256 "
+          "FHI:256 FLO:256 EHL:512 EM:256 SW:128 GO:256 CN:256 AT:256 BL:512 B0:512 YC:512")
+_decl(FH, "UF:64 I16:128 IN16:128 I37:128 L32:128 KT:768 OP:256 ZS:128 NL:512 YA:256 YB:256 "
           "IN00:128 IN01:128 IN10:128 IN11:128 OUT00:128 OUT01:128 OUT10:128 OUT11:128")
 _decl(I4, "OCN:256 QW:512 THI:16 QI:8 KI:8 PI:32 H:512 HA:512 TM:32 UU:64 SUI:16 BT:256 BT2:256 WSI:32 WSJ:32")
 _decl(U2, "LC:32 OU:256 OU2:256 HU:512 SU:16 WL:512")
-_decl(F4, "IF:128 INF:128 BOF:128 I24F:128 IN24F:128 ZF:128 TB:128 TI:128 TJ:128 TK:128 ONE:256 TA:256 TC:16 TD:256 TE:256 TH:256 VV:256 VW:256 "
-          "KC:8 KB:8 KW:16 WR:8 THF:8 LIM:8 JW:8 BC:8 G0:8 RMX:512 RMN:512 RK:128 JC:16 XC:512 K1K:256 NPB:256 YP:256 YO:256 YQ:512 "
-          "T1:256 EE:256 FS:128 O2:256 T2:128 SMX:512 PMN:512 MYK:32 KK:64 K:32 KD:32 KD1:32 L4P:32 W4:32 HOLD:32 AP:32 TU:32 "
+_decl(F4, "IF:128 INF:128 I24F:128 IN24F:128 ZF:128 TB:128 TI:128 TJ:128 TK:128 ONE:256 TA:256 TC:16 TC2:16 TD:256 TE:256 TH:256 VV:256 VW:256 "
+          "KC:8 KB:8 KW:16 WR:8 LIM:8 JW:8 BC:8 G0:8 RMX:512 RMN:512 RK:128 JC:16 XC:512 K1K:256 CF:512 C1:256 YP:256 YO:256 YQ:512 "
+          "EE:256 FS:128 T2:128 SMX:512 PMN:512 MYK:32 KK:64 K:32 KD:32 L4P:32 W4:32 HOLD:32 AP:32 TU:32 "
           "LT:128 PEN:128 K2:128 KM:128 PF:16 PM:16 PN:16 LZ:16 CV:16 Z1:16 ZW:16 LEN:16 XK:256 Y:272 XS:512 LAND0:128 LAND1:128 LAND2:128")
 SCRATCH["O"] = ("sbuf", [128, 16, 16], FH)
+SCRATCH["T1"] = ("sbuf", [128, 16, 16], F4)
+SCRATCH["NP8"] = ("sbuf", [128, 16, 16], F4)
 SCRATCH["O16"] = ("sbuf", [128, 8, 2, 16], FH)
 SCRATCH["OE"] = ("sbuf", [128, 8, 2, 16], FH)
 SCRATCH["P0"] = ("psum", [128, 32, 16], F4)
@@ -42,13 +44,12 @@ for _n in ("P1", "P3", "P4", "P5", "P6", "P7"):
     WHERE[_n] = (_n, 0)
 SEMAPHORES = ["qv", "qs", "qt", "qg", "sent"] + ["arr%d" % t for t in range(3)] + ["d%d" % i for i in range(20)]
 
-CYCLE, PE_CYCLE, GATHER, GATHER2, SCATTER = 0.83, 0.44, 1.05, 1.5, 3.2
+CYCLE, PE_CYCLE, GATHER, GATHER2, SCATTER = 0.83, 0.44, 1.3, 1.3, 3.2
 CALL = {"v": 40.0, "s": 220.0, "g": 0.0}
 BANK, PE_OUT = 95.0, 400.0
-HOP, DMA, SEND, REMOTE = 200.0, 1500.0, 2000.0, 1000.0
-
-
-SHARED = ((2,), (), ())
+HOP, DMA, SEND, REMOTE = 130.0, 1500.0, 1500.0, 500.0
+AHEAD, SLACK, PATIENCE = 400.0, 100.0, 0.6
+SHARED = ((1, 2), (), ())
 
 
 def _bank(name):
@@ -71,9 +72,9 @@ def rank_program(g, core, T, topo):
             return (T.P0[:, lo // 16:hi // 16, :], [(n, lo, hi, 1)])
         if n == "P2":
             return (T.P2[:, lo // 32:hi // 32], [(n, lo, hi, 1)])
-        if n == "O":
+        if n in ("O", "T1", "NP8"):
             hi = 256 if hi is None else hi
-            return (T.O[:, lo // 16:hi // 16, :], [(n, lo, hi, 1)])
+            return (T[n][:, lo // 16:hi // 16, :], [(n, lo, hi, 1)])
         hi = WIDTH[n] if hi is None else hi
         buf, c0 = WHERE[n]
         ap = T[buf][:, c0 + lo:c0 + hi] if st == 1 else T[buf][:, c0 + lo:c0 + hi:st]
@@ -87,8 +88,8 @@ def rank_program(g, core, T, topo):
     def M(ap, *names):
         return (ap, [(n, 0, 512, 1) for n in names])
 
-    def whole(o, c=3):
-        return (o[0], o[1] + [("open" + o[1][0][0], 0 if c == 3 else c, c + 1, 1)])
+    def whole(o):
+        return (o[0], o[1] + [("open" + o[1][0][0], 0, 1, 1)])
 
     def IND(win, off):
         return (win[0].indirect(off[0]), win[1] + off[1], True)
@@ -123,11 +124,11 @@ def rank_program(g, core, T, topo):
                     keep.append(e)
             log[n] = keep + [((lo, hi, st), tok, q, True)]
 
-    def step(queues, time, reads, writes, go, later=0.0):
+    def step(q, time, reads, writes, go, later=0.0):
         k = len(steps)
-        steps.append({"queue": queues, "time": time, "later": later, "issue": go,
-                      "before": sorted(set(p for p, _ in before(seen, queues, reads, writes)))})
-        note(seen, queues, reads, writes, k)
+        steps.append({"queue": q, "time": time, "later": later, "issue": go,
+                      "before": sorted(set(p for p, _ in before(seen, q, reads, writes)))})
+        note(seen, q, reads, writes, k)
 
     def need(q, token):
         sem, n = token
@@ -216,17 +217,15 @@ def rank_program(g, core, T, topo):
     def act(o, a, func=Act.Copy, bias=0.0, scale=1.0):
         run("s", lambda: g.scalar.activation(o[0], a[0], func, bias=val(bias), scale=val(scale)), R(a, bias, scale), o[1], cycles(size(o)))
 
-    def copy(queues, o, a):
+    def gather(o, win, off, q):
+        a = IND(win, off)
+
         def go(on):
             if on == "v":
                 issue(on, lambda: g.vector.tensor_copy(o[0], a[0]), a[1], o[1])
             else:
                 issue(on, lambda: g.scalar.activation(o[0], a[0], Act.Copy), a[1], o[1])
-        step(queues, 60.0 + GATHER * size(o) if picked(a) else CALL[queues[0]] + cycles(size(o)), a[1],
-             o[1] + ([("line" + queues + o[1][0][0], 0, 1, 1)] if picked(a) else []), go)
-
-    def gather(o, win, off, queues="sv"):
-        copy(queues, o, IND(win, off))
+        step(q, 60.0 + GATHER * size(o), a[1], o[1] + [("line" + q + o[1][0][0], 0, 1, 1)], go)
 
     def mm(o, l, r, start=True, stop=True, more=False, cut=False):
         wide = WHERE.get(l[1][0][0], ("",))[0] == "pool_" + F4
@@ -254,6 +253,9 @@ def rank_program(g, core, T, topo):
 
     def aff(o, a, pattern, op, fillv, base, cm):
         run("g", lambda: g.affine_select(o[0], a[0], pattern, op, fillv, base, cm), a[1], o[1], 170.0 + 2 * CYCLE * size(o))
+
+    def const(o, v):
+        aff(o, A("ZF", 0, size(o)), [[0, size(o)]], Op.not_equal, v, 0, 0)
 
     ndma = [0]
 
@@ -287,22 +289,23 @@ def rank_program(g, core, T, topo):
         for k in range(n - 1, -1, -1):
             way[k] = steps[k]["time"] + max([way[x] + gap(k, x) for x in after[k]] + [steps[k]["later"]])
         way[:loads] = [1.0e9 - k for k in range(loads)]
-        at, busy, left = {}, {q: [] for q in Q}, [len(s["before"]) for s in steps]
-        ready = [k for k in range(n) if not left[k]]
+        at, free, left = {}, {q: 0.0 for q in Q}, [len(s["before"]) for s in steps]
+        ready = {k: 0.0 for k in range(n) if not left[k]}
         while ready:
-            k = min(ready, key=lambda x: (-way[x], x))
-            ready.remove(k)
-            time, line, i = steps[k]["time"], busy[steps[k]["queue"]], 0
-            t = max([0.0] + [at[p] + steps[p]["time"] + gap(p, k) for p in steps[k]["before"]])
-            while i < len(line) and line[i][0] < t + time:
-                t = max(t, line[i][1])
-                i += 1
-            line.insert(i, (t, t + time))
-            at[k] = t
+            can = {k: max(t, free[steps[k]["queue"]]) for k, t in ready.items()}
+            q = steps[min(can, key=lambda k: (can[k] - (0.0 if steps[k]["queue"] == "v" else AHEAD), k))]["queue"]
+            mine = sorted([k for k in can if steps[k]["queue"] == q], key=lambda k: (-way[k], k))
+            first = min(can[k] for k in mine)
+            best = [k for k in mine if can[k] <= first + SLACK][0]
+            best = [k for k in mine if can[k] <= can[best] + PATIENCE * steps[best]["time"]][0]
+            k = ([k for k in mine if can[k] + steps[k]["time"] <= can[best]] + [best])[0]
+            at[k] = can[k]
+            free[q] = at[k] + steps[k]["time"]
+            del ready[k]
             for x in after[k]:
                 left[x] -= 1
                 if not left[x]:
-                    ready.append(x)
+                    ready[x] = max(at[p] + steps[p]["time"] + gap(p, x) for p in steps[x]["before"])
         for k in sorted(range(n), key=lambda x: (at[x], x)):
             steps[k]["issue"](steps[k]["queue"])
 
@@ -310,7 +313,8 @@ def rank_program(g, core, T, topo):
         return (ap, [])
 
     def ez(n, k):
-        return A(n, 15 - k, 143 - k)
+        at = 144 * ("EZ4", "EZM", "EZP").index(n)
+        return A("EZ4", at + 15 - k, at + 143 - k)
 
     def rows(sel, n, lo, width):
         return [(ez(sel, r), A(n, lo + r, lo + width - 15 + r, 16)) for r in range(16)]
@@ -323,39 +327,46 @@ def rank_program(g, core, T, topo):
 
     q1, kc, one = A("QI", 0, 1), A("KC", 0, 1), A("ONE", 0, 128)
 
+    def to_window(row, hi, lo):
+        dmas("y", [(PART("WD", row + i, 128, 16, 0, 4096), x) for i, x in enumerate((hi, lo))])
+
     def constants():
         iota(q1, [[0, 1]], 0, 1, False)
         fill(A("ONE"), 1.0)
-        fill(A("ZB"), 0.0)
         fill(A("ZF"), 0.0)
+        iota(A("XC"), [[1, 16], [0, 32]], 512)
         ts(A("KI", 0, 1), q1, 15, Op.bitwise_and)
         cp(kc, A("KI", 0, 1))
-        for name, v in (("IF", 1.0), ("INF", -1.0), ("I24F", 2.0 ** 24), ("IN24F", -2.0 ** 24), ("IB", 1.0), ("INB", -1.0), ("I8K", 8192.0),
+        for name, v in (("IF", 1.0), ("I24F", 2.0 ** 24), ("IN24F", -2.0 ** 24), ("IB", 1.0), ("INB", -1.0), ("I8K", 8192.0),
                         ("IN8K", -8192.0), ("I24", 2.0 ** 24), ("IN24", -2.0 ** 24), ("IPEN", -65536.0), ("I128", 128.0), ("IM128", -128.0),
-                        ("I16", 1.0), ("IN16", -1.0), ("I2", 2.0), ("I37", 37.0)):
+                        ("I16", 1.0), ("IN16", -1.0), ("I37", 37.0)):
             aff(A(name), A("ZF"), [[-1, 128]], Op.not_equal, v, 0, 1)
         for h in range(2):
             for b in range(2):
                 aff(A("IN%d%d" % (h, b)), A("ZF"), [[-32, 4], [1000, 2], [-2, 16]], Op.not_equal, 1.0, -b - 1000 * h, 1)
                 aff(A("OUT%d%d" % (h, b)), A("ZF"), [[-32, 4], [-1, 16], [1000, 2]], Op.not_equal, 1.0, -16 * h - 1000 * b, 1)
         aff(A("TB"), one, [[-16, 8], [0, 16]], Op.is_ge, 0.0, 0, 1)
-        aff(A("BOF"), A("TB"), [[16, 8], [0, 16]], Op.is_ge, 0.0, 15, -1)
         aff(A("BO"), A("TB"), [[16, 8], [0, 16]], Op.is_ge, 0.0, 15, -1)
-        for name, v in (("EZ4", 4.0), ("EZM", -4.0), ("EZP", 2.0 ** 24)):
-            fill(A(name), 0.0)
-            ts(A(name, 15, 143, 16), A("BOF", 0, 128, 16), v, Op.mult)
+        ones = A("BO", 0, 128, 16)
+        fill(A("EZ4", 0, 432), 0.0)
+        for i, v in enumerate((4.0, -4.0, 2.0 ** 24)):
+            ts(A("EZ4", 144 * i + 15, 144 * i + 143, 16), ones, v, Op.mult)
         fill(PART("L32", 0, 64), 1.0 / 32)
         for t in range(3):
-            fill(PART("KC%d" % t, 0, 32), 77.0 * t - 1280.0)
-            fill(PART("KC%d" % t, 32, 64), -15.0 / 32)
-        fill(A("CADD"), float(7 - rank))
+            fill(PART("KT", 0, 32, 1, 256 * t, 256 * t + 256), 77.0 * t - 1280.0)
+        fill(PART("KT", 32, 64), -15.0 / 32)
+        iota(A("CADD"), [[0, 64]], 7 - rank)
         iota(A("TA"), [[1, 256]], 0)
         iota(A("TC"), [[2, 16]], 17)
         ts(A("KW", 0, 1), kc, 16.0, Op.mult)
         ts(A("KW", 1, 2), kc, 32.0, Op.mult)
-        ts(A("NPB"), A("TA"), 0.0625, Op.mult, A("KW", 0, 1), Op.add)
-        fill(A("C1"), -495.0)
-        ts(A("C1", 0, 256, 16), A("TC"), A("KW", 1, 2), Op.add)
+        act(A("NP8"), A("TA"), Act.Identity, bias=A("KW", 1, 2), scale=0.125)
+        fill(A("C1"), -247.5)
+        ts(A("C1", 0, 256, 16), A("TC"), 0.5, Op.mult, A("KW", 0, 1), Op.add)
+        tt(A("CF", 0, 256), A("C1"), A("NP8"), Op.mult)
+        for b in range(2):
+            act(A("CF", 256 + 128 * b, 384 + 128 * b), A("CF", 128 - 128 * b, 256 - 128 * b))
+        fill(A("T1"), 0.0)
         for y in range(8):
             ts(A("OP", 32 * y, 32 * y + 32), A("OCN", y, 256, 8), 256.0, Op.add)
         turn(M(T.O16[:], "O16"), A("OP"))
@@ -363,81 +374,77 @@ def rank_program(g, core, T, topo):
         for b in range(2):
             mms(A("P1", 128 * b, 128 * b + 128), [(A("IN%d%d" % (h, b)), M(T[n][:, :, h, :], n)) for n in ("O16", "OE") for h in range(2)], more=b < 1)
         cp(A("O"), A("P1", 0, 256))
-        fill(A("WT", 0, 16), 0.0)
+        const(A("WT", 0, 16), 0.0)
         cp(A("WL"), A("QW"))
+
+        def row(o, a, r, v):
+            aff(o, a, [[-16, 8]], Op.not_equal, v, -r, 1)
+
+        row(A("TI", 0, 8), A("ZF", 0, 8), 0, 1.0)
+        row(A("RS"), A("TI", 0, 8), 1, 1.0)
+        for t in range(3):
+            row(A("RS%d" % t), A("RS"), 5 + t, 1.0)
+        row(A("TI", 8, 16), A("ZF", 0, 8), 2, -1.0)
+        row(A("TI", 16, 24), A("TI", 8, 16), 3, 1.0)
+        row(A("RE"), A("TI", 16, 24), 4, 1.0)
         ts(A("WR", 0, 1), kc, 4.0, Op.is_equal, 2048.0, Op.mult)
         for lo in range(0, 4096, 1024):
-            act(A("WD", lo, lo + 1024), A("ZB"), Act.Identity, bias=A("WR", 0, 1))
+            act(A("WD", lo, lo + 1024), A("XT", lo, lo + 1024), Act.Identity, bias=A("WR", 0, 1), scale=0.0)
+        iota(A("WR", 1, 4), [[1, 3]], 5)
+        ts(A("WR", 5, 8), A("WR", 1, 4), kc, Op.is_equal, -65536.0, Op.mult)
         ts(A("WR", 4, 5), kc, 4.5, Op.is_gt, -65536.0, Op.mult)
-        ts(A("WD", 4096, 4112), A("ZB", 0, 16), A("WR", 4, 5), Op.add, A("WR", 0, 1), Op.add)
-        ts(A("KB", 0, 1), kc, 1.5, Op.is_lt)
-        ts(A("RS"), A("BOF", 0, 128, 16), A("KB", 0, 1), Op.mult)
         for t in range(3):
-            ts(A("KB", 1 + t, 2 + t), kc, 5.0 + t, Op.is_equal)
-            ts(A("WR", 1 + t, 2 + t), A("KB", 1 + t, 2 + t), -65536.0, Op.mult, A("WR", 0, 1), Op.add)
-            ts(A("WD", 16 * t, 4096, 128), A("ONE", 0, 32), A("WR", 1 + t, 2 + t), Op.mult)
-            ts(A("KB", 4 + t, 5 + t), A("KB", 1 + t, 2 + t), A("KB", 0, 1), Op.add)
-            ts(A("RS%d" % t), A("BOF", 0, 128, 16), A("KB", 4 + t, 5 + t), Op.mult)
+            ts(A("WD", 16 * t, 4096, 128), A("ZF", 0, 32), A("WR", 5 + t, 6 + t), Op.add, A("WR", 0, 1), Op.add)
+        ts(A("WD", 4096, 4112), A("ZF", 0, 16), A("WR", 4, 5), Op.add, A("WR", 0, 1), Op.add)
         iota(A("RMN"), [[0, 512]], -1000000)
-        fill(A("RMN", 0, 512, 16), 1.0e6)
-        iota(A("RMX"), [[0, 512]], 1000000)
-        fill(A("RMX", 0, 512, 16), -1.0e6)
-        iota(A("XC"), [[1, 16], [0, 32]], 512)
+        const(A("RMN", 0, 512, 16), 1.0e6)
+        act(A("RMX"), A("RMN"), scale=-1.0)
+        act(A("R01"), A("RMX", 0, 256), Act.Relu, scale=1.0e-6)
         iota(A("YC"), [[1, 16], [0, 32]], 0)
-        iota(A("K1K"), [[0, 16], [1024, 16]], 0)
         iota(A("TD"), [[0, 16], [1, 16]], 0)
-        iota(A("CLO"), [[0, 16], [1, 16]], 0)
+        act(A("K1K"), A("TD"), scale=1024.0)
+        act(A("CLO"), A("TD"))
         iota(A("VV"), [[16, 16], [256, 16]], -4096)
         iota(A("VW"), [[-16, 16], [0, 16]], 4096)
-        iota(A("JC"), [[16, 16]], 512)
+        iota(A("TC2"), [[16, 16]], 512)
         iota(A("PI"), [[1, 32]], 0, 0, False)
-        iota(A("R01"), [[0, 256]], 1)
-        fill(A("R01", 0, 256, 16), 0.0)
-        fill(A("BIG"), 65536.0)
-        fill(A("KILO"), -1024.0)
-        fill(A("ONEB"), 1.0)
-        ts(A("KW", 2, 3), kc, 2.0, Op.is_equal, -2.0, Op.mult)
-        ts(A("KW", 3, 4), kc, 1.5, Op.is_gt)
-        ts(A("KW", 4, 5), kc, 4.5, Op.is_lt, A("KW", 3, 4), Op.mult)
-        ts(A("KW", 5, 6), A("KW", 2, 3), A("KW", 4, 5), Op.add)
-        ts(A("RE"), A("BOF", 0, 128, 16), A("KW", 5, 6), Op.mult)
-        ts(A("RW"), A("BOF", 0, 128, 16), A("KW", 0, 1), Op.mult)
-        for lo in (0, 1024):
-            iota(A("AH", lo, lo + 512), [[0, 512]], 0)
-        iota(A("PT", 0, 512), [[0, 512]], 0)
-        iota(A("TT"), [[0, 512]], 0)
-        fill(A("MT", 0, 16), 131072.0)
-        fill(A("Y", 256, 272), 2.0 ** 25)
-        fill(A("CMP", 0, 16), 0.0)
-        for j in range(4):
-            fill(A("BC", 1 + j, 2 + j), -2.0 ** (23 - 3 * j))
+        iota(A("BIG"), [[0, 16]], 65536)
+        iota(A("ONEB"), [[0, 32]], 1)
+        act(A("RW"), ones, scale=A("KW", 0, 1))
+        for o in (A("AH", 0, 512), A("AH", 1024, 1536), A("PT", 0, 512), A("TT")):
+            iota(o, [[0, 512]], 0)
+        iota(A("MT", 0, 16), [[0, 16]], 131072)
+        iota(A("CMP", 0, 16), [[0, 16]], 0)
+        const(A("Y", 256, 272), 2.0 ** 25)
         ts(A("KW", 6, 7), kc, -256.0, Op.mult)
-        ts(A("CHI"), A("VW"), A("KW", 6, 7), Op.add)
+        act(A("CHI"), A("VW"), Act.Identity, bias=A("KW", 6, 7))
         ts(A("KW", 7, 8), kc, 0.5, Op.is_lt, 16.0, Op.mult)
         ts(A("KW", 8, 9), kc, -1.0, Op.add, A("KW", 7, 8), Op.add)
         ts(A("TH"), A("TD"), kc, Op.is_equal, 64.0, Op.mult)
         ts(A("TE"), A("TD"), A("KW", 8, 9), Op.is_equal)
         tt(A("TE"), A("TE"), A("VV"), Op.mult)
-        tt(A("CAT"), A("TE"), A("TH"), Op.add)
+        mms(A("P7", 0, 256), [(A("IF"), A("TE")), (A("IF"), A("TH"))])
+        act(A("CAT"), A("P7", 0, 256))
         cp(A("LC"), A("PI"))
-        ts(A("JC"), A("JC"), kc, Op.add)
-        fill(A("TI", 64, 128), 0.25)
+        const(A("BC", 0, 1), 2.0 ** -63.2)
+        act(A("BC", 1, 2), A("BC", 0, 1), Act.Ln)
+        act(A("BC", 2, 3), A("BC", 1, 2), scale=2000.0)
+        act(A("JC"), A("TC2"), Act.Identity, bias=kc)
+        const(A("TI", 64, 128), 0.25)
         scan(A("TJ", 0, 64), A("TI", 64, 128), A("ZF", 0, 64), 2.0 ** 65, Op.mult, Op.max)
         tt(A("TK", 0, 64), A("IF", 0, 64), A("IF", 64, 128), Op.add)
         tt(A("TJ", 64, 128), A("TJ", 0, 64), A("TK", 0, 64), Op.mult)
         total(A("JW", 0, 1), A("TJ", 64, 128))
-        fill(A("RK"), -128.0 * 2 * LN2)
-        fill(A("RK", 4, 128, 8), 320.0 * 2 * LN2)
-        fill(A("RK", 0, 128, 8), 1.0e6)
-        fill(A("BC", 0, 1), -2000.0 * 63.2 * LN2)
-        ts(A("KW", 9, 10), kc, 0.5, Op.is_lt)
-        cp(A("THF", 0, 1), A("THI", 0, 1))
-        ts(A("LIM", 0, 1), A("THF", 0, 1), 4.0, Op.mult, float(rank), Op.add)
-        ts(A("G0"), A("BOF", 0, 128, 16), A("KW", 9, 10), Op.mult, A("LIM", 0, 1), Op.mult)
+        ts(A("JW", 1, 2), A("JW", 0, 1), -1.0, Op.mult)
+        const(A("RK"), -128.0 * 2 * LN2)
+        const(A("RK", 4, 128, 8), 320.0 * 2 * LN2)
+        const(A("RK", 0, 128, 8), 1.0e6)
+        ts(A("LIM", 0, 1), A("THI", 0, 1), 4.0, Op.mult, float(rank), Op.add)
+        act(A("G0"), A("TI", 0, 8), scale=A("LIM", 0, 1))
         for c in range(4):
             mm(A("P6", 8 * c, 8 * c + 8), one, A("G0"), more=True)
             mm(A("P6", 32 + 8 * c, 40 + 8 * c), A("WT", 16 + 128 * c, 144 + 128 * c), A("RW"), more=c < 3)
-        cp(A("L4P"), A("P6", 0, 32))
+        act(A("L4P"), A("P6", 0, 32))
         ts(A("WSI"), A("P6", 32, 64), 255.0, Op.add)
         ts(A("WSJ"), A("WSI"), 255, Op.bitwise_and)
         ts(A("W4"), A("WSJ"), 4.0, Op.mult, 32768.0, Op.add)
@@ -445,11 +452,13 @@ def rank_program(g, core, T, topo):
     def lists(t):
         o = A("O")
         ts(A("OU"), o, -240.0, Op.add)
-        mm(A("P0", 0, 256), A("I16"), A("C1"), True, False)
-        mm((T.P0[:, 0:16, 1:16], [("P0", 0, 256, 1)]), A("I2"), (T.O[:, :, 0:15], o[1]), False, True, True)
-        mms(A("P0", 256, 512), [(PART("L32", 0, 64), PART("KC%d" % t, 0, 64)), (A("I37"), o)])
-        tt(A("T1"), A("NPB"), A("P0", 0, 256), Op.mult)
-        tt(A("H", 0, 256), A("T1"), A("P0", 256, 512), Op.add)
+        mm(whole(A("P0", 0, 512)), A("IF"), A("CF"), True, False)
+        for b in range(2):
+            mm(whole(A("P0", 256 * b, 256 * b + 256)), PART("L32", 0, 64), PART("KT", 0, 64, 1, 256 * t, 256 * t + 256), False, False, cut=b == 1)
+        for b in range(2):
+            mm(whole(A("P0", 256 * b, 256 * b + 256)), A("I37"), o, False, b == 1)
+        tt((T.T1[:, :, 1:16], [("T1", 0, 256, 1)]), (T.NP8[:, :, 1:16], [("NP8", 0, 256, 1)]), (T.O[:, :, 0:15], o[1]), Op.mult)
+        tt(A("H", 0, 256), A("T1"), A("P0", 0, 256), Op.add)
         ts(A("HA", 0, 256), A("H", 0, 256), 4095, Op.bitwise_and)
         cp(A("HU", 0, 256), A("HA", 0, 256))
         for b in range(2):
@@ -463,33 +472,29 @@ def rank_program(g, core, T, topo):
 
     def minima(c, shared):
         w, lo = A("WG", 1024 * c, 1024 * c + 1024), 1024 * c
-        d, pair = whole(A("P2", 64 * c, 64 * c + 64), c), whole(A("P3", 64 * (c & 1), 64 * (c & 1) + 64))
+        d = whole(A("P2", 64 * c, 64 * c + 64))
+        if c == 0:
+            mm(whole(A("P2", 0, 256)), A("IPEN"), A("EM"), True, False, cut=True)
         tt(A("D0", lo, lo + 1024), IND(A("XT"), A("HU", 64 * c, 64 * c + 64)), w, Op.min)
-        mms(A("P1", 64 * c, 64 * c + 64), [(A("IB"), A("CADD"))] + rows("EZ4", "D0", lo, 1024))
-        mms(pair, [(A("IPEN"), A("EM", 64 * c, 64 * c + 64))] + rows("EZM", "D0", lo, 1024), c < 2, False, cut=True)
-        early = rows("EZM", "D0", lo, 1024)
-        if c == 3:
-            mms(d, early, True, False, cut=True)
-            early = []
+        mms(A("P1", 64 * c, 64 * c + 64), [(A("IB"), A("CADD"))] + rows("EZ4", "D0", lo, 1024), more=True)
+        mms(d, rows("EZM", "D0", lo, 1024), False, False, cut=True)
         if c in shared:
             gather(A("D1", lo, lo + 1024), A("XT"), A("HU", 256 + 64 * c, 320 + 64 * c), "s")
+            mms(d, rows("EZ4", "WG", lo, 1024), False, False, cut=True)
             for b, bank in enumerate(("P4", "P5")):
                 part = (lo + 512 * b, lo + 512 * b + 512)
                 mms(A(bank), [(A("IB"), A("WG", *part)), (A("INB"), A("D1", *part))])
                 act(A("D1", *part), A(bank), Act.Relu)
-            late = rows("EZ4", "WG", lo, 1024) + rows("EZM", "D1", lo, 1024)
         else:
             tt(A("D1", lo, lo + 1024), IND(A("XT"), A("HU", 256 + 64 * c, 320 + 64 * c)), w, Op.min)
-            late = rows("EZ4", "D1", lo, 1024)
-        mms(pair, late, False, c > 1, True, cut=True)
-        mms(d, early + late, c < 3, True)
-
-    def to_window(row, hi, lo):
-        dmas("y", [(PART("WD", row + i, 128, 16, 0, 4096), x) for i, x in enumerate((hi, lo))])
+            for x in shared if c == 3 else ():
+                mms(whole(A("P2", 64 * x, 64 * x + 64)), rows("EZM", "D1", 1024 * x, 1024), False, False, cut=True)
+            mms(d, rows("EZ4", "D1", lo, 1024), False, c == 3, cut=True)
 
     def decide():
         f = A("P1", 256, 512)
-        ts(A("SW"), A("P3", 0, 128), 0.0, Op.is_gt)
+        ts(A("EE", 0, 128), A("P2", 128, 256), -1.0, Op.mult)
+        tt(A("SW"), A("P2", 0, 128), A("EE", 0, 128), Op.is_gt)
         for b in range(2):
             tt(A("EE", 128 * b, 128 * b + 128), A("P2", 128 * b, 128 * b + 128), A("SW"), Op.mult)
         tt(f, A("EE"), A("P1", 0, 256), Op.add)
@@ -497,18 +502,28 @@ def rank_program(g, core, T, topo):
         tt(A("FLO"), f, A("FHI"), Op.subtract)
         to_window(0, A("FHI"), A("FLO"))
 
+    def exchanged(o, more):
+        mm(o, A("I16"), A("O"), True, False)
+        mm(A("P0", 256, 384), A("IN16"), A("ZS"), False, False)
+        mm(A("P0", 384, 512), A("I16"), A("ZS"), False, not more)
+        if more:
+            mms(o, more, False, True)
+
     def exchange():
         mms(A("P0", 0, 128), [(A("I16"), A("O", 0, 128)), (A("IN16"), A("O", 128, 256))], more=True)
         mms(A("P2", 256, 384), [(A(l), A(n, lo, lo + 128)) for l, lo in (("IB", 0), ("INB", 128)) for n in ("FHI", "FLO")])
         tt(A("ZS"), A("P0", 0, 128), A("SW"), Op.mult)
         tt(A("FS"), A("P2", 256, 384), A("SW"), Op.mult)
-        for b, l in enumerate(("IN16", "I16")):
-            mms(A("P0", 256 + 128 * b, 384 + 128 * b), [(A("I16"), A("O", 128 * b, 128 * b + 128)), (A(l), A("ZS"))], more=b < 1)
+        exchanged(A("P0", 256, 512), [])
         ts(A("OU2"), A("P0", 256, 512), -240.0, Op.add)
-        act(A("O2"), A("P0", 256, 512))
+        mm(A("P3", 0, 256), A("IB"), A("CHI"), True, False)
+        mm(A("P3", 0, 128), A("IM128"), A("SW"), False, False)
+        mm(A("P3", 128, 256), A("I128"), A("SW"), False, True)
+        act(A("EHL", 0, 256), A("P3", 0, 256))
 
-    def by_slot(n, m, both):
-        gather(A(n, 1024 * m, 1024 * m + 1024), A("WD"), A("WL", 64 * m, 64 * m + 64), "sv"[m & 1] if both else "s")
+    def by_slot(n, c, queues):
+        for m in (2 * c, 2 * c + 1):
+            gather(A(n, 1024 * m, 1024 * m + 1024), A("WD"), A("WL", 64 * m, 64 * m + 64), queues[m & 1])
 
     def read(bank, n, sel, c):
         for s in range(16):
@@ -562,9 +577,7 @@ def rank_program(g, core, T, topo):
             for b, l in enumerate(("I24F", "IN24F")):
                 mm(whole(A("P1", 128 * b, 128 * b + 128)), A(l), A("FS"), False, False)
             mm(whole(A("P1", 16 * t, 256, 128)), A("I24"), A("BIG", 0, 2), False, False, cut=True)
-        mms(whole(A("P1", *w)), rows("EZP", "MG", 1024 * c, 1024), False, False, cut=c < 3)
-        if c == 3:
-            mm(whole(A("P1", 0, 256)), A("IB"), A("KILO"), False, True)
+        mms(whole(A("P1", *w)), rows("EZP", "MG", 1024 * c, 1024), False, c == 3, cut=c < 3)
 
     def applicants():
         tt(A("HOLD"), A("K"), A("MYK"), Op.is_equal)
@@ -576,12 +589,15 @@ def rank_program(g, core, T, topo):
         ts(A("UU", 32, 64), A("TM"), 2, Op.arith_shift_right, 15, Op.bitwise_and)
         cp(A("UF"), A("UU"))
         for x in range(16):
-            mm(A("P6", 32 * x, 32 * x + 32), A("I16"), A("UF", 0, 32), more=x < 15)
+            mm(A("P5", 32 * x, 32 * x + 32), A("I16"), A("UF", 0, 32), more=x < 15)
         mm(A("P7"), A("INB"), A("YC"), True, False)
         for y in range(16):
             mm(A("P7", 32 * y, 32 * y + 32), A("I16"), A("UF", 32, 64), False, y == 15)
-        tt(A("AH", 512, 1024), A("P6"), A("XC"), Op.is_equal)
-        ts(A("BL"), A("P7"), 0.0, Op.is_equal, A("JW", 0, 1), Op.mult)
+        tt(A("AH", 512, 1024), A("P5"), A("XC"), Op.is_equal)
+        act(A("B0"), A("P7"), Act.Abs)
+        act(A("BL"), A("B0"), Act.Relu, bias=A("JW", 0, 1), scale=A("JW", 1, 2))
+
+    def logs():
         for j in range(2):
             for c in range(4):
                 for x in range(8):
@@ -589,33 +605,31 @@ def rank_program(g, core, T, topo):
                     reg = ("P4", 512, 640, 1) if (j, c, x) == (1, 0, 0) else ("P4", 512 + 128 * j + a + col, 513 + 128 * j + a + col, 1)
                     mm((PART("P4", a, a + 32, 1, col, 128 - 7 + col, 8)[0], [reg]),
                        PART("AH", 64 * j, 64 * j + 64, 1, w0, w0 + 1024 - 31, 32), PART("BL", 64 * j, 64 * j + 64, 1, 8 * c + x, 512, 32),
-                       not x & 1, bool(x & 1), 32 * j + 8 * c + x < 63)
+                       not x & 1, bool(x & 1), 8 * c + x < 31)
         act(A("LT"), A("P4", 0, 128), Act.Ln, bias=2.0 ** -64)
-        act(A("PEN"), A("LT"), Act.Relu, bias=A("BC", 0, 1), scale=-2000.0)
+        act(A("PEN"), A("LT"), Act.Relu, bias=A("BC", 2, 3), scale=-2000.0)
 
     def leave():
         ts(A("GO"), A("P1", 0, 256), 0.0, Op.is_gt)
-        tt(A("P1", 256, 512), A("O2"), A("P1", 0, 256), Op.max)
+        exchanged(whole(A("P0", 256, 512)), [(A("I24"), A("GO"))])
         scan(A("CN"), A("R01"), A("GO"), 0.0, Op.mult, Op.add)
         ts(A("BT"), A("CN"), float(2 ** 23 + 2 ** 19 + 2 ** 15 + 2 ** 11), Op.mult)
         ts(A("BT2"), A("BT"), 2 ** 23 + 2 ** 20 + 2 ** 17 + 2 ** 14, Op.bitwise_and)
-        tt(A("Y", 0, 256), A("BT2"), A("P1", 256, 512), Op.add)
+        tt(A("Y", 0, 256), A("BT2"), A("P0", 256, 512), Op.add)
 
     def new_places():
         mms(A("P2", 384, 512), [(A("IB"), A("CN", 0, 128)), (A("INB"), A("CN", 128, 256)), (A("IN8K"), A("GO", 0, 128)), (A("I8K"), A("GO", 128, 256))], more=True)
-        mm(A("P0", 0, 256), A("IB"), A("CHI"), True, False)
-        mm(A("P0", 0, 128), A("IM128"), A("SW"), False, False)
-        mm(A("P0", 128, 256), A("I128"), A("SW"), False, True)
+        mms(A("P5", 256, 512), [(A("IB"), A("CLO")), (A("INB"), A("CN")), (A("I8K"), A("GO"))])
         tt(A("T2"), A("P2", 384, 512), A("SW"), Op.mult)
-        mms(A("P0", 256, 512), [(A("IB"), A("CLO")), (A("INB"), A("CN")), (A("I8K"), A("GO"))], True, False)
-        mm(A("P0", 256, 384), A("IF"), A("T2"), False, False)
-        mm(A("P0", 384, 512), A("INF"), A("T2"), False, True)
-        act(A("EHL"), A("P0", 0, 512))
+        tt(A("EHL", 256, 384), A("P5", 256, 384), A("T2"), Op.add)
+        tt(A("EHL", 384, 512), A("P5", 384, 512), A("T2"), Op.subtract)
         to_window(2, A("EHL", 0, 256), A("EHL", 256, 512))
 
     def close_up(j):
-        act(A("P3", 0, 272), A("Y"), Act.Abs, bias=A("BC", 1 + j, 2 + j))
-        tt(A("Y", 0, 256), A("Y", 0, 256), A("P3", 1 << j, 256 + (1 << j)), Op.min)
+        act(A("P1", 0, 272), A("Y"), Act.Abs, bias=-2.0 ** (23 - 3 * j))
+        if j == 3:
+            tt(A("XK"), A("Y", 0, 256), A("XK"), Op.min)
+        tt(A("O") if j == 3 else A("Y", 0, 256), A("XK") if j == 3 else A("Y", 0, 256), A("P1", 1 << j, 256 + (1 << j)), Op.min)
 
     def winners():
         left = A("CN", 15, 256, 16)
@@ -631,30 +645,27 @@ def rank_program(g, core, T, topo):
         tt(A("ZW"), A("Z1"), A("CV"), Op.add)
         tt(A("XK"), IND(A("ZW"), A("LC", 0, 16)), A("K1K"), Op.subtract)
 
-    def append():
-        tt(A("O"), A("Y", 0, 256), A("XK"), Op.min)
-
     def new_entries():
-        ts(A("LEN"), A("CN", 15, 256, 16), -1.0, Op.mult, 16.0, Op.add)
         cp(A("SU"), A("SUI"))
+        ts(A("LEN"), A("CN", 15, 256, 16), -1.0, Op.mult, 16.0, Op.add)
         tt(A("AT"), IND(A("LEN"), A("LC", 0, 16)), A("CAT"), Op.min)
         scatter(A("PT"), A("SU"), A("AT"))
-        mms(A("P7"), [(A("I8K"), A("CMP", 16, 528)), (A("IN8K"), A("CMP", 15, 527))], True, False)
-        mms(A("P7", 0, 512, 16), [(A("I8K"), A("CMP", 15, 527, 16)), (A("IN8K"), A("ONEB"))], False, False)
+        mms(whole(A("P7")), [(A("I8K"), A("CMP", 16, 528)), (A("IN8K"), A("CMP", 15, 527))], True, False)
+        mms(whole(A("P7", 0, 512, 16)), [(A("I8K"), A("CMP", 15, 527, 16)), (A("IN8K"), A("ONEB"))], False, False, cut=True)
         for c in range(4):
-            mm(A("P7", 128 * c, 128 * c + 128), A("PT", 128 * c, 128 * c + 128), A("BO"), False, c == 3)
+            mm(whole(A("P7", 128 * c, 128 * c + 128)), A("PT", 128 * c, 128 * c + 128), A("BO"), False, c == 3)
         act(A("XS"), A("P7"), bias=8192.0 + 2048.0)
 
     def new_slots(out, lo, hi):
         tt(A("NL", lo, hi), A("P6", lo, hi), A("XS", lo, hi), Op.min)
         for c in range(lo, hi, 128):
-            mm(A("P5", c, c + 128), A("NL", c, c + 128), A("I16"), more=c + 128 < hi)
-        ts(A(out, lo, hi), A("P5", lo, hi), 2048.0, Op.add, 4096.0, Op.min)
+            mm(A("P7", c, c + 128), A("NL", c, c + 128), A("I16"), more=c + 128 < hi)
+        ts(A(out, lo, hi), A("P7", lo, hi), 2048.0, Op.add, 4096.0, Op.min)
 
     constants()
     for t in range(3):
         lists(t)
-        for c in (0, 2, 1, 3):
+        for c in range(4):
             wants(c)
             minima(c, SHARED[t])
         decide()
@@ -662,8 +673,7 @@ def rank_program(g, core, T, topo):
         if t:
             new_slots("WL", 0, 512)
         for c in range(4):
-            by_slot("GS", 2 * c, True)
-            by_slot("GS", 2 * c + 1, True)
+            by_slot("GS", c, "sv")
             read("P4", "GS", "RS", c)
             read("P5", "GS", "RS%d" % t, c)
         roll(t)
@@ -673,16 +683,15 @@ def rank_program(g, core, T, topo):
         applicants()
         leave()
         new_places()
+        logs()
         winners()
         for j in range(4):
             close_up(j)
-        append()
         new_entries()
         if t < 2:
             iota(A("PT", 0, 512), [[0, 512]], 0)
         for c in range(4):
-            by_slot("GE", 2 * c, t == 2)
-            by_slot("GE", 2 * c + 1, t == 2)
+            by_slot("GE", c, "ss" if t < 2 else "sv")
             read("P6", "GE", "RE", c)
 
     ts(A("YA"), A("O"), 255.5, Op.is_lt, 512.0, Op.mult)
@@ -692,7 +701,7 @@ def rank_program(g, core, T, topo):
             [(A("OUT%d%d" % (h, b)), A(n, 128 * b, 128 * b + 128)) for n in ("YA", "YB") for b in range(2)], more=h < 1)
     turn(A("YP"), A("P2", 0, 256))
     for y in range(8):
-        copy("v", A("YO", y, 256, 8), A("YP", 32 * y, 32 * y + 32))
+        (act if y % 3 == 2 else cp)(A("YO", y, 256, 8), A("YP", 32 * y, 32 * y + 32))
     dmas("y", [(ext(T.yoc[:]), A("YO"))])
     for lo in (0, 256):
         new_slots("YQ", lo, lo + 256)

@@ -19,37 +19,39 @@ def _decl(dtype, spec):
     SCRATCH[pool] = ("sbuf", [128, at], dtype)
 
 
-_decl(BF, "XT:4096 WT:528 MT:528 WG:4096 D0:4096 D1:4096 MG:4096 WD:4112 GS:8192 GE:8192 TT:512 PT:768 AH:1536 CMP:528 "
-          "EZ4:432 IB:128 INB:128 I8K:128 IN8K:128 I24:128 IN24:128 IPEN:128 I128:128 IM128:128 BO:128 "
-          "RS:8 RS0:8 RS1:8 RS2:8 RE:8 RW:8 CADD:64 R01:256 BIG:16 ONEB:32 CAT:256 CHI:256 CLO:256 "
-          "FHI:256 FLO:256 EHL:512 EM:256 SW:128 GO:256 CN:256 AT:256 BL:512 B0:512 YC:512")
-_decl(FH, "UF:64 I16:128 IN16:128 I37:128 L32:128 KT:768 OP:256 ZS:128 NL:512 YA:256 YB:256 "
+_decl(BF, "XT:4096 WT:528 WG:4096 D0:4096 D1:4096 PT:768 AH:1536 CMP:528 EZ:432 BO:128 RS:8 RS0:8 RS1:8 RS2:8 RW:8 CADD:64 "
+          "R01:256 BIG:16 CAT:256 EM:256 SW:128 GO:256 CN:256 AT:256 BL:512 B0:512 YC:512 NE:32")
+_decl(FH, "GS:8192 GE:8192 MG:4096 TT:512 UF:64 I16:128 IN16:128 I37:128 IN37:128 I8K:128 IN8K:128 I14:128 IPEN:128 IM2K:128 "
+          "IM1K:128 IP1K:128 L32:128 KT:768 OP:256 ZS:128 YA:256 YB:256 NPL:256 Q4:512 "
           "IN00:128 IN01:128 IN10:128 IN11:128 OUT00:128 OUT01:128 OUT10:128 OUT11:128")
-_decl(I4, "OCN:256 QW:512 THI:16 QI:8 KI:8 PI:32 H:512 HA:512 TM:32 UU:64 SUI:16 BT:256 BT2:256 WSI:32 WSJ:32")
-_decl(U2, "LC:32 OU:256 OU2:256 HU:512 SU:16 WL:512")
-_decl(F4, "IF:128 INF:128 I24F:128 IN24F:128 ZF:128 TB:128 TI:128 TJ:128 TK:128 ONE:256 TA:256 TC:16 TC2:16 TD:256 TE:256 TH:256 VV:256 VW:256 "
-          "KC:8 KB:8 KW:16 WR:8 LIM:8 JW:8 BC:8 G0:8 RMX:512 RMN:512 RK:128 JC:16 XC:512 K1K:256 CF:512 C1:256 YP:256 YO:256 YQ:512 "
-          "EE:256 FS:128 T2:128 SMX:512 PMN:512 MYK:32 KK:64 K:32 KD:32 L4P:32 W4:32 HOLD:32 AP:32 TU:32 "
-          "LT:128 PEN:128 K2:128 KM:128 PF:16 PM:16 PN:16 LZ:16 CV:16 Z1:16 ZW:16 LEN:16 XK:256 Y:272 XS:512 LAND0:128 LAND1:128 LAND2:128")
+_decl(I4, "OCN:256 QW:512 THI:16 QI:8 KI:8 H:512 HA:512 TM:32 UU:64 SUI:16 BT:256 BT2:256")
+_decl(U2, "LC:16 LC2:32 LX:32 LO:16 LY:16 OU:256 OU2:256 HU:512 SU:16 WL:512")
+_decl(F4, "WD:4112 WE:4112 MT:528 IF:128 INF:128 ZF:128 TB:128 TI:128 TJ:128 TK:128 TL:128 ONE:128 TA:256 TC:16 TC2:16 TD:256 TE:256 TH:256 VV:256 "
+          "KC:8 KW:16 WR:16 LIM:8 JW:8 BC:8 G0:8 RMX:512 RMN:512 RK:128 JC:16 XC:512 K1K:256 CF:512 C1:256 YP:256 YO:256 YQ:512 "
+          "E1:128 EE:256 F:256 FS:128 T2:128 EH:256 SMX:512 PMN:512 KK:64 K:32 KD:48 KQ:32 THP:32 W2:32 "
+          "LT:128 PEN:128 K2:128 KM:128 PF:16 PM:16 PN:16 CV:16 ZP:16 ZW:16 LEN:16 XK:256 Y:272 XS:512 NL:512 LAND0:128 LAND1:128 LAND2:128")
 SCRATCH["O"] = ("sbuf", [128, 16, 16], FH)
 SCRATCH["T1"] = ("sbuf", [128, 16, 16], F4)
-SCRATCH["NP8"] = ("sbuf", [128, 16, 16], F4)
 SCRATCH["O16"] = ("sbuf", [128, 8, 2, 16], FH)
 SCRATCH["OE"] = ("sbuf", [128, 8, 2, 16], FH)
 SCRATCH["P0"] = ("psum", [128, 32, 16], F4)
-SCRATCH["P2"] = ("psum", [128, 16, 2, 16], F4)
-for _n in ("P1", "P3", "P4", "P5", "P6", "P7"):
+SCRATCH["P6"] = ("psum", [128, 32, 16], F4)
+for _n in ("P1", "P2", "P3", "P4", "P5", "P7"):
     SCRATCH[_n] = ("psum", [128, 512], F4)
     WIDTH[_n] = 512
     WHERE[_n] = (_n, 0)
 SEMAPHORES = ["qv", "qs", "qt", "qg", "sent"] + ["arr%d" % t for t in range(3)] + ["d%d" % i for i in range(20)]
 
-CYCLE, PE_CYCLE, GATHER, GATHER2, SCATTER = 0.83, 0.44, 1.3, 1.3, 3.2
-CALL = {"v": 40.0, "s": 220.0, "g": 0.0}
-BANK, PE_OUT = 95.0, 400.0
-HOP, DMA, SEND, REMOTE = 130.0, 1500.0, 1500.0, 500.0
-AHEAD, SLACK, PATIENCE = 400.0, 100.0, 0.6
-SHARED = ((1, 2), (), ())
+CYCLE, PE_CYCLE, GATHER, GATHER2, SCATTER = 0.83, 0.42, 1.3, 1.3, 3.2
+CALL = {"v": 60.0, "s": 200.0, "g": 0.0}
+BANK, PE_OUT = 60.0, 250.0
+HOP, DMA, SEND, REMOTE = 100.0, 2200.0, 1000.0, 1200.0
+AHEAD, SLACK, PATIENCE = 400.0, 50.0, 0.3
+OWN, PASSES, GREEDY, SPANS = 60.0, 4, 2, []
+ORDER = (2, 3, 0, 1)
+SHARED = ((2, 3), (), ())
+MID = 2040.0
+MOVES = "WE"
 
 
 def _bank(name):
@@ -68,11 +70,7 @@ def rank_program(g, core, T, topo):
     hist = {}
 
     def A(n, lo=0, hi=None, st=1):
-        if n == "P0":
-            return (T.P0[:, lo // 16:hi // 16, :], [(n, lo, hi, 1)])
-        if n == "P2":
-            return (T.P2[:, lo // 32:hi // 32], [(n, lo, hi, 1)])
-        if n in ("O", "T1", "NP8"):
+        if n in ("P0", "P6", "O", "T1"):
             hi = 256 if hi is None else hi
             return (T[n][:, lo // 16:hi // 16, :], [(n, lo, hi, 1)])
         hi = WIDTH[n] if hi is None else hi
@@ -191,10 +189,11 @@ def rank_program(g, core, T, topo):
         run("v", lambda: g.vector.tensor_tensor(o[0], a[0], b[0], op), R(a, b), o[1], time, [("lineD", 0, 1, 1)] if n == 1024 else [])
 
     def ts(o, a, s1, op0, s2=None, op1=None):
+        time = GATHER * size(o) if picked(a) else cycles(size(o), o, a)
         if op1 is None:
-            run("v", lambda: g.vector.tensor_scalar(o[0], a[0], val(s1), None, op0), R(a, s1), o[1], cycles(size(o), o, a))
+            run("v", lambda: g.vector.tensor_scalar(o[0], a[0], val(s1), None, op0), R(a, s1), o[1], time)
         else:
-            run("v", lambda: g.vector.tensor_scalar(o[0], a[0], val(s1), val(s2), op0, op1), R(a, s1, s2), o[1], cycles(size(o), o, a))
+            run("v", lambda: g.vector.tensor_scalar(o[0], a[0], val(s1), val(s2), op0, op1), R(a, s1, s2), o[1], time)
 
     def cp(o, a):
         run("v", lambda: g.vector.tensor_copy(o[0], a[0]), a[1], o[1], cycles(size(o), o, a))
@@ -283,38 +282,65 @@ def rank_program(g, core, T, topo):
 
         def gap(p, k):
             same = steps[p]["queue"] == steps[k]["queue"]
-            return 0.0 if same and steps[p]["queue"] == "t" else steps[p]["later"] + (0.0 if same else HOP)
+            return 0.0 if same and steps[p]["queue"] == "t" else steps[p]["later"] + (OWN if same else HOP)
 
-        way = [0.0] * n
+        def place(order, back):
+            end, taken = {}, {q: [] for q in Q}
+            for k in order:
+                d = steps[k]["time"]
+                if back:
+                    t = max([end[x] + gap(k, x) for x in after[k]] + [steps[k]["later"]])
+                else:
+                    t = max([end[p] + gap(p, k) for p in steps[k]["before"]] + [0.0])
+                line = taken[steps[k]["queue"]]
+                i = 0
+                while i < len(line) and line[i][0] < t + d:
+                    t = max(t, line[i][1])
+                    i += 1
+                line.insert(i, (t, t + d))
+                end[k] = t + d
+            return end
+
+        def greedy(way):
+            way = [1.0e9 - k if k < loads else way[k] for k in range(n)]
+            end, free, left = {}, {q: 0.0 for q in Q}, [len(s["before"]) for s in steps]
+            ready = {k: 0.0 for k in range(n) if not left[k]}
+            while ready:
+                can = {k: max(t, free[steps[k]["queue"]]) for k, t in ready.items()}
+                q = steps[min(can, key=lambda k: (can[k] - (0.0 if steps[k]["queue"] == "v" else AHEAD), k))]["queue"]
+                mine = sorted([k for k in can if steps[k]["queue"] == q], key=lambda k: (-way[k], k))
+                first = min(can[k] for k in mine)
+                best = [k for k in mine if can[k] <= first + SLACK][0]
+                best = [k for k in mine if can[k] <= can[best] + PATIENCE * steps[best]["time"]][0]
+                k = ([k for k in mine if can[k] + steps[k]["time"] <= can[best]] + [best])[0]
+                end[k] = free[q] = can[k] + steps[k]["time"]
+                del ready[k]
+                for x in after[k]:
+                    left[x] -= 1
+                    if not left[x]:
+                        ready[x] = max(end[p] + gap(p, x) for p in steps[x]["before"])
+            return end
+
+        way = {}
         for k in range(n - 1, -1, -1):
             way[k] = steps[k]["time"] + max([way[x] + gap(k, x) for x in after[k]] + [steps[k]["later"]])
-        way[:loads] = [1.0e9 - k for k in range(loads)]
-        at, free, left = {}, {q: 0.0 for q in Q}, [len(s["before"]) for s in steps]
-        ready = {k: 0.0 for k in range(n) if not left[k]}
-        while ready:
-            can = {k: max(t, free[steps[k]["queue"]]) for k, t in ready.items()}
-            q = steps[min(can, key=lambda k: (can[k] - (0.0 if steps[k]["queue"] == "v" else AHEAD), k))]["queue"]
-            mine = sorted([k for k in can if steps[k]["queue"] == q], key=lambda k: (-way[k], k))
-            first = min(can[k] for k in mine)
-            best = [k for k in mine if can[k] <= first + SLACK][0]
-            best = [k for k in mine if can[k] <= can[best] + PATIENCE * steps[best]["time"]][0]
-            k = ([k for k in mine if can[k] + steps[k]["time"] <= can[best]] + [best])[0]
-            at[k] = can[k]
-            free[q] = at[k] + steps[k]["time"]
-            del ready[k]
-            for x in after[k]:
-                left[x] -= 1
-                if not left[x]:
-                    ready[x] = max(at[p] + steps[p]["time"] + gap(p, x) for p in steps[x]["before"])
-        for k in sorted(range(n), key=lambda x: (at[x], x)):
+        best = None
+        for turn_ in range(PASSES):
+            end = greedy(way) if turn_ < GREEDY else place(sorted(range(n), key=lambda k: (k >= loads, -way[k] if k >= loads else k, k)), False)
+            span = max(end[k] + steps[k]["later"] for k in range(n))
+            SPANS.append(span)
+            if best is None or span < best[0]:
+                best = (span, end)
+            way = place(sorted(range(n), key=lambda k: (-end[k], -k)), True)
+        for k in sorted(range(n), key=lambda x: (best[1][x] - steps[x]["time"], x)):
             steps[k]["issue"](steps[k]["queue"])
 
     def ext(ap):
         return (ap, [])
 
     def ez(n, k):
-        at = 144 * ("EZ4", "EZM", "EZP").index(n)
-        return A("EZ4", at + 15 - k, at + 143 - k)
+        at = 144 * ("EZ1", "EZM", "EZR").index(n)
+        return A("EZ", at + 15 - k, at + 143 - k)
 
     def rows(sel, n, lo, width):
         return [(ez(sel, r), A(n, lo + r, lo + width - 15 + r, 16)) for r in range(16)]
@@ -325,21 +351,22 @@ def rank_program(g, core, T, topo):
     dmas("y", [(A("QW"), ext(T.qs[:])), (A("THI", 0, 1), ext(T.th[:]))], 5000.0)
     loads = len(steps)
 
-    q1, kc, one = A("QI", 0, 1), A("KC", 0, 1), A("ONE", 0, 128)
+    q1, kc, one = A("QI", 0, 1), A("KC", 0, 1), A("ONE")
+    part = (1.5 - rank) / 8.0
+    move_row = 1
 
-    def to_window(row, hi, lo):
-        dmas("y", [(PART("WD", row + i, 128, 16, 0, 4096), x) for i, x in enumerate((hi, lo))])
+    def to_window(win, row, x):
+        dmas("y", [(PART(win, row, 128, 16, 0, 4096), x)])
 
     def constants():
         iota(q1, [[0, 1]], 0, 1, False)
         fill(A("ONE"), 1.0)
         fill(A("ZF"), 0.0)
-        iota(A("XC"), [[1, 16], [0, 32]], 512)
         ts(A("KI", 0, 1), q1, 15, Op.bitwise_and)
         cp(kc, A("KI", 0, 1))
-        for name, v in (("IF", 1.0), ("I24F", 2.0 ** 24), ("IN24F", -2.0 ** 24), ("IB", 1.0), ("INB", -1.0), ("I8K", 8192.0),
-                        ("IN8K", -8192.0), ("I24", 2.0 ** 24), ("IN24", -2.0 ** 24), ("IPEN", -65536.0), ("I128", 128.0), ("IM128", -128.0),
-                        ("I16", 1.0), ("IN16", -1.0), ("I37", 37.0)):
+        for name, v in (("IF", 1.0), ("INF", -1.0), ("I16", 1.0), ("IN16", -1.0), ("I37", 37.0), ("IN37", -37.0), ("I8K", 8192.0),
+                        ("IN8K", -8192.0), ("I14", 16384.0), ("IPEN", -32768.0), ("IM2K", -1.0 / 2048), ("IM1K", -1.0 / 1024),
+                        ("IP1K", 1.0 / 1024)):
             aff(A(name), A("ZF"), [[-1, 128]], Op.not_equal, v, 0, 1)
         for h in range(2):
             for b in range(2):
@@ -348,27 +375,34 @@ def rank_program(g, core, T, topo):
         aff(A("TB"), one, [[-16, 8], [0, 16]], Op.is_ge, 0.0, 0, 1)
         aff(A("BO"), A("TB"), [[16, 8], [0, 16]], Op.is_ge, 0.0, 15, -1)
         ones = A("BO", 0, 128, 16)
-        fill(A("EZ4", 0, 432), 0.0)
-        for i, v in enumerate((4.0, -4.0, 2.0 ** 24)):
-            ts(A("EZ4", 144 * i + 15, 144 * i + 143, 16), ones, v, Op.mult)
+
+        def row(o, a, r, v):
+            aff(o, a, [[-16, 8]], Op.not_equal, v, -r, 1)
+
+        fill(A("EZ"), 0.0)
+        for i, v in enumerate((1.0, -1.0)):
+            ts(A("EZ", 144 * i + 15, 144 * i + 143, 16), ones, v, Op.mult)
+        row(A("TI", 8, 16), A("ZF", 0, 8), move_row, 1.0)
+        cp(A("EZ", 288 + 15, 288 + 143, 16), A("TI", 8, 16))
         fill(PART("L32", 0, 64), 1.0 / 32)
         for t in range(3):
             fill(PART("KT", 0, 32, 1, 256 * t, 256 * t + 256), 77.0 * t - 1280.0)
         fill(PART("KT", 32, 64), -15.0 / 32)
-        iota(A("CADD"), [[0, 64]], 7 - rank)
+        iota(A("CADD"), [[0, 64]], -int(MID))
         iota(A("TA"), [[1, 256]], 0)
         iota(A("TC"), [[2, 16]], 17)
         ts(A("KW", 0, 1), kc, 16.0, Op.mult)
         ts(A("KW", 1, 2), kc, 32.0, Op.mult)
-        act(A("NP8"), A("TA"), Act.Identity, bias=A("KW", 1, 2), scale=0.125)
+        act(A("P6"), A("TA"), Act.Identity, bias=A("KW", 1, 2), scale=0.125)
         fill(A("C1"), -247.5)
         ts(A("C1", 0, 256, 16), A("TC"), 0.5, Op.mult, A("KW", 0, 1), Op.add)
-        tt(A("CF", 0, 256), A("C1"), A("NP8"), Op.mult)
-        for b in range(2):
-            act(A("CF", 256 + 128 * b, 384 + 128 * b), A("CF", 128 - 128 * b, 256 - 128 * b))
+        tt(A("CF", 0, 256), A("C1"), A("P6"), Op.mult)
+        act(A("CF", 256, 512), A("CF", 0, 256))
         fill(A("T1"), 0.0)
-        for y in range(8):
-            ts(A("OP", 32 * y, 32 * y + 32), A("OCN", y, 256, 8), 256.0, Op.add)
+        iota(A("TL", 0, 16), [[1, 8], [128, 2]], 0)
+        ts(A("KW", 2, 3), kc, 8.0, Op.mult)
+        ts(A("LO"), A("TL", 0, 16), A("KW", 2, 3), Op.add)
+        ts(A("OP"), IND(A("OCN"), A("LO")), 256.0, Op.add)
         turn(M(T.O16[:], "O16"), A("OP"))
         ts(M(T.OE[:], "OE"), M(T.O16[:], "O16"), 767.5, Op.is_ge, -768.0, Op.mult)
         for b in range(2):
@@ -377,47 +411,59 @@ def rank_program(g, core, T, topo):
         const(A("WT", 0, 16), 0.0)
         cp(A("WL"), A("QW"))
 
-        def row(o, a, r, v):
-            aff(o, a, [[-16, 8]], Op.not_equal, v, -r, 1)
-
         row(A("TI", 0, 8), A("ZF", 0, 8), 0, 1.0)
-        row(A("RS"), A("TI", 0, 8), 1, 1.0)
+        cp(A("RS"), A("TI", 0, 8))
         for t in range(3):
-            row(A("RS%d" % t), A("RS"), 5 + t, 1.0)
-        row(A("TI", 8, 16), A("ZF", 0, 8), 2, -1.0)
-        row(A("TI", 16, 24), A("TI", 8, 16), 3, 1.0)
-        row(A("RE"), A("TI", 16, 24), 4, 1.0)
-        ts(A("WR", 0, 1), kc, 4.0, Op.is_equal, 2048.0, Op.mult)
-        for lo in range(0, 4096, 1024):
-            act(A("WD", lo, lo + 1024), A("XT", lo, lo + 1024), Act.Identity, bias=A("WR", 0, 1), scale=0.0)
+            row(A("RS%d" % t), A("TI", 0, 8), 5 + t, 1.0)
+        fill(A("WD", 0, 512), 0.0)
+        for lo in (512, 1024, 2048):
+            act(A("WD", lo, 2 * lo), A("WD", 0, lo))
         iota(A("WR", 1, 4), [[1, 3]], 5)
-        ts(A("WR", 5, 8), A("WR", 1, 4), kc, Op.is_equal, -65536.0, Op.mult)
-        ts(A("WR", 4, 5), kc, 4.5, Op.is_gt, -65536.0, Op.mult)
+        ts(A("WR", 5, 8), A("WR", 1, 4), kc, Op.is_equal, -8192.0, Op.mult)
+        ts(A("WR", 4, 5), kc, 4.5, Op.is_gt, -8192.0, Op.mult)
+        ts(A("WR", 8, 9), kc, 0.5, Op.is_lt, -4096.0, Op.mult)
+        ts(A("WR", 9, 10), kc, float(move_row), Op.is_equal, 2048.0, Op.mult)
+        ts(A("WR", 10, 11), A("WR", 4, 5), A("WR", 8, 9), Op.add, A("WR", 9, 10), Op.add)
         for t in range(3):
-            ts(A("WD", 16 * t, 4096, 128), A("ZF", 0, 32), A("WR", 5 + t, 6 + t), Op.add, A("WR", 0, 1), Op.add)
-        ts(A("WD", 4096, 4112), A("ZF", 0, 16), A("WR", 4, 5), Op.add, A("WR", 0, 1), Op.add)
+            ts(A("WD", 16 * t, 4096, 128), A("ZF", 0, 32), A("WR", 5 + t, 6 + t), Op.add)
+        ts(A("WD", 4096, 4112), A("ZF", 0, 16), A("WR", 10, 11), Op.add)
+        if MOVES != "WD":
+            ts(A("WE", 4096, 4112), A("ZF", 0, 16), A("WR", 10, 11), Op.add)
+            for lo in range(0, 4096, 1024):
+                act(A("WE", lo, lo + 1024), A("XT", lo, lo + 1024))
         iota(A("RMN"), [[0, 512]], -1000000)
         const(A("RMN", 0, 512, 16), 1.0e6)
         act(A("RMX"), A("RMN"), scale=-1.0)
         act(A("R01"), A("RMX", 0, 256), Act.Relu, scale=1.0e-6)
         iota(A("YC"), [[1, 16], [0, 32]], 0)
+        act(A("XC"), A("YC"), bias=part, scale=1.0 / 128)
+        act(A("Q4"), A("YC"), bias=0.25, scale=0.0)
         iota(A("TD"), [[0, 16], [1, 16]], 0)
-        act(A("K1K"), A("TD"), scale=1024.0)
-        act(A("CLO"), A("TD"))
+        act(A("K1K"), A("TD"), bias=-16640.0, scale=1024.0)
         iota(A("VV"), [[16, 16], [256, 16]], -4096)
-        iota(A("VW"), [[-16, 16], [0, 16]], 4096)
         iota(A("TC2"), [[16, 16]], 512)
-        iota(A("PI"), [[1, 32]], 0, 0, False)
         iota(A("BIG"), [[0, 16]], 65536)
-        iota(A("ONEB"), [[0, 32]], 1)
         act(A("RW"), ones, scale=A("KW", 0, 1))
         for o in (A("AH", 0, 512), A("AH", 1024, 1536), A("PT", 0, 512), A("TT")):
             iota(o, [[0, 512]], 0)
-        iota(A("MT", 0, 16), [[0, 16]], 131072)
-        iota(A("CMP", 0, 16), [[0, 16]], 0)
+        iota(A("PT", 512, 768), [[0, 256]], 0)
+        iota(A("MT", 0, 16), [[0, 16]], 32768)
+        iota(A("CMP", 0, 16), [[0, 16]], 1)
+        iota(A("KD", 32, 48), [[0, 16]], -1000000)
         const(A("Y", 256, 272), 2.0 ** 25)
-        ts(A("KW", 6, 7), kc, -256.0, Op.mult)
-        act(A("CHI"), A("VW"), Act.Identity, bias=A("KW", 6, 7))
+        ts(A("KW", 6, 7), kc, 256.0, Op.mult, -2048.0, Op.add)
+        act(A("NPL"), A("TA"), Act.Identity, bias=A("KW", 6, 7))
+        iota(A("TL", 16, 48), [[1, 32]], 0)
+        cp(A("LC"), A("TL", 16, 32))
+        ts(A("KW", 3, 4), kc, 14.5, Op.is_lt)
+        ts(A("KW", 4, 5), kc, 14.5, Op.is_gt, 32.0, Op.mult)
+        ts(A("LC2"), A("TL", 16, 48), A("KW", 3, 4), Op.mult, A("KW", 4, 5), Op.add)
+        ts(A("KW", 5, 6), A("KW", 3, 4), 8192.0, Op.mult, 2048.0, Op.add)
+        iota(A("TL", 48, 80), [[0, 16], [16, 2]], 0)
+        ts(A("LX"), A("TL", 48, 80), kc, Op.add)
+        ts(A("KW", 9, 10), kc, 7.5, Op.is_gt, -255.0, Op.mult)
+        iota(A("TL", 80, 96), [[2, 16]], 0)
+        ts(A("LY"), A("TL", 80, 96), A("KW", 1, 2), Op.add, A("KW", 9, 10), Op.add)
         ts(A("KW", 7, 8), kc, 0.5, Op.is_lt, 16.0, Op.mult)
         ts(A("KW", 8, 9), kc, -1.0, Op.add, A("KW", 7, 8), Op.add)
         ts(A("TH"), A("TD"), kc, Op.is_equal, 64.0, Op.mult)
@@ -425,7 +471,6 @@ def rank_program(g, core, T, topo):
         tt(A("TE"), A("TE"), A("VV"), Op.mult)
         mms(A("P7", 0, 256), [(A("IF"), A("TE")), (A("IF"), A("TH"))])
         act(A("CAT"), A("P7", 0, 256))
-        cp(A("LC"), A("PI"))
         const(A("BC", 0, 1), 2.0 ** -63.2)
         act(A("BC", 1, 2), A("BC", 0, 1), Act.Ln)
         act(A("BC", 2, 3), A("BC", 1, 2), scale=2000.0)
@@ -439,15 +484,14 @@ def rank_program(g, core, T, topo):
         const(A("RK"), -128.0 * 2 * LN2)
         const(A("RK", 4, 128, 8), 320.0 * 2 * LN2)
         const(A("RK", 0, 128, 8), 1.0e6)
-        ts(A("LIM", 0, 1), A("THI", 0, 1), 4.0, Op.mult, float(rank), Op.add)
+        cp(A("LIM", 0, 1), A("THI", 0, 1))
+        ts(A("LIM", 1, 2), A("THI", 0, 1), 0.5, Op.add)
         act(A("G0"), A("TI", 0, 8), scale=A("LIM", 0, 1))
         for c in range(4):
-            mm(A("P6", 8 * c, 8 * c + 8), one, A("G0"), more=True)
-            mm(A("P6", 32 + 8 * c, 40 + 8 * c), A("WT", 16 + 128 * c, 144 + 128 * c), A("RW"), more=c < 3)
-        act(A("L4P"), A("P6", 0, 32))
-        ts(A("WSI"), A("P6", 32, 64), 255.0, Op.add)
-        ts(A("WSJ"), A("WSI"), 255, Op.bitwise_and)
-        ts(A("W4"), A("WSJ"), 4.0, Op.mult, 32768.0, Op.add)
+            mm(A("P7", 256 + 8 * c, 264 + 8 * c), one, A("G0"), more=True)
+            mm(A("P7", 288 + 8 * c, 296 + 8 * c), A("WT", 16 + 128 * c, 144 + 128 * c), A("RW"), more=c < 3)
+        act(A("THP"), A("P7", 256, 288))
+        act(A("W2"), A("P7", 288, 320), bias=MID + 8192.0)
 
     def lists(t):
         o = A("O")
@@ -455,79 +499,76 @@ def rank_program(g, core, T, topo):
         mm(whole(A("P0", 0, 512)), A("IF"), A("CF"), True, False)
         for b in range(2):
             mm(whole(A("P0", 256 * b, 256 * b + 256)), PART("L32", 0, 64), PART("KT", 0, 64, 1, 256 * t, 256 * t + 256), False, False, cut=b == 1)
+        mm(whole(A("P0", 0, 256)), A("I37"), o, False, False)
         for b in range(2):
-            mm(whole(A("P0", 256 * b, 256 * b + 256)), A("I37"), o, False, b == 1)
-        tt((T.T1[:, :, 1:16], [("T1", 0, 256, 1)]), (T.NP8[:, :, 1:16], [("NP8", 0, 256, 1)]), (T.O[:, :, 0:15], o[1]), Op.mult)
-        tt(A("H", 0, 256), A("T1"), A("P0", 0, 256), Op.add)
-        ts(A("HA", 0, 256), A("H", 0, 256), 4095, Op.bitwise_and)
-        cp(A("HU", 0, 256), A("HA", 0, 256))
+            mm(whole(A("P0", 256 + 128 * b, 384 + 128 * b)), A("I37"), A("O", 128 - 128 * b, 256 - 128 * b), False, b == 1)
+        tt((T.T1[:, :, 1:16], [("T1", 0, 256, 1)]), (T.O[:, :, 0:15], o[1]), (T.P6[:, 0:16, 1:16], [("P6", 0, 256, 1)]), Op.mult)
         for b in range(2):
-            tt(A("H", 256 + 128 * b, 384 + 128 * b), A("T1", 128 - 128 * b, 256 - 128 * b), A("P0", 256 + 128 * b, 384 + 128 * b), Op.add)
-        ts(A("HA", 256, 512), A("H", 256, 512), 4095, Op.bitwise_and)
-        cp(A("HU", 256, 512), A("HA", 256, 512))
+            tt(A("H", 256 * b, 256 * b + 256), A("T1"), A("P0", 256 * b, 256 * b + 256), Op.add)
+        ts(A("HA"), A("H"), 4095, Op.bitwise_and)
+        cp(A("HU"), A("HA"))
         ts(A("EM"), o, 255.5, Op.is_lt)
 
     def wants(c):
         gather(A("WG", 1024 * c, 1024 * c + 1024), A("WT"), A("OU", 64 * c, 64 * c + 64), "s")
 
     def minima(c, shared):
-        w, lo = A("WG", 1024 * c, 1024 * c + 1024), 1024 * c
-        d = whole(A("P2", 64 * c, 64 * c + 64))
-        if c == 0:
-            mm(whole(A("P2", 0, 256)), A("IPEN"), A("EM"), True, False, cut=True)
+        w, lo, bank = A("WG", 1024 * c, 1024 * c + 1024), 1024 * c, "P3" if c & 2 else "P2"
+        mate = A("HU", 256 + 64 * (c ^ 2), 320 + 64 * (c ^ 2))
+
+        def d(x):
+            return whole(A(bank, 64 * (x & 1), 64 * (x & 1) + 64))
+        if not c & 1:
+            mm(whole(A(bank, 0, 128)), A("IPEN"), A("EM", 64 * c, 64 * c + 128), True, False, cut=True)
         tt(A("D0", lo, lo + 1024), IND(A("XT"), A("HU", 64 * c, 64 * c + 64)), w, Op.min)
-        mms(A("P1", 64 * c, 64 * c + 64), [(A("IB"), A("CADD"))] + rows("EZ4", "D0", lo, 1024), more=True)
-        mms(d, rows("EZM", "D0", lo, 1024), False, False, cut=True)
+        mms(A("P1", 64 * c, 64 * c + 64), [(A("I16"), A("CADD"))] + rows("EZ1", "D0", lo, 1024), more=True)
+        mms(d(c), rows("EZM", "D0", lo, 1024), False, False, cut=True)
         if c in shared:
-            gather(A("D1", lo, lo + 1024), A("XT"), A("HU", 256 + 64 * c, 320 + 64 * c), "s")
-            mms(d, rows("EZ4", "WG", lo, 1024), False, False, cut=True)
-            for b, bank in enumerate(("P4", "P5")):
-                part = (lo + 512 * b, lo + 512 * b + 512)
-                mms(A(bank), [(A("IB"), A("WG", *part)), (A("INB"), A("D1", *part))])
-                act(A("D1", *part), A(bank), Act.Relu)
+            gather(A("D1", lo, lo + 1024), A("XT"), mate, "s")
+            mms(d(c), rows("EZ1", "WG", lo, 1024), False, False, cut=True)
+            for b, stage in enumerate(("P4", "P5")):
+                piece = (lo + 512 * b, lo + 512 * b + 512)
+                mms(A(stage), [(A("I16"), A("WG", *piece)), (A("IN16"), A("D1", *piece))])
+                act(A("D1", *piece), A(stage), Act.Relu)
         else:
-            tt(A("D1", lo, lo + 1024), IND(A("XT"), A("HU", 256 + 64 * c, 320 + 64 * c)), w, Op.min)
-            for x in shared if c == 3 else ():
-                mms(whole(A("P2", 64 * x, 64 * x + 64)), rows("EZM", "D1", 1024 * x, 1024), False, False, cut=True)
-            mms(d, rows("EZ4", "D1", lo, 1024), False, c == 3, cut=True)
+            tt(A("D1", lo, lo + 1024), IND(A("XT"), mate), w, Op.min)
+        if c & 1:
+            late = [x for x in (c - 1, c) if x in shared] + [x for x in (c,) if x not in shared]
+            for x in late:
+                mms(d(x), rows("EZM" if x in shared else "EZ1", "D1", 1024 * x, 1024), False, x == late[-1], cut=True)
+        elif c not in shared:
+            mms(d(c), rows("EZ1", "D1", lo, 1024), False, False, cut=True)
+        if c == 3:
+            act(A("E1"), A("P3", 0, 128), scale=-1.0)
 
     def decide():
-        f = A("P1", 256, 512)
-        ts(A("EE", 0, 128), A("P2", 128, 256), -1.0, Op.mult)
-        tt(A("SW"), A("P2", 0, 128), A("EE", 0, 128), Op.is_gt)
-        for b in range(2):
-            tt(A("EE", 128 * b, 128 * b + 128), A("P2", 128 * b, 128 * b + 128), A("SW"), Op.mult)
-        tt(f, A("EE"), A("P1", 0, 256), Op.add)
-        cp(A("FHI"), f)
-        tt(A("FLO"), f, A("FHI"), Op.subtract)
-        to_window(0, A("FHI"), A("FLO"))
+        tt(A("SW"), A("P2", 0, 128), A("E1"), Op.is_gt)
+        tt(A("EE", 0, 128), A("P2", 0, 128), A("SW"), Op.mult)
+        tt(A("EE", 128, 256), A("P3", 0, 128), A("SW"), Op.mult)
+        tt(A("F"), A("EE"), A("P1", 0, 256), Op.add)
+        to_window("WD", 0, A("F"))
 
-    def exchanged(o, more):
-        mm(o, A("I16"), A("O"), True, False)
-        mm(A("P0", 256, 384), A("IN16"), A("ZS"), False, False)
-        mm(A("P0", 384, 512), A("I16"), A("ZS"), False, not more)
+    def exchanged(more):
+        mm(whole(A("P0", 256, 512)), A("I16"), A("O"), True, False)
+        mm(whole(A("P0", 256, 384)), A("IN16"), A("ZS"), False, False)
+        mm(whole(A("P0", 384, 512)), A("I16"), A("ZS"), False, not more, cut=True)
         if more:
-            mms(o, more, False, True)
+            mms(whole(A("P0", 256, 512)), more, False, True)
 
     def exchange():
         mms(A("P0", 0, 128), [(A("I16"), A("O", 0, 128)), (A("IN16"), A("O", 128, 256))], more=True)
-        mms(A("P2", 256, 384), [(A(l), A(n, lo, lo + 128)) for l, lo in (("IB", 0), ("INB", 128)) for n in ("FHI", "FLO")])
+        mms(A("P0", 128, 256), [(A("IF"), A("F", 0, 128)), (A("INF"), A("F", 128, 256))])
         tt(A("ZS"), A("P0", 0, 128), A("SW"), Op.mult)
-        tt(A("FS"), A("P2", 256, 384), A("SW"), Op.mult)
-        exchanged(A("P0", 256, 512), [])
+        tt(A("FS"), A("P0", 128, 256), A("SW"), Op.mult)
+        exchanged([])
         ts(A("OU2"), A("P0", 256, 512), -240.0, Op.add)
-        mm(A("P3", 0, 256), A("IB"), A("CHI"), True, False)
-        mm(A("P3", 0, 128), A("IM128"), A("SW"), False, False)
-        mm(A("P3", 128, 256), A("I128"), A("SW"), False, True)
-        act(A("EHL", 0, 256), A("P3", 0, 256))
 
-    def by_slot(n, c, queues):
-        for m in (2 * c, 2 * c + 1):
-            gather(A(n, 1024 * m, 1024 * m + 1024), A("WD"), A("WL", 64 * m, 64 * m + 64), queues[m & 1])
+    def by_slot(n, win, m, q):
+        gather(A(n, 1024 * m, 1024 * m + 1024), A(win), A("WL", 64 * m, 64 * m + 64), q)
 
-    def read(bank, n, sel, c):
+    def read(bank, at, sel, c):
         for s in range(16):
-            mm(A(bank, 128 * c + s, 128 * c + 128 - 15 + s, 16), A(n, 2048 * c + s, 2048 * c + 2048 - 15 + s, 16), A(sel), more=s < 15)
+            mm(A(bank, at + s, at + 128 - 15 + s, 16), A("GS", 2048 * c + s, 2048 * c + 2048 - 15 + s, 16), A(sel), more=s < 15)
 
     used, plan = [], []
     for d in sorted([d for d in T.cores if d != core], key=lambda d: len(topo.engines(core, d))):
@@ -535,11 +576,14 @@ def rank_program(g, core, T, topo):
         used += es
         plan.append((d, sum(1 << e for e in es), len(es)))
 
+    best = A("SMX", 15, 512, 16)
+
     def roll(t):
         land = "LAND%d" % t
         own = A(land, 32 * rank, 32 * rank + 32)
-        scan(A("SMX"), A("RMX"), A("P4"), 0.0, Op.min, Op.max)
-        cp(own, A("SMX", 15, 512, 16))
+        scan(A("SMX", 0, 384), A("RMX", 0, 384), A("P1", 0, 384), 0.0, Op.min, Op.max)
+        scan(A("SMX", 384, 512), A("RMX", 0, 128), A("P2", 0, 128), 0.0, Op.min, Op.max)
+        ts(own, best, part, Op.add, -3000.0, Op.max)
         others = [(land, 32 * r, 32 * r + 32, 1) for r in range(4) if r != rank]
 
         def go(on):
@@ -555,75 +599,74 @@ def rank_program(g, core, T, topo):
             snap[tok] = {tok[0]: tok[1]}
             note(hist, "net", [], others, tok)
         step("g", SEND, own[1], others, go, REMOTE)
-        scan(A("PMN"), A("RMN"), A("P5"), 0.0, Op.max, Op.min)
-        ts(A("MYK"), own, 0.5, Op.max)
+
+    def as_holder():
+        scan(A("PMN"), A("RMN"), A("P3"), 0.0, Op.max, Op.min)
+        tt(A("TM"), best, A("W2"), Op.add)
+        ts(A("UU", 0, 32), A("TM"), 0xF0, Op.bitwise_and)
+        ts(A("UU", 32, 64), A("TM"), 15, Op.bitwise_and)
+        cp(A("UF"), A("UU"))
+        tt(A("KD", 0, 32), best, A("THP"), Op.subtract)
+        tt(A("NE"), A("PMN", 15, 512, 16), A("KD", 0, 32), Op.is_ge)
+        mms(A("P2", 384, 416), [(A("IF"), best), (A("IM2K"), A("UF", 0, 32)), (A("I8K"), A("NE"))])
+        mm(A("P7"), A("IN16"), A("YC"), True, False)
+        for y in range(16):
+            mm(A("P7", 32 * y, 32 * y + 32), A("I16"), A("UF", 32, 64), False, y == 15)
+        act(A("B0"), A("P7"), Act.Abs)
+        act(A("BL"), A("B0"), Act.Relu, bias=A("JW", 0, 1), scale=A("JW", 1, 2))
+        tt(A("CMP", 16, 528), IND(A("KD"), A("LC2")), A("PMN"), Op.is_le)
 
     def thresholds(t):
         land = "LAND%d" % t
         tt(A("KK"), A(land, 0, 64), A(land, 64, 128), Op.max)
-        tt(A("K"), A("KK", 0, 32), A("KK", 32, 64), Op.max)
-        tt(A("KD"), A("K"), A("L4P"), Op.subtract)
-        cp(A("TT", 0, 512, 16), A("KD"))
-        tt(A("TT", 1, 512, 16), A("KD"), A("TT", 0, 512, 16), Op.subtract)
+        tt(A("TT", 0, 512, 16), A("KK", 0, 32), A("KK", 32, 64), Op.max)
         for c in range(4):
-            mm(A("P3", 128 * c, 128 * c + 128), A("TT", 128 * c, 128 * c + 128), A("IB"), more=c < 3)
-        act(A("MT", 16, 528), A("P3"))
+            mm(A("P1", 128 * c, 128 * c + 128), A("TT", 128 * c, 128 * c + 128), A("I16"), more=c < 3)
+        act(A("MT", 16, 528), A("P1"))
+        tt(A("K"), A("KK", 0, 32), A("KK", 32, 64), Op.max)
+        tt(A("KQ"), A("K"), A("P2", 384, 416), Op.subtract)
+        tt(A("AH", 512, 1024), IND(A("KQ"), A("LX")), A("XC"), Op.is_equal)
 
     def limits(t, c):
         w = (64 * c, 64 * c + 64)
         gather(A("MG", 1024 * c, 1024 * c + 1024), A("MT"), A("OU2", *w), "sv"[c & 1])
         if c == 0:
-            mms(whole(A("P1", 0, 256)), [(A("IN24"), A("FHI")), (A("IN24"), A("FLO"))], True, False)
-            for b, l in enumerate(("I24F", "IN24F")):
-                mm(whole(A("P1", 128 * b, 128 * b + 128)), A(l), A("FS"), False, False)
-            mm(whole(A("P1", 16 * t, 256, 128)), A("I24"), A("BIG", 0, 2), False, False, cut=True)
-        mms(whole(A("P1", *w)), rows("EZP", "MG", 1024 * c, 1024), False, c == 3, cut=c < 3)
-
-    def applicants():
-        tt(A("HOLD"), A("K"), A("MYK"), Op.is_equal)
-        tt(A("TU"), A("K"), A("W4"), Op.add)
-        tt(A("CMP", 16, 528), IND(A("KD"), A("LC")), A("PMN"), Op.is_le)
-        tt(A("AP"), A("HOLD"), A("CMP", 31, 528, 16), Op.is_gt)
-        tt(A("TM"), A("TU"), A("AP"), Op.mult)
-        ts(A("UU", 0, 32), A("TM"), 6, Op.arith_shift_right, 0x20F, Op.bitwise_and)
-        ts(A("UU", 32, 64), A("TM"), 2, Op.arith_shift_right, 15, Op.bitwise_and)
-        cp(A("UF"), A("UU"))
-        for x in range(16):
-            mm(A("P5", 32 * x, 32 * x + 32), A("I16"), A("UF", 0, 32), more=x < 15)
-        mm(A("P7"), A("INB"), A("YC"), True, False)
-        for y in range(16):
-            mm(A("P7", 32 * y, 32 * y + 32), A("I16"), A("UF", 32, 64), False, y == 15)
-        tt(A("AH", 512, 1024), A("P5"), A("XC"), Op.is_equal)
-        act(A("B0"), A("P7"), Act.Abs)
-        act(A("BL"), A("B0"), Act.Relu, bias=A("JW", 0, 1), scale=A("JW", 1, 2))
+            mm(whole(A("P4", 0, 256)), A("INF"), A("F"), True, False)
+            for b, l in enumerate(("IF", "INF")):
+                mm(whole(A("P4", 128 * b, 128 * b + 128)), A(l), A("FS"), False, False)
+            mm(whole(A("P4", 16 * t, 256, 128)), A("I16"), A("BIG", 0, 2), False, False, cut=True)
+        mms(whole(A("P4", *w)), rows("EZ1", "MG", 1024 * c, 1024), False, c == 3, cut=c < 3)
 
     def logs():
         for j in range(2):
             for c in range(4):
                 for x in range(8):
                     w0, a, col = 512 - 512 * (x & 1) + 8 * c + x, 32 * (x >> 1), 4 * j + c
-                    reg = ("P4", 512, 640, 1) if (j, c, x) == (1, 0, 0) else ("P4", 512 + 128 * j + a + col, 513 + 128 * j + a + col, 1)
-                    mm((PART("P4", a, a + 32, 1, col, 128 - 7 + col, 8)[0], [reg]),
+                    reg = ("P3", 512, 640, 1) if (j, c, x) == (1, 0, 0) else ("P3", 512 + 128 * j + a + col, 513 + 128 * j + a + col, 1)
+                    mm((PART("P3", a, a + 32, 1, col, 128 - 7 + col, 8)[0], [reg]),
                        PART("AH", 64 * j, 64 * j + 64, 1, w0, w0 + 1024 - 31, 32), PART("BL", 64 * j, 64 * j + 64, 1, 8 * c + x, 512, 32),
                        not x & 1, bool(x & 1), 8 * c + x < 31)
-        act(A("LT"), A("P4", 0, 128), Act.Ln, bias=2.0 ** -64)
+        act(A("LT"), A("P3", 0, 128), Act.Ln, bias=2.0 ** -64)
         act(A("PEN"), A("LT"), Act.Relu, bias=A("BC", 2, 3), scale=-2000.0)
+        tt(A("K2"), A("PEN"), A("LT"), Op.subtract)
+        scan(A("KM"), A("RK"), A("K2"), 0.0, Op.add, Op.min)
 
     def leave():
-        ts(A("GO"), A("P1", 0, 256), 0.0, Op.is_gt)
-        exchanged(whole(A("P0", 256, 512)), [(A("I24"), A("GO"))])
+        ts(A("GO"), A("P4", 0, 256), A("LIM", 1, 2), Op.is_gt, 1024.0, Op.mult)
+        exchanged([(A("I14"), A("GO"))])
         scan(A("CN"), A("R01"), A("GO"), 0.0, Op.mult, Op.add)
-        ts(A("BT"), A("CN"), float(2 ** 23 + 2 ** 19 + 2 ** 15 + 2 ** 11), Op.mult)
+        ts(A("BT"), A("CN"), float(2 ** 13 + 2 ** 9 + 2 ** 5 + 2), Op.mult)
         ts(A("BT2"), A("BT"), 2 ** 23 + 2 ** 20 + 2 ** 17 + 2 ** 14, Op.bitwise_and)
         tt(A("Y", 0, 256), A("BT2"), A("P0", 256, 512), Op.add)
 
     def new_places():
-        mms(A("P2", 384, 512), [(A("IB"), A("CN", 0, 128)), (A("INB"), A("CN", 128, 256)), (A("IN8K"), A("GO", 0, 128)), (A("I8K"), A("GO", 128, 256))], more=True)
-        mms(A("P5", 256, 512), [(A("IB"), A("CLO")), (A("INB"), A("CN")), (A("I8K"), A("GO"))])
-        tt(A("T2"), A("P2", 384, 512), A("SW"), Op.mult)
-        tt(A("EHL", 256, 384), A("P5", 256, 384), A("T2"), Op.add)
-        tt(A("EHL", 384, 512), A("P5", 384, 512), A("T2"), Op.subtract)
-        to_window(2, A("EHL", 0, 256), A("EHL", 256, 512))
+        mms(A("P2", 256, 384), [(A(l), A(n, lo, lo + 128)) for n, two in (("NPL", ("I16", "IN16")), ("GO", ("I37", "IN37")), ("CN", ("IM1K", "IP1K")))
+                                for l, lo in zip(two, (0, 128))], more=True)
+        mms(A("P2", 0, 256), [(A("I16"), A("NPL")), (A("I37"), A("GO")), (A("IM1K"), A("CN"))])
+        tt(A("T2"), A("P2", 256, 384), A("SW"), Op.mult)
+        tt(A("EH", 0, 128), A("P2", 0, 128), A("T2"), Op.subtract)
+        tt(A("EH", 128, 256), A("P2", 128, 256), A("T2"), Op.add)
+        to_window(MOVES, move_row, A("EH"))
 
     def close_up(j):
         act(A("P1", 0, 272), A("Y"), Act.Abs, bias=-2.0 ** (23 - 3 * j))
@@ -633,79 +676,87 @@ def rank_program(g, core, T, topo):
 
     def winners():
         left = A("CN", 15, 256, 16)
-        tt(A("K2"), A("PEN"), A("LT"), Op.subtract)
         ts(A("PF"), left, 0.5, Op.is_lt, 1.0e4, Op.mult)
-        scan(A("KM"), A("RK"), A("K2"), 0.0, Op.add, Op.min)
-        ts(A("LZ"), left, -1024.0, Op.mult, 256.0 + 16384.0, Op.add)
         tt(A("PM"), A("KM", 7, 128, 8), A("PF"), Op.add)
         ts(A("PN"), A("PM"), 0.5 / LN2, Op.mult, 479.6, Op.add)
         tt(A("SUI"), A("PN"), A("JC"), Op.min)
         ts(A("CV"), A("SUI"), 511.5, Op.is_ge, -768.0, Op.mult)
-        tt(A("Z1"), A("SUI"), A("LZ"), Op.add)
-        tt(A("ZW"), A("Z1"), A("CV"), Op.add)
-        tt(A("XK"), IND(A("ZW"), A("LC", 0, 16)), A("K1K"), Op.subtract)
+        tt(A("ZP"), A("SUI"), left, Op.subtract)
+        tt(A("ZW"), A("ZP"), A("CV"), Op.add)
+        tt(A("XK"), IND(A("ZW"), A("LC")), A("K1K"), Op.subtract)
 
-    def new_entries():
+    def new_entries(last):
         cp(A("SU"), A("SUI"))
-        ts(A("LEN"), A("CN", 15, 256, 16), -1.0, Op.mult, 16.0, Op.add)
-        tt(A("AT"), IND(A("LEN"), A("LC", 0, 16)), A("CAT"), Op.min)
+        ts(A("LEN"), A("CN", 15, 256, 16), -1.0 / 1024, Op.mult, 16.0, Op.add)
+        tt(A("AT"), IND(A("LEN"), A("LC")), A("CAT"), Op.min)
         scatter(A("PT"), A("SU"), A("AT"))
-        mms(whole(A("P7")), [(A("I8K"), A("CMP", 16, 528)), (A("IN8K"), A("CMP", 15, 527))], True, False)
-        mms(whole(A("P7", 0, 512, 16)), [(A("I8K"), A("CMP", 15, 527, 16)), (A("IN8K"), A("ONEB"))], False, False, cut=True)
+        mm(whole(A("P7")), A("I8K"), A("Q4"), True, False)
         for c in range(4):
-            mm(whole(A("P7", 128 * c, 128 * c + 128)), A("PT", 128 * c, 128 * c + 128), A("BO"), False, c == 3)
-        act(A("XS"), A("P7"), bias=8192.0 + 2048.0)
+            o = whole(A("P7", 128 * c, 128 * c + 128))
+            mm(o, A("CMP", 16 + 128 * c, 144 + 128 * c), A("I8K"), False, False)
+            mm(o, A("CMP", 15 + 128 * c, 143 + 128 * c), A("IN8K"), False, False, cut=c == 3)
+        mm(whole(A("P7")), A("BO"), A("PT", 0, 512), False, True)
+        if last:
+            ts(A("XS"), A("P7"), A("KW", 5, 6), Op.add, 4096.0, Op.min)
+        else:
+            act(A("XS"), A("P7"), Act.Identity, bias=A("KW", 5, 6))
 
-    def new_slots(out, lo, hi):
-        tt(A("NL", lo, hi), A("P6", lo, hi), A("XS", lo, hi), Op.min)
-        for c in range(lo, hi, 128):
-            mm(A("P7", c, c + 128), A("NL", c, c + 128), A("I16"), more=c + 128 < hi)
-        ts(A(out, lo, hi), A("P7", lo, hi), 2048.0, Op.add, 4096.0, Op.min)
+    def move(m, q):
+        bank = "P5" if m & 4 else "P4"
+        by_slot("GE", MOVES, m, q)
+        if not m & 3:
+            mm(whole(A(bank, 0, 256)), A("I8K"), A("Q4", 0, 256), True, False, cut=True)
+        mms(whole(A(bank, 64 * (m & 3), 64 * (m & 3) + 64)), rows("EZR", "GE", 1024 * m, 1024), False, m & 3 == 3, cut=True)
+
+    def new_slots(out, h):
+        w = (256 * h, 256 * h + 256)
+        tt(A(out, *w), A("P5" if h else "P4", 0, 256), A("XS", *w), Op.min)
+        if out == "NL":
+            ts(A("WL", *w), A("NL", *w), 4096.0, Op.min)
 
     constants()
     for t in range(3):
         lists(t)
-        for c in range(4):
+        for c in ORDER:
             wants(c)
             minima(c, SHARED[t])
         decide()
         exchange()
-        if t:
-            new_slots("WL", 0, 512)
+        for h in range(2) if t else ():
+            new_slots("NL", h)
         for c in range(4):
-            by_slot("GS", c, "sv")
-            read("P4", "GS", "RS", c)
-            read("P5", "GS", "RS%d" % t, c)
+            for m in (2 * c, 2 * c + 1):
+                by_slot("GS", "WD", m, "sv"[m & 1])
+            read("P1" if c < 3 else "P2", 128 * (c % 3), "RS", c)
+            read("P3", 128 * c, "RS%d" % t, c)
         roll(t)
+        as_holder()
         thresholds(t)
         for c in range(4):
             limits(t, c)
-        applicants()
+        logs()
         leave()
         new_places()
-        logs()
         winners()
         for j in range(4):
             close_up(j)
-        new_entries()
+        new_entries(t == 2)
         if t < 2:
             iota(A("PT", 0, 512), [[0, 512]], 0)
-        for c in range(4):
-            by_slot("GE", c, "ss" if t < 2 else "sv")
-            read("P6", "GE", "RE", c)
+        for m in range(8):
+            move(m, "s" if t < 2 else "sv"[m & 1])
 
     ts(A("YA"), A("O"), 255.5, Op.is_lt, 512.0, Op.mult)
     ts(A("YB"), A("O"), -256.0, Op.add, 0.0, Op.max)
     for h in range(2):
-        mms((T.P2[:, 0:8, h, :], [("P2", 0, 256, 1)]),
+        mms((T.P0[:, h:16:2, :], [("P0", 0, 256, 1)]),
             [(A("OUT%d%d" % (h, b)), A(n, 128 * b, 128 * b + 128)) for n in ("YA", "YB") for b in range(2)], more=h < 1)
-    turn(A("YP"), A("P2", 0, 256))
-    for y in range(8):
-        (act if y % 3 == 2 else cp)(A("YO", y, 256, 8), A("YP", 32 * y, 32 * y + 32))
+    turn(A("YP"), A("P0", 0, 256))
+    gather(A("YO"), A("YP"), A("LY"), "s")
     dmas("y", [(ext(T.yoc[:]), A("YO"))])
-    for lo in (0, 256):
-        new_slots("YQ", lo, lo + 256)
-        dmas("y", [(ext(T.yq[:, lo:lo + 256]), A("YQ", lo, lo + 256))])
+    for h in range(2):
+        new_slots("YQ", h)
+        dmas("y", [(ext(T.yq[:, 256 * h:256 * h + 256]), A("YQ", 256 * h, 256 * h + 256))])
     issue_all()
     for s in sorted(cnt):
         if known["g"].get(s, 0) < cnt[s]:

@@ -19,39 +19,62 @@ def _decl(dtype, spec):
     SCRATCH[pool] = ("sbuf", [128, at], dtype)
 
 
-_decl(BF, "XT:4096 WT:528 WG:4096 D0:4096 D1:4096 PT:768 AH:1536 CMP:528 EZ:432 BO:128 RS:8 RS0:8 RS1:8 RS2:8 RW:8 CADD:64 "
-          "R01:256 BIG:16 CAT:256 EM:256 SW:128 GO:256 CN:256 AT:256 BL:512 B0:512 YC:512 NE:32")
-_decl(FH, "GS:8192 GE:8192 MG:4096 TT:512 UF:64 I16:128 IN16:128 I37:128 IN37:128 I8K:128 IN8K:128 I14:128 IPEN:128 IM2K:128 "
-          "IM1K:128 IP1K:128 L32:128 KT:768 OP:256 ZS:128 YA:256 YB:256 NPL:256 Q4:512 "
+_decl(BF, "XT:4096 WI:512 WT:528 WG:4096 D0:4096 D1:4096 PT:768 AH:1536 CMP:528 EZ:432 BO:128 RS:8 RS0:8 RS1:8 RS2:8 RW:8 CADD:64 "
+          "R01:256 BIG:16 CAT:256 EM:256 SW:128 GO:256 CN:256 AT:256 BL:512 YC:512 NE:32 TE:256 TH:256 VV:256 REP:128")
+_decl(FH, "GS:8192 GE:8192 MG:4096 TT:512 SMX:512 PMN:512 THB:512 K1K:256 Q16:256 SUI:16 I4K:128 IN4K:128 UF:64 I16:128 IN16:128 I37:128 I2K:128 I8K:128 IN8K:128 I14:128 IPEN:128 IM2K:128 "
+          "IM1K:128 IN37:128 IP1K:128 OP:256 ZS:128 YA:256 J16:128 NPL:512 Q1:256 XS:512 "
           "IN00:128 IN01:128 IN10:128 IN11:128 OUT00:128 OUT01:128 OUT10:128 OUT11:128")
-_decl(I4, "OCN:256 QW:512 THI:16 QI:8 KI:8 H:512 HA:512 TM:32 UU:64 SUI:16 BT:256 BT2:256")
-_decl(U2, "LC:16 LC2:32 LX:32 LO:16 LY:16 OU:256 OU2:256 HU:512 SU:16 WL:512")
-_decl(F4, "WD:4112 WE:4112 MT:528 IF:128 INF:128 ZF:128 TB:128 TI:128 TJ:128 TK:128 TL:128 ONE:128 TA:256 TC:16 TC2:16 TD:256 TE:256 TH:256 VV:256 "
-          "KC:8 KW:16 WR:16 LIM:8 JW:8 BC:8 G0:8 RMX:512 RMN:512 RK:128 JC:16 XC:512 K1K:256 CF:512 C1:256 YP:256 YO:256 YQ:512 "
-          "E1:128 EE:256 F:256 FS:128 T2:128 EH:256 SMX:512 PMN:512 KK:64 K:32 KD:48 KQ:32 THP:32 W2:32 "
-          "LT:128 PEN:128 K2:128 KM:128 PF:16 PM:16 PN:16 CV:16 ZP:16 ZW:16 LEN:16 XK:256 Y:272 XS:512 NL:512 LAND0:128 LAND1:128 LAND2:128")
+_decl(I4, "OCN:256 QW:512 THI:16 QI:8 KI:8 H:512 HA:512 TM:32 UU:64 BT:256 BT2:256")
+_decl(U2, "LC:16 LC2:32 LX:32 LR:32 LO:16 LY:16 OU:256 OU2:256 HU:512 SU:16 WL:512")
+_decl(F4, "WD:4112 WE:4112 MT:528 IF:128 INF:128 ZF:128 TB:128 TI:128 TJ:128 TK:128 TL:128 ONE:128 TA:256 TC:16 TC2:16 "
+          "KC:8 KW:16 WR:16 LIM:8 JW:8 BC:8 G0:8 RMX:512 RMN:512 RK:128 JC:16 XC:512 CF:512 C1:256 YP:256 YO:256 YQ:512 "
+          "E1:128 EE:256 F:256 FS:128 EA:256 EH:256 KK:64 K:32 KQ:32 THP:48 W2:32 "
+          "LT:128 PEN:128 K2:128 KM:128 PF:16 PM:16 PN:16 CV:16 ZP:16 ZW:16 LEN:16 XK:256 Y:272 LAND0:128 LAND1:128 LAND2:128")
 SCRATCH["O"] = ("sbuf", [128, 16, 16], FH)
 SCRATCH["T1"] = ("sbuf", [128, 16, 16], F4)
 SCRATCH["O16"] = ("sbuf", [128, 8, 2, 16], FH)
-SCRATCH["OE"] = ("sbuf", [128, 8, 2, 16], FH)
 SCRATCH["P0"] = ("psum", [128, 32, 16], F4)
 SCRATCH["P6"] = ("psum", [128, 32, 16], F4)
 for _n in ("P1", "P2", "P3", "P4", "P5", "P7"):
     SCRATCH[_n] = ("psum", [128, 512], F4)
     WIDTH[_n] = 512
     WHERE[_n] = (_n, 0)
-SEMAPHORES = ["qv", "qs", "qt", "qg", "sent"] + ["arr%d" % t for t in range(3)] + ["d%d" % i for i in range(20)]
+SEMAPHORES = ["qv", "qs", "qt", "qg", "sent"] + ["arr%d" % t for t in range(4)] + ["d%d" % i for i in range(20)]
 
-CYCLE, PE_CYCLE, GATHER, GATHER2, SCATTER = 0.83, 0.42, 1.3, 1.3, 3.2
+CYCLE, PE_CYCLE, GATHER, GATHER2, SCATTER = 0.83, 0.42, 1.25, 1.25, 3.2
 CALL = {"v": 60.0, "s": 200.0, "g": 0.0}
 BANK, PE_OUT = 60.0, 250.0
 HOP, DMA, SEND, REMOTE = 100.0, 2200.0, 1000.0, 1200.0
 AHEAD, SLACK, PATIENCE = 400.0, 50.0, 0.3
 OWN, PASSES, GREEDY, SPANS = 60.0, 4, 2, []
 ORDER = (2, 3, 0, 1)
-SHARED = ((2, 3), (), ())
+SHARED = ((3,), (), ())
 MID = 2040.0
 MOVES = "WE"
+MOVERS = [["ss"] + 7 * ["s"]] * 2 + ["svssvsvs"]
+_LISTS = "OU T1 EM H H:256 HA HU "
+_SCORES = "D02 D12 D03 D13 D00 D10 D01 D11 -PT SW EE EE:128 F -XS ZS WL FS GS1 WL:256 GS3 GS5 GS7 SMX OU2 SMX:384 LAND"
+_KEYS = " PMN TM UU UU:32 UF KK TT K KQ BL AH:512 MG1 MG3"
+_CLOSE = " K2 KM GO CN BT BT2 Y PF PM EH Y' PN SUI SU Y'' AT Y''' XK O"
+VECTOR = ["-ZF -C1 -KI -KC -KW:12 -C1' -LO -C1'' -CF:256 -LR -T1 -OP -O16 -O " + _LISTS
+          + "D02 D12 D03 D00 D10 -WR:5 D01 D11 -WL -LIM -KW:3 -KW:4 SW EE EE:128 F -LC2 -TK -TJ -LX -TJ:64 ZS FS -JW -JC -LIM:1 "
+          + "GS1 GS3 GS5 SMX LAND GS7 SMX:256 OU2 SMX:384 LAND''" + _KEYS + " -KW:5 -KW:10 -KW:9" + _CLOSE,
+          _LISTS + _SCORES + _KEYS + " --LY" + _CLOSE,
+          _LISTS + _SCORES + _KEYS + _CLOSE + " PT GE1 XS YA GE4 GE6 YP YO YQ:384"]
+_WANTS = "-GE0 WG2 -GE0b WG3 -GE1 WG0 -GE2 WG1 -GE3 E1 -GE4 -GE5 -GE6 -GE7 GS0 GS2 GS4 GS6"
+_LIMITS = " MT:16 MG0 MG2 LT PEN"
+_SHIFTS = " CMP:16 EA P1 P1' P1'' P1'''"
+SCALAR = ["-P6 -CF -WD0 -WD0b -WT:16 -WD0b' -WD0b'' WG2 WG3 WG0 D13 WG1 D13' D13b -WD1 -WD2 E1 -WD0' -WD0b''' -WD0b'''' -RMX -RW -G0 "
+          + "-XC -BC:1 -CAT -W2 -THP GS0 GS2 GS4 GS6 -THB NPL NPL:256 NPL:384 -BC:2 NE -R01 -WE0" + _LIMITS + " CF" + _SHIFTS,
+          _WANTS + " CF NE" + _LIMITS + _SHIFTS,
+          _WANTS + " NE" + _LIMITS + _SHIFTS + " GE0 GE2 GE3 GE5 GE7 YQ YQ:256"]
+GPSIMD = ["-QI -WR:8 -TA -TC -TL -TL:96 -IF -IN00 -IN01 -IN10 -IN11 -IN37 -WT -EZ -TI:8 -TI:16 -EZ:15 -IPEN -I16 -CADD -TI:8' -TI:16' "
+          + "-EZ:159 -IN16 -WR:1 LAND' LAND''' -Q16 -K1K -Y:256 -IN4K -CMP -WE1b -WE2b -WE3b -EZ:303 -TL:80 -PT -PT:512 -RS1 -RS2 "
+          + "-OUT00 -OUT01 -OUT10 -OUT11", "", ""]
+PIECES = [(("P4", 0, 4, 4), ("P5", 4, 8, 7))] * 2 + [(("P4", 0, 4, 3), ("P5", 4, 6, 4), ("P3", 6, 8, 6))]
+COPIES = "ssv"
+LIMITS = (0, 64, 128, 192, 256)
+EARLY = True
 
 
 def _bank(name):
@@ -127,6 +150,20 @@ def rank_program(g, core, T, topo):
         steps.append({"queue": q, "time": time, "later": later, "issue": go,
                       "before": sorted(set(p for p, _ in before(seen, q, reads, writes)))})
         note(seen, q, reads, writes, k)
+        if q in "vsg" and writes:
+            n, lo = ("LAND", 0) if writes[0][0].startswith("LAND") else writes[0][:2]
+            n += str(lo // 1024) + "b" * (lo % 1024 > 0) if WIDTH.get(n, 0) >= 4096 else ":%d" % lo if lo else ""
+            while (now[0], n) in names:
+                n += "'"
+            names[now[0], n] = k
+
+    now, names = [-1], {}
+
+    def in_order():
+        for lists_ in (VECTOR, SCALAR, GPSIMD):
+            line = [names[t - n.count("-"), n.lstrip("-")] for t in range(3) for n in lists_[t].split()]
+            for p, k in zip(line, line[1:]):
+                steps[k]["before"].append(p)
 
     def need(q, token):
         sem, n = token
@@ -186,7 +223,7 @@ def rank_program(g, core, T, topo):
     def tt(o, a, b, op):
         n = size(o)
         time = GATHER2 * n if picked(a) else cycles(n if _bank(a[1][0][0]) or _bank(b[1][0][0]) else 2 * n)
-        run("v", lambda: g.vector.tensor_tensor(o[0], a[0], b[0], op), R(a, b), o[1], time, [("lineD", 0, 1, 1)] if n == 1024 else [])
+        run("v", lambda: g.vector.tensor_tensor(o[0], a[0], b[0], op), R(a, b), o[1], time)
 
     def ts(o, a, s1, op0, s2=None, op1=None):
         time = GATHER * size(o) if picked(a) else cycles(size(o), o, a)
@@ -216,15 +253,17 @@ def rank_program(g, core, T, topo):
     def act(o, a, func=Act.Copy, bias=0.0, scale=1.0):
         run("s", lambda: g.scalar.activation(o[0], a[0], func, bias=val(bias), scale=val(scale)), R(a, bias, scale), o[1], cycles(size(o)))
 
-    def gather(o, win, off, q):
+    def gather(o, win, off, q, plus=0.0):
         a = IND(win, off)
 
         def go(on):
-            if on == "v":
-                issue(on, lambda: g.vector.tensor_copy(o[0], a[0]), a[1], o[1])
+            if on == "s":
+                issue(on, lambda: g.scalar.activation(o[0], a[0], Act.Copy, bias=plus), a[1], o[1])
+            elif plus:
+                issue(on, lambda: g.vector.tensor_scalar(o[0], a[0], plus, None, Op.add), a[1], o[1])
             else:
-                issue(on, lambda: g.scalar.activation(o[0], a[0], Act.Copy), a[1], o[1])
-        step(q, 60.0 + GATHER * size(o), a[1], o[1] + [("line" + q + o[1][0][0], 0, 1, 1)], go)
+                issue(on, lambda: g.vector.tensor_copy(o[0], a[0]), a[1], o[1])
+        step(q, 60.0 + GATHER * size(o), a[1], o[1], go)
 
     def mm(o, l, r, start=True, stop=True, more=False, cut=False):
         wide = WHERE.get(l[1][0][0], ("",))[0] == "pool_" + F4
@@ -274,11 +313,19 @@ def rank_program(g, core, T, topo):
         step(q, 50.0 * len(items), sum([a[1] for o, a in items], []), sum([o[1] for o, a in items], []), go, later)
 
     def issue_all():
+        in_order()
         n = len(steps)
         after = [[] for _ in steps]
         for k, s in enumerate(steps):
             for p in s["before"]:
                 after[p].append(k)
+        line, left = [k for k in range(n) if not steps[k]["before"]], [len(s["before"]) for s in steps]
+        for p in line:
+            for k in after[p]:
+                left[k] -= 1
+                if not left[k]:
+                    line.append(k)
+        assert len(line) == n
 
         def gap(p, k):
             same = steps[p]["queue"] == steps[k]["queue"]
@@ -322,7 +369,7 @@ def rank_program(g, core, T, topo):
             return end
 
         way = {}
-        for k in range(n - 1, -1, -1):
+        for k in reversed(line):
             way[k] = steps[k]["time"] + max([way[x] + gap(k, x) for x in after[k]] + [steps[k]["later"]])
         best = None
         for turn_ in range(PASSES):
@@ -346,10 +393,10 @@ def rank_program(g, core, T, topo):
         return [(ez(sel, r), A(n, lo + r, lo + width - 15 + r, 16)) for r in range(16)]
 
     dmas("y", [(A("OCN"), ext(T.oc[:]))])
-    dmas("s", [(A("WT", 16, 528), ext(T.want[:]))])
-    dmas("y", [(A("XT", 2048 * c, 2048 * c + 2048), ext(T.x[:, 2048 * c:2048 * c + 2048])) for c in range(2)], 4000.0)
-    dmas("y", [(A("QW"), ext(T.qs[:])), (A("THI", 0, 1), ext(T.th[:]))], 5000.0)
+    dmas("s", [(A("WI"), ext(T.want[:]))])
+    dmas("y", [(A("XT"), ext(T.x[:]))], 5000.0)
     loads = len(steps)
+    dmas("y", [(A("QW"), (T.qs[:], A("XT")[1])), (A("THI", 0, 1), ext(T.th[:]))])
 
     q1, kc, one = A("QI", 0, 1), A("KC", 0, 1), A("ONE")
     part = (1.5 - rank) / 8.0
@@ -360,18 +407,20 @@ def rank_program(g, core, T, topo):
 
     def constants():
         iota(q1, [[0, 1]], 0, 1, False)
-        fill(A("ONE"), 1.0)
+        iota(A("ONE"), [[0, 128]], 1)
         fill(A("ZF"), 0.0)
         ts(A("KI", 0, 1), q1, 15, Op.bitwise_and)
         cp(kc, A("KI", 0, 1))
-        for name, v in (("IF", 1.0), ("INF", -1.0), ("I16", 1.0), ("IN16", -1.0), ("I37", 37.0), ("IN37", -37.0), ("I8K", 8192.0),
+        for name, v in (("IF", 1.0), ("INF", -1.0), ("I16", 1.0), ("IN16", -1.0), ("I37", 37.0), ("I2K", 2048.0), ("I8K", 8192.0),
+                        ("I4K", 4096.0), ("IN4K", -4096.0),
                         ("IN8K", -8192.0), ("I14", 16384.0), ("IPEN", -32768.0), ("IM2K", -1.0 / 2048), ("IM1K", -1.0 / 1024),
-                        ("IP1K", 1.0 / 1024)):
+                        ("IN37", -37.0), ("IP1K", 1.0 / 1024)):
             aff(A(name), A("ZF"), [[-1, 128]], Op.not_equal, v, 0, 1)
         for h in range(2):
             for b in range(2):
                 aff(A("IN%d%d" % (h, b)), A("ZF"), [[-32, 4], [1000, 2], [-2, 16]], Op.not_equal, 1.0, -b - 1000 * h, 1)
-                aff(A("OUT%d%d" % (h, b)), A("ZF"), [[-32, 4], [-1, 16], [1000, 2]], Op.not_equal, 1.0, -16 * h - 1000 * b, 1)
+                aff(A("OUT%d%d" % (h, b)), A("ZF"), [[-32, 4], [-1, 16], [1000, 2]], Op.not_equal, -1.0, -16 * h - 1000 * b, 1)
+        aff(A("J16"), A("ZF"), [[1, 128]], Op.not_equal, 1.0, -127, 1)
         aff(A("TB"), one, [[-16, 8], [0, 16]], Op.is_ge, 0.0, 0, 1)
         aff(A("BO"), A("TB"), [[16, 8], [0, 16]], Op.is_ge, 0.0, 15, -1)
         ones = A("BO", 0, 128, 16)
@@ -379,132 +428,129 @@ def rank_program(g, core, T, topo):
         def row(o, a, r, v):
             aff(o, a, [[-16, 8]], Op.not_equal, v, -r, 1)
 
-        fill(A("EZ"), 0.0)
-        for i, v in enumerate((1.0, -1.0)):
-            ts(A("EZ", 144 * i + 15, 144 * i + 143, 16), ones, v, Op.mult)
-        row(A("TI", 8, 16), A("ZF", 0, 8), move_row, 1.0)
-        cp(A("EZ", 288 + 15, 288 + 143, 16), A("TI", 8, 16))
-        fill(PART("L32", 0, 64), 1.0 / 32)
-        for t in range(3):
-            fill(PART("KT", 0, 32, 1, 256 * t, 256 * t + 256), 77.0 * t - 1280.0)
-        fill(PART("KT", 32, 64), -15.0 / 32)
+        iota(A("EZ"), [[0, 432]], 0)
+        for i, v in enumerate((1, -1)):
+            iota(A("TI", 8, 16), [[0, 8]], v)
+            aff(A("TI", 16, 24), A("TI", 8, 16), [[-16, 8]], Op.is_ge, 0.0, 0, 1)
+            aff(A("EZ", 144 * i + 15, 144 * i + 143, 16), A("TI", 16, 24), [[16, 8]], Op.is_ge, 0.0, 15, -1)
+        row(A("EZ", 288 + 15, 288 + 143, 16), A("ZF", 0, 8), move_row, -1.0)
         iota(A("CADD"), [[0, 64]], -int(MID))
         iota(A("TA"), [[1, 256]], 0)
         iota(A("TC"), [[2, 16]], 17)
-        ts(A("KW", 0, 1), kc, 16.0, Op.mult)
-        ts(A("KW", 1, 2), kc, 32.0, Op.mult)
-        act(A("P6"), A("TA"), Act.Identity, bias=A("KW", 1, 2), scale=0.125)
-        fill(A("C1"), -247.5)
-        ts(A("C1", 0, 256, 16), A("TC"), 0.5, Op.mult, A("KW", 0, 1), Op.add)
-        tt(A("CF", 0, 256), A("C1"), A("P6"), Op.mult)
-        act(A("CF", 256, 512), A("CF", 0, 256))
+        iota(A("WR", 8, 12), [[8, 4]], 8)
+        ts(A("KW", 12, 16), A("WR", 8, 12), kc, Op.mult)
+        k8, k16, k32 = A("KW", 12, 13), A("KW", 13, 14), A("KW", 15, 16)
+        act(A("P6"), A("TA"), Act.Identity, bias=k32, scale=0.125)
+        fill(A("C1"), 775.5)
+        ts(A("C1", 0, 256, 16), A("TC"), 0.5, Op.mult, k16, Op.add)
+        tt(A("C1"), A("C1"), A("P6"), Op.mult)
+        act(A("CF", 0, 256), A("C1"), bias=37.0 * 767 - 15.0 / 32)
+        ts(A("CF", 256, 512), A("C1"), 37.0 * 767 - 15.0 / 32, Op.add)
         fill(A("T1"), 0.0)
         iota(A("TL", 0, 16), [[1, 8], [128, 2]], 0)
-        ts(A("KW", 2, 3), kc, 8.0, Op.mult)
-        ts(A("LO"), A("TL", 0, 16), A("KW", 2, 3), Op.add)
-        ts(A("OP"), IND(A("OCN"), A("LO")), 256.0, Op.add)
+        ts(A("LO"), A("TL", 0, 16), k8, Op.add)
+        ts(A("OP"), IND(A("OCN"), A("LO")), -1.0, Op.mult, 767.0, Op.add)
         turn(M(T.O16[:], "O16"), A("OP"))
-        ts(M(T.OE[:], "OE"), M(T.O16[:], "O16"), 767.5, Op.is_ge, -768.0, Op.mult)
+        iota(A("TL", 96, 128), [[-16, 32]], 511)
+        ts(A("LR"), A("TL", 96, 128), kc, Op.subtract)
+        gather(A("WT", 16, 528), A("WI"), A("LR"), "s")
         for b in range(2):
-            mms(A("P1", 128 * b, 128 * b + 128), [(A("IN%d%d" % (h, b)), M(T[n][:, :, h, :], n)) for n in ("O16", "OE") for h in range(2)], more=b < 1)
+            mms(A("P1", 128 * b, 128 * b + 128), [(A("IN%d%d" % (h, b)), M(T.O16[:, :, h, :], "O16")) for h in range(2)], more=b < 1)
         cp(A("O"), A("P1", 0, 256))
         const(A("WT", 0, 16), 0.0)
         cp(A("WL"), A("QW"))
 
         row(A("TI", 0, 8), A("ZF", 0, 8), 0, 1.0)
-        cp(A("RS"), A("TI", 0, 8))
+        row(A("RS"), A("ZF", 0, 8), 0, 1.0)
         for t in range(3):
             row(A("RS%d" % t), A("TI", 0, 8), 5 + t, 1.0)
-        fill(A("WD", 0, 512), 0.0)
-        for lo in (512, 1024, 2048):
+        act(A("WD", 0, 128), A("ZF"))
+        for lo in (128, 256, 512, 1024, 2048):
             act(A("WD", lo, 2 * lo), A("WD", 0, lo))
         iota(A("WR", 1, 4), [[1, 3]], 5)
         ts(A("WR", 5, 8), A("WR", 1, 4), kc, Op.is_equal, -8192.0, Op.mult)
-        ts(A("WR", 4, 5), kc, 4.5, Op.is_gt, -8192.0, Op.mult)
-        ts(A("WR", 8, 9), kc, 0.5, Op.is_lt, -4096.0, Op.mult)
-        ts(A("WR", 9, 10), kc, float(move_row), Op.is_equal, 2048.0, Op.mult)
-        ts(A("WR", 10, 11), A("WR", 4, 5), A("WR", 8, 9), Op.add, A("WR", 9, 10), Op.add)
         for t in range(3):
-            ts(A("WD", 16 * t, 4096, 128), A("ZF", 0, 32), A("WR", 5 + t, 6 + t), Op.add)
-        ts(A("WD", 4096, 4112), A("ZF", 0, 16), A("WR", 10, 11), Op.add)
-        if MOVES != "WD":
-            ts(A("WE", 4096, 4112), A("ZF", 0, 16), A("WR", 10, 11), Op.add)
-            for lo in range(0, 4096, 1024):
-                act(A("WE", lo, lo + 1024), A("XT", lo, lo + 1024))
+            act(A("WD", 16 * t, 4096, 128), A("ZF", 0, 32), Act.Identity, bias=A("WR", 5 + t, 6 + t))
+        iota(A("WD", 4096, 4112), [[0, 16]], -4096)
+        act(A("WE", 0, 1028), A("XT", 0, 1028))
+        for lo in range(1028, 4112, 1028):
+            iota(A("WE", lo, lo + 1028), [[0, 1028]], 0)
         iota(A("RMN"), [[0, 512]], -1000000)
         const(A("RMN", 0, 512, 16), 1.0e6)
         act(A("RMX"), A("RMN"), scale=-1.0)
         act(A("R01"), A("RMX", 0, 256), Act.Relu, scale=1.0e-6)
         iota(A("YC"), [[1, 16], [0, 32]], 0)
-        act(A("XC"), A("YC"), bias=part, scale=1.0 / 128)
-        act(A("Q4"), A("YC"), bias=0.25, scale=0.0)
-        iota(A("TD"), [[0, 16], [1, 16]], 0)
-        act(A("K1K"), A("TD"), bias=-16640.0, scale=1024.0)
-        iota(A("VV"), [[16, 16], [256, 16]], -4096)
-        iota(A("TC2"), [[16, 16]], 512)
+        act(A("XC"), A("YC"), bias=part + 4096.0, scale=1.0 / 128)
+        iota(A("Q1"), [[0, 256]], 1)
+        iota(A("K1K"), [[0, 16], [-1024, 16]], 15360)
+        iota(A("TC2"), [[-16, 16]], 1279)
         iota(A("BIG"), [[0, 16]], 65536)
-        act(A("RW"), ones, scale=A("KW", 0, 1))
+        act(A("RW"), ones, scale=k16)
         for o in (A("AH", 0, 512), A("AH", 1024, 1536), A("PT", 0, 512), A("TT")):
             iota(o, [[0, 512]], 0)
         iota(A("PT", 512, 768), [[0, 256]], 0)
         iota(A("MT", 0, 16), [[0, 16]], 32768)
         iota(A("CMP", 0, 16), [[0, 16]], 1)
-        iota(A("KD", 32, 48), [[0, 16]], -1000000)
+        iota(A("THP", 32, 48), [[0, 16]], 32768)
+        iota(A("Q16"), [[0, 256]], 16)
         const(A("Y", 256, 272), 2.0 ** 25)
-        ts(A("KW", 6, 7), kc, 256.0, Op.mult, -2048.0, Op.add)
-        act(A("NPL"), A("TA"), Act.Identity, bias=A("KW", 6, 7))
         iota(A("TL", 16, 48), [[1, 32]], 0)
-        cp(A("LC"), A("TL", 16, 32))
         ts(A("KW", 3, 4), kc, 14.5, Op.is_lt)
         ts(A("KW", 4, 5), kc, 14.5, Op.is_gt, 32.0, Op.mult)
         ts(A("LC2"), A("TL", 16, 48), A("KW", 3, 4), Op.mult, A("KW", 4, 5), Op.add)
-        ts(A("KW", 5, 6), A("KW", 3, 4), 8192.0, Op.mult, 2048.0, Op.add)
+        ts(A("KW", 5, 6), A("KW", 3, 4), -8192.0, Op.mult)
+        ts(A("KW", 10, 11), A("KW", 3, 4), 8192.0, Op.mult, 2048.0, Op.add)
         iota(A("TL", 48, 80), [[0, 16], [16, 2]], 0)
         ts(A("LX"), A("TL", 48, 80), kc, Op.add)
         ts(A("KW", 9, 10), kc, 7.5, Op.is_gt, -255.0, Op.mult)
         iota(A("TL", 80, 96), [[2, 16]], 0)
-        ts(A("LY"), A("TL", 80, 96), A("KW", 1, 2), Op.add, A("KW", 9, 10), Op.add)
-        ts(A("KW", 7, 8), kc, 0.5, Op.is_lt, 16.0, Op.mult)
-        ts(A("KW", 8, 9), kc, -1.0, Op.add, A("KW", 7, 8), Op.add)
-        ts(A("TH"), A("TD"), kc, Op.is_equal, 64.0, Op.mult)
-        ts(A("TE"), A("TD"), A("KW", 8, 9), Op.is_equal)
-        tt(A("TE"), A("TE"), A("VV"), Op.mult)
-        mms(A("P7", 0, 256), [(A("IF"), A("TE")), (A("IF"), A("TH"))])
+        ts(A("LY"), A("TL", 80, 96), k32, Op.add, A("KW", 9, 10), Op.add)
+        iota(PART("VV", 0, 16), [[16, 16], [256, 16]], -4096)
+        aff(PART("TE", 0, 16), PART("VV", 0, 16), [[0, 16], [1, 16]], Op.is_equal, 0.0, 1, -1)
+        aff(PART("TE", 0, 16), PART("TE", 0, 16), [[0, 16], [1, 16]], Op.not_equal, 64.0, 0, -1)
+        aff(PART("TH", 0, 16), PART("VV", 0, 16), [[0, 16], [1, 16]], Op.is_equal, 0.0, -15, -1)
+        aff(PART("REP", 0, 16), PART("ZF", 0, 16), [[0, 8], [1, 16]], Op.not_equal, 1.0, 0, -1)
+        mms(A("P7", 0, 256), [(PART("REP", 0, 16), PART(n, 0, 16)) for n in ("TE", "TH")])
         act(A("CAT"), A("P7", 0, 256))
         const(A("BC", 0, 1), 2.0 ** -63.2)
         act(A("BC", 1, 2), A("BC", 0, 1), Act.Ln)
         act(A("BC", 2, 3), A("BC", 1, 2), scale=2000.0)
-        act(A("JC"), A("TC2"), Act.Identity, bias=kc)
+        ts(A("JC"), A("TC2"), kc, Op.subtract)
         const(A("TI", 64, 128), 0.25)
         scan(A("TJ", 0, 64), A("TI", 64, 128), A("ZF", 0, 64), 2.0 ** 65, Op.mult, Op.max)
         tt(A("TK", 0, 64), A("IF", 0, 64), A("IF", 64, 128), Op.add)
         tt(A("TJ", 64, 128), A("TJ", 0, 64), A("TK", 0, 64), Op.mult)
         total(A("JW", 0, 1), A("TJ", 64, 128))
-        ts(A("JW", 1, 2), A("JW", 0, 1), -1.0, Op.mult)
-        const(A("RK"), -128.0 * 2 * LN2)
-        const(A("RK", 4, 128, 8), 320.0 * 2 * LN2)
-        const(A("RK", 0, 128, 8), 1.0e6)
+        const(A("RK"), 128.0 * 2 * LN2)
+        const(A("RK", 4, 128, 8), -320.0 * 2 * LN2)
+        const(A("RK", 0, 128, 8), -1.0e6)
         cp(A("LIM", 0, 1), A("THI", 0, 1))
         ts(A("LIM", 1, 2), A("THI", 0, 1), 0.5, Op.add)
         act(A("G0"), A("TI", 0, 8), scale=A("LIM", 0, 1))
         for c in range(4):
             mm(A("P7", 256 + 8 * c, 264 + 8 * c), one, A("G0"), more=True)
-            mm(A("P7", 288 + 8 * c, 296 + 8 * c), A("WT", 16 + 128 * c, 144 + 128 * c), A("RW"), more=c < 3)
-        act(A("THP"), A("P7", 256, 288))
+            mm(A("P7", 288 + 8 * c, 296 + 8 * c), A("WI", 128 * c, 128 + 128 * c), A("RW"), more=c < 3)
+        act(A("THP", 0, 32), A("P7", 256, 288), bias=-MID)
+        gather(A("THB"), A("THP"), A("LC2"), "s")
         act(A("W2"), A("P7", 288, 320), bias=MID + 8192.0)
+
+    def later_constants():
+        act(A("NPL", 0, 256), A("P6"), bias=-2048.0, scale=8.0)
+        for b in range(2):
+            act(A("NPL", 256 + 128 * b, 384 + 128 * b), A("NPL", 128 - 128 * b, 256 - 128 * b), scale=-1.0)
 
     def lists(t):
         o = A("O")
         ts(A("OU"), o, -240.0, Op.add)
-        mm(whole(A("P0", 0, 512)), A("IF"), A("CF"), True, False)
+        mm(whole(A("P0", 0, 512)), A("IF"), A("CF"), True, False, cut=True)
+        if t < 2:
+            act(A("CF"), A("CF"), bias=77.0)
+        mm(whole(A("P0", 0, 256)), A("IN37"), o, False, False)
         for b in range(2):
-            mm(whole(A("P0", 256 * b, 256 * b + 256)), PART("L32", 0, 64), PART("KT", 0, 64, 1, 256 * t, 256 * t + 256), False, False, cut=b == 1)
-        mm(whole(A("P0", 0, 256)), A("I37"), o, False, False)
-        for b in range(2):
-            mm(whole(A("P0", 256 + 128 * b, 384 + 128 * b)), A("I37"), A("O", 128 - 128 * b, 256 - 128 * b), False, b == 1)
+            mm(whole(A("P0", 256 + 128 * b, 384 + 128 * b)), A("IN37"), A("O", 128 - 128 * b, 256 - 128 * b), False, b == 1)
         tt((T.T1[:, :, 1:16], [("T1", 0, 256, 1)]), (T.O[:, :, 0:15], o[1]), (T.P6[:, 0:16, 1:16], [("P6", 0, 256, 1)]), Op.mult)
         for b in range(2):
-            tt(A("H", 256 * b, 256 * b + 256), A("T1"), A("P0", 256 * b, 256 * b + 256), Op.add)
+            tt(A("H", 256 * b, 256 * b + 256), A("P0", 256 * b, 256 * b + 256), A("T1"), Op.subtract)
         ts(A("HA"), A("H"), 4095, Op.bitwise_and)
         cp(A("HU"), A("HA"))
         ts(A("EM"), o, 255.5, Op.is_lt)
@@ -563,8 +609,11 @@ def rank_program(g, core, T, topo):
         exchanged([])
         ts(A("OU2"), A("P0", 256, 512), -240.0, Op.add)
 
-    def by_slot(n, win, m, q):
-        gather(A(n, 1024 * m, 1024 * m + 1024), A(win), A("WL", 64 * m, 64 * m + 64), q)
+    def by_slot(n, win, m, q, plus=0.0):
+        w = 64 // len(q)
+        for i, on in enumerate(q):
+            lo = 64 * m + w * i
+            gather(A(n, 16 * lo, 16 * lo + 16 * w), A(win), A("WL", lo, lo + w), on, plus)
 
     def read(bank, at, sel, c):
         for s in range(16):
@@ -578,18 +627,19 @@ def rank_program(g, core, T, topo):
 
     best = A("SMX", 15, 512, 16)
 
-    def roll(t):
+    def largest(bank, at, lo, hi):
+        scan(A("SMX", lo, hi), A("RMX", 0, hi - lo), A(bank, at, at + hi - lo), 0.0, Op.min, Op.max)
+
+    def roll(t, lo, hi):
         land = "LAND%d" % t
-        own = A(land, 32 * rank, 32 * rank + 32)
-        scan(A("SMX", 0, 384), A("RMX", 0, 384), A("P1", 0, 384), 0.0, Op.min, Op.max)
-        scan(A("SMX", 384, 512), A("RMX", 0, 128), A("P2", 0, 128), 0.0, Op.min, Op.max)
-        ts(own, best, part, Op.add, -3000.0, Op.max)
-        others = [(land, 32 * r, 32 * r + 32, 1) for r in range(4) if r != rank]
+        own = A(land, 32 * rank + lo, 32 * rank + hi)
+        ts(own, A("SMX", 16 * lo + 15, 16 * hi, 16), part, Op.add, -3000.0, Op.max)
+        others = [(land, 32 * r + lo, 32 * r + hi, 1) for r in range(4) if r != rank]
 
         def go(on):
             deps(on, own[1], [])
             tr = []
-            tok = ("arr%d" % t, sum([p[2] for p in plan]))
+            tok = ("arr%d" % (t if hi == 32 else 3), sum([p[2] for p in plan]))
             for d, mask, ne in plan:
                 rid, pid = topo.addr(d, core)
                 tr.append(RemoteDMATransfer(dst_ids=[DstId(rid=rid, pnc=pid)], dma_engine_mask=mask, remote_sem=T.sem[tok[0]], src=own[0], dst=own[0]))
@@ -606,36 +656,40 @@ def rank_program(g, core, T, topo):
         ts(A("UU", 0, 32), A("TM"), 0xF0, Op.bitwise_and)
         ts(A("UU", 32, 64), A("TM"), 15, Op.bitwise_and)
         cp(A("UF"), A("UU"))
-        tt(A("KD", 0, 32), best, A("THP"), Op.subtract)
-        tt(A("NE"), A("PMN", 15, 512, 16), A("KD", 0, 32), Op.is_ge)
-        mms(A("P2", 384, 416), [(A("IF"), best), (A("IM2K"), A("UF", 0, 32)), (A("I8K"), A("NE"))])
+        mms(A("P2", 416, 448), [(A("I16"), A("THB", 0, 512, 16)), (A("IN16"), best), (A("I16"), A("PMN", 15, 512, 16))])
+        act(A("NE"), A("P2", 416, 448), Act.Sign, bias=MID + 0.5)
+        mms(A("P2", 384, 416), [(A("I16"), best), (A("IM2K"), A("UF", 0, 32)), (A("I4K"), A("NE"))])
         mm(A("P7"), A("IN16"), A("YC"), True, False)
         for y in range(16):
             mm(A("P7", 32 * y, 32 * y + 32), A("I16"), A("UF", 32, 64), False, y == 15)
-        act(A("B0"), A("P7"), Act.Abs)
-        act(A("BL"), A("B0"), Act.Relu, bias=A("JW", 0, 1), scale=A("JW", 1, 2))
-        tt(A("CMP", 16, 528), IND(A("KD"), A("LC2")), A("PMN"), Op.is_le)
+        ts(A("BL"), A("P7"), 0.0, Op.is_equal, A("JW", 0, 1), Op.mult)
+
+    def staying():
+        mms(A("P5"), [(A("I16"), A("THB")), (A("I16"), A("PMN"))], True, False)
+        for s in range(15):
+            mm(A("P5", s, 512, 16), A("IN16"), best, False, s == 14)
+        act(A("CMP", 16, 528), A("P5"), Act.Sign, bias=MID + 0.5)
 
     def thresholds(t):
         land = "LAND%d" % t
         tt(A("KK"), A(land, 0, 64), A(land, 64, 128), Op.max)
         tt(A("TT", 0, 512, 16), A("KK", 0, 32), A("KK", 32, 64), Op.max)
         for c in range(4):
-            mm(A("P1", 128 * c, 128 * c + 128), A("TT", 128 * c, 128 * c + 128), A("I16"), more=c < 3)
+            mm(A("P1", 384 - 128 * c, 512 - 128 * c), A("TT", 128 * c, 128 * c + 128), A("J16"), more=c < 3)
         act(A("MT", 16, 528), A("P1"))
         tt(A("K"), A("KK", 0, 32), A("KK", 32, 64), Op.max)
         tt(A("KQ"), A("K"), A("P2", 384, 416), Op.subtract)
         tt(A("AH", 512, 1024), IND(A("KQ"), A("LX")), A("XC"), Op.is_equal)
 
     def limits(t, c):
-        w = (64 * c, 64 * c + 64)
-        gather(A("MG", 1024 * c, 1024 * c + 1024), A("MT"), A("OU2", *w), "sv"[c & 1])
+        w = LIMITS[c:c + 2]
+        gather(A("MG", 16 * w[0], 16 * w[1]), A("MT"), A("OU2", *w), "sv"[c & 1])
         if c == 0:
             mm(whole(A("P4", 0, 256)), A("INF"), A("F"), True, False)
             for b, l in enumerate(("IF", "INF")):
                 mm(whole(A("P4", 128 * b, 128 * b + 128)), A(l), A("FS"), False, False)
             mm(whole(A("P4", 16 * t, 256, 128)), A("I16"), A("BIG", 0, 2), False, False, cut=True)
-        mms(whole(A("P4", *w)), rows("EZ1", "MG", 1024 * c, 1024), False, c == 3, cut=c < 3)
+        mms(whole(A("P4", *w)), rows("EZ1", "MG", 16 * w[0], 16 * (w[1] - w[0])), False, c == 3, cut=c < 3)
 
     def logs():
         for j in range(2):
@@ -648,8 +702,8 @@ def rank_program(g, core, T, topo):
                        not x & 1, bool(x & 1), 8 * c + x < 31)
         act(A("LT"), A("P3", 0, 128), Act.Ln, bias=2.0 ** -64)
         act(A("PEN"), A("LT"), Act.Relu, bias=A("BC", 2, 3), scale=-2000.0)
-        tt(A("K2"), A("PEN"), A("LT"), Op.subtract)
-        scan(A("KM"), A("RK"), A("K2"), 0.0, Op.add, Op.min)
+        tt(A("K2"), A("LT"), A("PEN"), Op.subtract)
+        scan(A("KM"), A("RK"), A("K2"), 0.0, Op.add, Op.max)
 
     def leave():
         ts(A("GO"), A("P4", 0, 256), A("LIM", 1, 2), Op.is_gt, 1024.0, Op.mult)
@@ -660,103 +714,125 @@ def rank_program(g, core, T, topo):
         tt(A("Y", 0, 256), A("BT2"), A("P0", 256, 512), Op.add)
 
     def new_places():
-        mms(A("P2", 256, 384), [(A(l), A(n, lo, lo + 128)) for n, two in (("NPL", ("I16", "IN16")), ("GO", ("I37", "IN37")), ("CN", ("IM1K", "IP1K")))
-                                for l, lo in zip(two, (0, 128))], more=True)
-        mms(A("P2", 0, 256), [(A("I16"), A("NPL")), (A("I37"), A("GO")), (A("IM1K"), A("CN"))])
-        tt(A("T2"), A("P2", 256, 384), A("SW"), Op.mult)
-        tt(A("EH", 0, 128), A("P2", 0, 128), A("T2"), Op.subtract)
-        tt(A("EH", 128, 256), A("P2", 128, 256), A("T2"), Op.add)
+        mm(whole(A("P2")), A("I16"), A("NPL"), True, False)
+        for l in ("IN8K", "I2K"):
+            mm(whole(A("P2", 256, 512)), A(l), A("Q1", 0, 256), False, False)
+        for b in range(4):
+            mm(whole(A("P2", 128 * b, 128 * b + 128)), A("I8K"), A("SW"), False, False, cut=b == 3)
+        for l, m, n in (("I37", "IN37", "GO"), ("IM1K", "IP1K", "CN")):
+            mm(whole(A("P2", 0, 256)), A(l), A(n), False, False)
+            for b in range(2):
+                mm(whole(A("P2", 256 + 128 * b, 384 + 128 * b)), A(m), A(n, 128 - 128 * b, 256 - 128 * b), False, n == "CN" and b == 1, cut=b == 1)
+        act(A("EA"), A("P2", 0, 256), Act.Relu, bias=2048.0, scale=-1.0)
+        tt(A("EH"), A("EA"), A("P2", 256, 512), Op.max)
         to_window(MOVES, move_row, A("EH"))
 
     def close_up(j):
         act(A("P1", 0, 272), A("Y"), Act.Abs, bias=-2.0 ** (23 - 3 * j))
         if j == 3:
-            tt(A("XK"), A("Y", 0, 256), A("XK"), Op.min)
+            tt(A("XK"), A("Y", 0, 256), A("P3", 0, 256), Op.min)
         tt(A("O") if j == 3 else A("Y", 0, 256), A("XK") if j == 3 else A("Y", 0, 256), A("P1", 1 << j, 256 + (1 << j)), Op.min)
 
     def winners():
         left = A("CN", 15, 256, 16)
         ts(A("PF"), left, 0.5, Op.is_lt, 1.0e4, Op.mult)
-        tt(A("PM"), A("KM", 7, 128, 8), A("PF"), Op.add)
-        ts(A("PN"), A("PM"), 0.5 / LN2, Op.mult, 479.6, Op.add)
-        tt(A("SUI"), A("PN"), A("JC"), Op.min)
-        ts(A("CV"), A("SUI"), 511.5, Op.is_ge, -768.0, Op.mult)
-        tt(A("ZP"), A("SUI"), left, Op.subtract)
-        tt(A("ZW"), A("ZP"), A("CV"), Op.add)
-        tt(A("XK"), IND(A("ZW"), A("LC")), A("K1K"), Op.subtract)
+        tt(A("PM"), A("KM", 7, 128, 8), A("PF"), Op.subtract)
+        ts(A("PN"), A("PM"), 0.5 / LN2, Op.mult, 1280.0 + 31.4, Op.add)
+        tt(A("SUI"), A("PN"), A("JC"), Op.max)
+        mm(whole(A("P3", 0, 256)), A("I16"), A("K1K"), True, False)
+        for k in range(16):
+            mm(whole(A("P3", k, 256, 16)), A("IN16"), left, False, False, cut=k == 15)
+        for k in range(16):
+            mm(whole(A("P3", k, 256, 16)), A("I16"), A("SUI"), False, k == 15)
 
-    def new_entries(last):
-        cp(A("SU"), A("SUI"))
-        ts(A("LEN"), A("CN", 15, 256, 16), -1.0 / 1024, Op.mult, 16.0, Op.add)
-        tt(A("AT"), IND(A("LEN"), A("LC")), A("CAT"), Op.min)
+    def new_entries():
+        ts(A("SU"), A("SUI"), -1.0, Op.mult, 1280.0 + 511.0, Op.add)
+        mm(A("P5", 0, 256), A("I16"), A("Q16"), True, False)
+        for k in range(16):
+            mm(A("P5", k, 256, 16), A("IM1K"), A("CN", 15, 256, 16), False, k == 15)
+        tt(A("AT"), A("P5", 0, 256), A("CAT"), Op.min)
         scatter(A("PT"), A("SU"), A("AT"))
-        mm(whole(A("P7")), A("I8K"), A("Q4"), True, False)
+        mm(whole(A("P7")), A("I16"), A("AH", 0, 512), True, False)
         for c in range(4):
             o = whole(A("P7", 128 * c, 128 * c + 128))
-            mm(o, A("CMP", 16 + 128 * c, 144 + 128 * c), A("I8K"), False, False)
-            mm(o, A("CMP", 15 + 128 * c, 143 + 128 * c), A("IN8K"), False, False, cut=c == 3)
+            mm(o, A("CMP", 16 + 128 * c, 144 + 128 * c), A("I4K"), False, False)
+            mm(o, A("CMP", 15 + 128 * c, 143 + 128 * c), A("IN4K"), False, False, cut=c == 3)
         mm(whole(A("P7")), A("BO"), A("PT", 0, 512), False, True)
-        if last:
-            ts(A("XS"), A("P7"), A("KW", 5, 6), Op.add, 4096.0, Op.min)
-        else:
-            act(A("XS"), A("P7"), Act.Identity, bias=A("KW", 5, 6))
+        ts(A("XS"), A("P7"), A("KW", 5, 6), Op.min, A("KW", 10, 11), Op.add)
 
-    def move(m, q):
-        bank = "P5" if m & 4 else "P4"
-        by_slot("GE", MOVES, m, q)
-        if not m & 3:
-            mm(whole(A(bank, 0, 256)), A("I8K"), A("Q4", 0, 256), True, False, cut=True)
-        mms(whole(A(bank, 64 * (m & 3), 64 * (m & 3) + 64)), rows("EZR", "GE", 1024 * m, 1024), False, m & 3 == 3, cut=True)
+    def move(m, q, last):
+        bank, lo, hi, news = [x for x in last if x[1] <= m < x[2]][0]
+        o, new = whole(A(bank, 0, 64 * (hi - lo))), (A("I16"), A("XS", 64 * lo, 64 * hi))
+        by_slot("GE", MOVES, m, q, -2048.0)
+        if m == lo:
+            mm(o, *(new if news == lo else (A("I16"), A("AH", 0, 64 * (hi - lo)))), True, False, cut=news == lo)
+        elif m == news:
+            mm(o, *new, False, False, cut=True)
+        mms(whole(A(bank, 64 * (m - lo), 64 * (m - lo) + 64)), rows("EZR", "GE", 1024 * m, 1024), False, m == hi - 1 and news < hi, cut=True)
+        if m == hi - 1 and news == hi:
+            mm(o, *new, False, True)
 
-    def new_slots(out, h):
-        w = (256 * h, 256 * h + 256)
-        tt(A(out, *w), A("P5" if h else "P4", 0, 256), A("XS", *w), Op.min)
-        if out == "NL":
-            ts(A("WL", *w), A("NL", *w), 4096.0, Op.min)
+    def new_slots(out, piece, copy):
+        bank, lo, hi, _ = piece
+        copy(A(out, 64 * lo, 64 * hi), A(bank, 0, 64 * (hi - lo)))
 
     constants()
     for t in range(3):
+        now[0] = t
         lists(t)
         for c in ORDER:
             wants(c)
             minima(c, SHARED[t])
         decide()
         exchange()
-        for h in range(2) if t else ():
-            new_slots("NL", h)
+        for piece in PIECES[t - 1] if t else ():
+            new_slots("WL", piece, cp)
         for c in range(4):
             for m in (2 * c, 2 * c + 1):
                 by_slot("GS", "WD", m, "sv"[m & 1])
-            read("P1" if c < 3 else "P2", 128 * (c % 3), "RS", c)
+            if t == 0 and EARLY:
+                read(("P1", "P1", "P5", "P2")[c], 128 * (c == 1), "RS", c)
+            else:
+                read("P1" if c < 3 else "P2", 128 * (c % 3), "RS", c)
             read("P3", 128 * c, "RS%d" % t, c)
-        roll(t)
+            if t == 0 and EARLY and c == 1:
+                largest("P1", 0, 0, 256)
+                roll(t, 0, 16)
+        if t == 0 and EARLY:
+            largest("P5", 0, 256, 384)
+        else:
+            largest("P1", 0, 0, 384)
+        largest("P2", 0, 384, 512)
+        roll(t, 16 if t == 0 and EARLY else 0, 32)
         as_holder()
+        if t == 0:
+            later_constants()
         thresholds(t)
         for c in range(4):
             limits(t, c)
+        staying()
         logs()
         leave()
         new_places()
         winners()
         for j in range(4):
             close_up(j)
-        new_entries(t == 2)
+        new_entries()
         if t < 2:
             iota(A("PT", 0, 512), [[0, 512]], 0)
         for m in range(8):
-            move(m, "s" if t < 2 else "sv"[m & 1])
+            move(m, MOVERS[t][m], PIECES[t])
 
-    ts(A("YA"), A("O"), 255.5, Op.is_lt, 512.0, Op.mult)
-    ts(A("YB"), A("O"), -256.0, Op.add, 0.0, Op.max)
+    ts(A("YA"), A("O"), 255.0, Op.max, 767.0, Op.subtract)
     for h in range(2):
         mms((T.P0[:, h:16:2, :], [("P0", 0, 256, 1)]),
-            [(A("OUT%d%d" % (h, b)), A(n, 128 * b, 128 * b + 128)) for n in ("YA", "YB") for b in range(2)], more=h < 1)
+            [(A("OUT%d%d" % (h, b)), A("YA", 128 * b, 128 * b + 128)) for b in range(2)], more=h < 1)
     turn(A("YP"), A("P0", 0, 256))
-    gather(A("YO"), A("YP"), A("LY"), "s")
+    gather(A("YO"), A("YP"), A("LY"), "v")
     dmas("y", [(ext(T.yoc[:]), A("YO"))])
-    for h in range(2):
-        new_slots("YQ", h)
-        dmas("y", [(ext(T.yq[:, 256 * h:256 * h + 256]), A("YQ", 256 * h, 256 * h + 256))])
+    for piece, copy in zip(PIECES[2], COPIES):
+        new_slots("YQ", piece, act if copy == "s" else cp)
+        dmas("y", [(ext(T.yq[:, 64 * piece[1]:64 * piece[2]]), A("YQ", 64 * piece[1], 64 * piece[2]))])
     issue_all()
     for s in sorted(cnt):
         if known["g"].get(s, 0) < cnt[s]:

import math
from concourse.bass import DstId, RemoteDMATransfer
from concourse.mybir import dt, AluOpType as Op, ActivationFunctionType as Act, AxisListType as Ax

LN2 = math.log(2.0)
BF, F4, FH, I4, U2 = "bfloat16", "float32", "float16", "int32", "uint16"
WIDTH = {}
WHERE = {}
SCRATCH = {}


def _decl(dtype, spec):
    pool, at = "pool_" + dtype, 0
    for item in spec.split():
        n, w = item.split(":")
        WIDTH[n] = int(w)
        WHERE[n] = (pool, at)
        at += (int(w) + 15) // 16 * 16
    SCRATCH[pool] = ("sbuf", [128, at], dtype)


_decl(BF, "XT:4096 WI:512 WT:528 WG:4096 D0:4096 D1:4096 PT:768 AH:1536 CMP:528 EZ:432 BO:128 RS:8 RS0:8 RS1:8 RS2:8 RW:8 CADD:64 "
          "R01:256 BIG:16 CAT:256 EM:256 SW:128 GO:256 CN:256 AT:256 BL:512 YC:512 NE:32 TE:256 TH:256 VV:256 REP:128")
_decl(FH, "GS:8192 GE:8192 MG:4096 TT:512 SMX:512 PMN:512 THB:512 K1K:256 Q16:256 SUI:16 I4K:128 IN4K:128 UF:64 I16:128 IN16:128 I37:128 I2K:128 I8K:128 IN8K:128 I14:128 IPEN:128 IM2K:128 "
          "IM1K:128 IN37:128 IP1K:128 OP:256 ZS:128 YA:256 J16:128 NPL:512 Q1:256 XS:512 "
          "IN00:128 IN01:128 IN10:128 IN11:128 OUT00:128 OUT01:128 OUT10:128 OUT11:128")
_decl(I4, "OCN:256 QW:512 THI:16 QI:8 KI:8 H:512 HA:512 TM:32 UU:64 BT:256 BT2:256")
_decl(U2, "LC:16 LC2:32 LX:32 LR:32 LO:16 LY:16 OU:256 OU2:256 HU:512 SU:16 WL:512")
_decl(F4, "WD:4112 WE:4112 MT:528 IF:128 INF:128 ZF:128 TB:128 TI:128 TJ:128 TK:128 TL:128 ONE:128 TA:256 TC:16 TC2:16 "
          "KC:8 KW:16 WR:16 LIM:8 JW:8 BC:8 G0:8 RMX:512 RMN:512 RK:128 JC:16 XC:512 CF:512 C1:256 YP:256 YO:256 YQ:512 "
          "E1:128 EE:256 F:256 FS:128 EA:256 EH:256 KK:64 K:32 KQ:32 THP:48 W2:32 "
          "LT:128 PEN:128 K2:128 KM:128 PF:16 PM:16 PN:16 CV:16 ZP:16 ZW:16 LEN:16 XK:256 Y:272 LAND0:128 LAND1:128 LAND2:128")
SCRATCH["O"] = ("sbuf", [128, 16, 16], FH)
SCRATCH["T1"] = ("sbuf", [128, 16, 16], F4)
SCRATCH["O16"] = ("sbuf", [128, 8, 2, 16], FH)
SCRATCH["P0"] = ("psum", [128, 32, 16], F4)
SCRATCH["P6"] = ("psum", [128, 32, 16], F4)
for _n in ("P1", "P2", "P3", "P4", "P5", "P7"):
    SCRATCH[_n] = ("psum", [128, 512], F4)
    WIDTH[_n] = 512
    WHERE[_n] = (_n, 0)
SEMAPHORES = ["qv", "qs", "qt", "qg", "sent"] + ["arr%d" % t for t in range(4)] + ["d%d" % i for i in range(20)]

CYCLE, PE_CYCLE, GATHER, GATHER2, SCATTER = 0.83, 0.42, 1.25, 1.25, 3.2
CALL = {"v": 60.0, "s": 200.0, "g": 0.0}
BANK, PE_OUT = 60.0, 250.0
HOP, DMA, SEND, REMOTE = 100.0, 2200.0, 1000.0, 1200.0
AHEAD, SLACK, PATIENCE = 400.0, 50.0, 0.3
OWN, PASSES, GREEDY, SPANS = 60.0, 4, 2, []
ORDER = (2, 3, 0, 1)
SHARED = ((3,), (), ())
MID = 2040.0
MOVES = "WE"
MOVERS = [["ss"] + 7 * ["s"]] * 2 + ["svssvsvs"]
_LISTS = "OU T1 EM H H:256 HA HU "
_SCORES = "D02 D12 D03 D13 D00 D10 D01 D11 -PT SW EE EE:128 F -XS ZS WL FS GS1 WL:256 GS3 GS5 GS7 SMX OU2 SMX:384 LAND"
_KEYS = " PMN TM UU UU:32 UF KK TT K KQ BL AH:512 MG1 MG3"
_CLOSE = " K2 KM GO CN BT BT2 Y PF PM EH Y' PN SUI SU Y'' AT Y''' XK O"
VECTOR = ["-ZF -C1 -KI -KC -KW:12 -C1' -LO -C1'' -CF:256 -LR -T1 -OP -O16 -O " + _LISTS
          + "D02 D12 D03 D00 D10 -WR:5 D01 D11 -WL -LIM -KW:3 -KW:4 SW EE EE:128 F -LC2 -TK -TJ -LX -TJ:64 ZS FS -JW -JC -LIM:1 "
          + "GS1 GS3 GS5 SMX LAND GS7 SMX:256 OU2 SMX:384 LAND''" + _KEYS + " -KW:5 -KW:10 -KW:9" + _CLOSE,
          _LISTS + _SCORES + _KEYS + " --LY" + _CLOSE,
          _LISTS + _SCORES + _KEYS + _CLOSE + " PT GE1 XS YA GE4 GE6 YP YO YQ:384"]
_WANTS = "-GE0 WG2 -GE0b WG3 -GE1 WG0 -GE2 WG1 -GE3 E1 -GE4 -GE5 -GE6 -GE7 GS0 GS2 GS4 GS6"
_LIMITS = " MT:16 MG0 MG2 LT PEN"
_SHIFTS = " CMP:16 EA P1 P1' P1'' P1'''"
SCALAR = ["-P6 -CF -WD0 -WD0b -WT:16 -WD0b' -WD0b'' WG2 WG3 WG0 D13 WG1 D13' D13b -WD1 -WD2 E1 -WD0' -WD0b''' -WD0b'''' -RMX -RW -G0 "
          + "-XC -BC:1 -CAT -W2 -THP GS0 GS2 GS4 GS6 -THB NPL NPL:256 NPL:384 -BC:2 NE -R01 -WE0" + _LIMITS + " CF" + _SHIFTS,
          _WANTS + " CF NE" + _LIMITS + _SHIFTS,
          _WANTS + " NE" + _LIMITS + _SHIFTS + " GE0 GE2 GE3 GE5 GE7 YQ YQ:256"]
GPSIMD = ["-QI -WR:8 -TA -TC -TL -TL:96 -IF -IN00 -IN01 -IN10 -IN11 -IN37 -WT -EZ -TI:8 -TI:16 -EZ:15 -IPEN -I16 -CADD -TI:8' -TI:16' "
          + "-EZ:159 -IN16 -WR:1 LAND' LAND''' -Q16 -K1K -Y:256 -IN4K -CMP -WE1b -WE2b -WE3b -EZ:303 -TL:80 -PT -PT:512 -RS1 -RS2 "
          + "-OUT00 -OUT01 -OUT10 -OUT11", "", ""]
PIECES = [(("P4", 0, 4, 4), ("P5", 4, 8, 7))] * 2 + [(("P4", 0, 4, 3), ("P5", 4, 6, 4), ("P3", 6, 8, 6))]
COPIES = "ssv"
LIMITS = (0, 64, 128, 192, 256)
EARLY = True


def _bank(name):
    return name[0] == "P" and name[1:].isdigit()


def rank_program(g, core, T, topo):
    rank = T.rank_of(core)
    if rank is None:
        return
    Q = {"v": g.vector, "s": g.scalar, "t": g.tensor, "g": g, "y": g.sync}
    SEM = {"v": "qv", "s": "qs", "t": "qt", "g": "qg"}
    cnt = {}
    known = {q: {} for q in Q}
    snap = {}
    hist = {}

    def A(n, lo=0, hi=None, st=1):
        if n in ("P0", "P6", "O", "T1"):
            hi = 256 if hi is None else hi
            return (T[n][:, lo // 16:hi // 16, :], [(n, lo, hi, 1)])
        hi = WIDTH[n] if hi is None else hi
        buf, c0 = WHERE[n]
        ap = T[buf][:, c0 + lo:c0 + hi] if st == 1 else T[buf][:, c0 + lo:c0 + hi:st]
        return (ap, [(n, lo, hi, st)])

    def PART(n, p0, p1, ps=1, lo=0, hi=None, st=1):
        hi = WIDTH[n] if hi is None else hi
        buf, c0 = WHERE[n]
        return (T[buf][p0:p1:ps, c0 + lo:c0 + hi:st], [(n, lo, hi, st)])

    def M(ap, *names):
        return (ap, [(n, 0, 512, 1) for n in names])

    def whole(o):
        return (o[0], o[1] + [("open" + o[1][0][0], 0, 1, 1)])

    def IND(win, off):
        return (win[0].indirect(off[0]), win[1] + off[1], True)

    def clash(a, b):
        if a[1] <= b[0] or b[1] <= a[0]:
            return False
        return (a[0] - b[0]) % math.gcd(a[2], b[2]) == 0

    steps = []
    seen = {}
    group = []

    def before(log, q, reads, writes):
        out = []
        for regs, wr in ((reads, False), (writes, True)):
            for n, lo, hi, st in regs:
                bank = _bank(n)
                for (r2, tok, q2, w2) in log.get(n, []):
                    if bank and q2 != q or clash((lo, hi, st), r2) and (w2 or wr):
                        out.append((tok, q2))
        return out

    def note(log, q, reads, writes, tok):
        for n, lo, hi, st in reads:
            log.setdefault(n, []).append(((lo, hi, st), tok, q, False))
        for n, lo, hi, st in writes:
            keep = []
            for e in log.get(n, []):
                covered = st == 1 and lo <= e[0][0] and e[0][1] <= hi or e[0] == (lo, hi, st)
                if not (covered or log is hist and _bank(n) and e[2] != q):
                    keep.append(e)
            log[n] = keep + [((lo, hi, st), tok, q, True)]

    def step(q, time, reads, writes, go, later=0.0):
        k = len(steps)
        steps.append({"queue": q, "time": time, "later": later, "issue": go,
                      "before": sorted(set(p for p, _ in before(seen, q, reads, writes)))})
        note(seen, q, reads, writes, k)
        if q in "vsg" and writes:
            n, lo = ("LAND", 0) if writes[0][0].startswith("LAND") else writes[0][:2]
            n += str(lo // 1024) + "b" * (lo % 1024 > 0) if WIDTH.get(n, 0) >= 4096 else ":%d" % lo if lo else ""
            while (now[0], n) in names:
                n += "'"
            names[now[0], n] = k

    now, names = [-1], {}

    def in_order():
        for lists_ in (VECTOR, SCALAR, GPSIMD):
            line = [names[t - n.count("-"), n.lstrip("-")] for t in range(3) for n in lists_[t].split()]
            for p, k in zip(line, line[1:]):
                steps[k]["before"].append(p)

    def need(q, token):
        sem, n = token
        if known[q].get(sem, 0) >= n:
            return
        Q[q].wait_ge(T.sem[sem], n)
        for k2, v2 in snap[token].items():
            if known[q].get(k2, 0) < v2:
                known[q][k2] = v2
        known[q][sem] = n

    def deps(q, reads, writes, adds=False):
        best = {}
        for tok, q2 in before(hist, q, reads, writes):
            if not (q2 == q == "t" and (adds or tok[1] > cnt.get("qt", 0))):
                best[tok[0]] = max(best.get(tok[0], 0), tok[1])
        for s in sorted(best):
            need(q, (s, best[s]))

    def issue(q, call, reads, writes, inc=True, adds=False):
        deps(q, reads, writes, adds)
        sem = SEM[q]
        inst = call()
        tok = (sem, cnt.get(sem, 0) + 1)
        if inc:
            inst.then_inc(T.sem[sem], 1)
            cnt[sem] = tok[1]
            s = dict(known[q])
            s[sem] = tok[1]
            snap[tok] = s
        note(hist, q, reads, writes, tok)

    def run(q, call, reads, writes, time, line=()):
        time += CALL[q] + (BANK if any(_bank(r[0]) for r in reads + writes) else 0.0)
        step(q, time, reads, writes + list(line), lambda on: issue(on, call, reads, writes))

    def R(*ops):
        out = []
        for o in ops:
            if isinstance(o, tuple):
                out += o[1]
        return out

    def val(o):
        return o[0] if isinstance(o, tuple) else o

    def size(o):
        return math.prod(o[0].shape[1:])

    def cycles(n, *sides):
        narrow = all(WHERE.get(o[1][0][0], ("pool_" + FH,))[0][5:] in (BF, FH, U2) and not _bank(o[1][0][0]) for o in sides)
        return CYCLE * max(64, n / 2 if sides and narrow else n)

    def picked(a):
        return len(a) == 3

    def tt(o, a, b, op):
        n = size(o)
        time = GATHER2 * n if picked(a) else cycles(n if _bank(a[1][0][0]) or _bank(b[1][0][0]) else 2 * n)
        run("v", lambda: g.vector.tensor_tensor(o[0], a[0], b[0], op), R(a, b), o[1], time)

    def ts(o, a, s1, op0, s2=None, op1=None):
        time = GATHER * size(o) if picked(a) else cycles(size(o), o, a)
        if op1 is None:
            run("v", lambda: g.vector.tensor_scalar(o[0], a[0], val(s1), None, op0), R(a, s1), o[1], time)
        else:
            run("v", lambda: g.vector.tensor_scalar(o[0], a[0], val(s1), val(s2), op0, op1), R(a, s1, s2), o[1], time)

    def cp(o, a):
        run("v", lambda: g.vector.tensor_copy(o[0], a[0]), a[1], o[1], cycles(size(o), o, a))

    def scatter(win, off, a):
        run("v", lambda: g.vector.tensor_copy(win[0].indirect(off[0]), a[0]), R(a, off), win[1], SCATTER * size(a))

    def fill(o, c):
        run("v", lambda: g.vector.memset(o[0], c), [], o[1], cycles(size(o), o))

    def scan(o, d0, d1, init, op0, op1):
        run("v", lambda: g.vector.tensor_tensor_scan(o[0], d0[0], d1[0], init, op0, op1), R(d0, d1), o[1], cycles(size(o), o, d0, d1))

    def turn(o, a):
        run("v", lambda: g.vector.transpose(o[0], a[0]), a[1], o[1], cycles(size(o), o, a))

    def total(o, a):
        run("v", lambda: g.vector.tensor_reduce(o[0], a[0], Ax.X, Op.add), a[1], o[1], cycles(size(a)))

    def act(o, a, func=Act.Copy, bias=0.0, scale=1.0):
        run("s", lambda: g.scalar.activation(o[0], a[0], func, bias=val(bias), scale=val(scale)), R(a, bias, scale), o[1], cycles(size(o)))

    def gather(o, win, off, q, plus=0.0):
        a = IND(win, off)

        def go(on):
            if on == "s":
                issue(on, lambda: g.scalar.activation(o[0], a[0], Act.Copy, bias=plus), a[1], o[1])
            elif plus:
                issue(on, lambda: g.vector.tensor_scalar(o[0], a[0], plus, None, Op.add), a[1], o[1])
            else:
                issue(on, lambda: g.vector.tensor_copy(o[0], a[0]), a[1], o[1])
        step(q, 60.0 + GATHER * size(o), a[1], o[1], go)

    def mm(o, l, r, start=True, stop=True, more=False, cut=False):
        wide = WHERE.get(l[1][0][0], ("",))[0] == "pool_" + F4
        group.append((o, l, r, start, stop, PE_CYCLE * max(min(64, size(l)), size(r)) * (4 if wide else 1)))
        if stop and not more or cut:
            mine = list(group)
            del group[:]

            def go(on):
                for i, (o, l, r, start, stop, _) in enumerate(mine):
                    issue(on, lambda: g.tensor.matmul(o[0], l[0], r[0], start, stop), R(l, r), o[1][:1], stop or i == len(mine) - 1, not start)
            step("t", sum(m[5] for m in mine), sum([R(m[1], m[2]) for m in mine], []), sum([m[0][1] for m in mine], []), go, PE_OUT)

    def mms(o, pairs, start=True, stop=True, more=False, cut=False):
        for i, (l, r) in enumerate(pairs):
            last = i == len(pairs) - 1
            mm(o, l, r, start and i == 0, stop and last, more, cut and last)

    def iota(o, pattern, base, cm=0, small=True):
        time = 130.0 + 2 * CYCLE * size(o)
        if small:
            run("g", lambda: g.iota(o[0], pattern, base, cm, allow_small_or_imprecise_dtypes=True), [], o[1], time)
        else:
            run("g", lambda: g.iota(o[0], pattern, base, cm), [], o[1], time)

    def aff(o, a, pattern, op, fillv, base, cm):
        run("g", lambda: g.affine_select(o[0], a[0], pattern, op, fillv, base, cm), a[1], o[1], 170.0 + 2 * CYCLE * size(o))

    def const(o, v):
        aff(o, A("ZF", 0, size(o)), [[0, size(o)]], Op.not_equal, v, 0, 0)

    ndma = [0]

    def dmas(q, items, later=DMA):
        def go(on):
            sem = "d%d" % ndma[0]
            ndma[0] += 1
            tok = (sem, 16 * len(items))
            for o, a in items:
                deps(on, a[1], o[1])
                Q[on].dma_start(o[0], a[0]).then_inc(T.sem[sem], 16)
            cnt[sem] = tok[1]
            snap[tok] = dict(known[on])
            snap[tok][sem] = tok[1]
            for o, a in items:
                note(hist, on, a[1], o[1], tok)
        step(q, 50.0 * len(items), sum([a[1] for o, a in items], []), sum([o[1] for o, a in items], []), go, later)

    def issue_all():
        in_order()
        n = len(steps)
        after = [[] for _ in steps]
        for k, s in enumerate(steps):
            for p in s["before"]:
                after[p].append(k)
        line, left = [k for k in range(n) if not steps[k]["before"]], [len(s["before"]) for s in steps]
        for p in line:
            for k in after[p]:
                left[k] -= 1
                if not left[k]:
                    line.append(k)
        assert len(line) == n

        def gap(p, k):
            same = steps[p]["queue"] == steps[k]["queue"]
            return 0.0 if same and steps[p]["queue"] == "t" else steps[p]["later"] + (OWN if same else HOP)

        def place(order, back):
            end, taken = {}, {q: [] for q in Q}
            for k in order:
                d = steps[k]["time"]
                if back:
                    t = max([end[x] + gap(k, x) for x in after[k]] + [steps[k]["later"]])
                else:
                    t = max([end[p] + gap(p, k) for p in steps[k]["before"]] + [0.0])
                line = taken[steps[k]["queue"]]
                i = 0
                while i < len(line) and line[i][0] < t + d:
                    t = max(t, line[i][1])
                    i += 1
                line.insert(i, (t, t + d))
                end[k] = t + d
            return end

        def greedy(way):
            way = [1.0e9 - k if k < loads else way[k] for k in range(n)]
            end, free, left = {}, {q: 0.0 for q in Q}, [len(s["before"]) for s in steps]
            ready = {k: 0.0 for k in range(n) if not left[k]}
            while ready:
                can = {k: max(t, free[steps[k]["queue"]]) for k, t in ready.items()}
                q = steps[min(can, key=lambda k: (can[k] - (0.0 if steps[k]["queue"] == "v" else AHEAD), k))]["queue"]
                mine = sorted([k for k in can if steps[k]["queue"] == q], key=lambda k: (-way[k], k))
                first = min(can[k] for k in mine)
                best = [k for k in mine if can[k] <= first + SLACK][0]
                best = [k for k in mine if can[k] <= can[best] + PATIENCE * steps[best]["time"]][0]
                k = ([k for k in mine if can[k] + steps[k]["time"] <= can[best]] + [best])[0]
                end[k] = free[q] = can[k] + steps[k]["time"]
                del ready[k]
                for x in after[k]:
                    left[x] -= 1
                    if not left[x]:
                        ready[x] = max(end[p] + gap(p, x) for p in steps[x]["before"])
            return end

        way = {}
        for k in reversed(line):
            way[k] = steps[k]["time"] + max([way[x] + gap(k, x) for x in after[k]] + [steps[k]["later"]])
        best = None
        for turn_ in range(PASSES):
            end = greedy(way) if turn_ < GREEDY else place(sorted(range(n), key=lambda k: (k >= loads, -way[k] if k >= loads else k, k)), False)
            span = max(end[k] + steps[k]["later"] for k in range(n))
            SPANS.append(span)
            if best is None or span < best[0]:
                best = (span, end)
            way = place(sorted(range(n), key=lambda k: (-end[k], -k)), True)
        for k in sorted(range(n), key=lambda x: (best[1][x] - steps[x]["time"], x)):
            steps[k]["issue"](steps[k]["queue"])

    def ext(ap):
        return (ap, [])

    def ez(n, k):
        at = 144 * ("EZ1", "EZM", "EZR").index(n)
        return A("EZ", at + 15 - k, at + 143 - k)

    def rows(sel, n, lo, width):
        return [(ez(sel, r), A(n, lo + r, lo + width - 15 + r, 16)) for r in range(16)]

    dmas("y", [(A("OCN"), ext(T.oc[:]))])
    dmas("s", [(A("WI"), ext(T.want[:]))])
    dmas("y", [(A("XT"), ext(T.x[:]))], 5000.0)
    loads = len(steps)
    dmas("y", [(A("QW"), (T.qs[:], A("XT")[1])), (A("THI", 0, 1), ext(T.th[:]))])

    q1, kc, one = A("QI", 0, 1), A("KC", 0, 1), A("ONE")
    part = (1.5 - rank) / 8.0
    move_row = 1

    def to_window(win, row, x):
        dmas("y", [(PART(win, row, 128, 16, 0, 4096), x)])

    def constants():
        iota(q1, [[0, 1]], 0, 1, False)
        iota(A("ONE"), [[0, 128]], 1)
        fill(A("ZF"), 0.0)
        ts(A("KI", 0, 1), q1, 15, Op.bitwise_and)
        cp(kc, A("KI", 0, 1))
        for name, v in (("IF", 1.0), ("INF", -1.0), ("I16", 1.0), ("IN16", -1.0), ("I37", 37.0), ("I2K", 2048.0), ("I8K", 8192.0),
                        ("I4K", 4096.0), ("IN4K", -4096.0),
                        ("IN8K", -8192.0), ("I14", 16384.0), ("IPEN", -32768.0), ("IM2K", -1.0 / 2048), ("IM1K", -1.0 / 1024),
                        ("IN37", -37.0), ("IP1K", 1.0 / 1024)):
            aff(A(name), A("ZF"), [[-1, 128]], Op.not_equal, v, 0, 1)
        for h in range(2):
            for b in range(2):
                aff(A("IN%d%d" % (h, b)), A("ZF"), [[-32, 4], [1000, 2], [-2, 16]], Op.not_equal, 1.0, -b - 1000 * h, 1)
                aff(A("OUT%d%d" % (h, b)), A("ZF"), [[-32, 4], [-1, 16], [1000, 2]], Op.not_equal, -1.0, -16 * h - 1000 * b, 1)
        aff(A("J16"), A("ZF"), [[1, 128]], Op.not_equal, 1.0, -127, 1)
        aff(A("TB"), one, [[-16, 8], [0, 16]], Op.is_ge, 0.0, 0, 1)
        aff(A("BO"), A("TB"), [[16, 8], [0, 16]], Op.is_ge, 0.0, 15, -1)
        ones = A("BO", 0, 128, 16)

        def row(o, a, r, v):
            aff(o, a, [[-16, 8]], Op.not_equal, v, -r, 1)

        iota(A("EZ"), [[0, 432]], 0)
        for i, v in enumerate((1, -1)):
            iota(A("TI", 8, 16), [[0, 8]], v)
            aff(A("TI", 16, 24), A("TI", 8, 16), [[-16, 8]], Op.is_ge, 0.0, 0, 1)
            aff(A("EZ", 144 * i + 15, 144 * i + 143, 16), A("TI", 16, 24), [[16, 8]], Op.is_ge, 0.0, 15, -1)
        row(A("EZ", 288 + 15, 288 + 143, 16), A("ZF", 0, 8), move_row, -1.0)
        iota(A("CADD"), [[0, 64]], -int(MID))
        iota(A("TA"), [[1, 256]], 0)
        iota(A("TC"), [[2, 16]], 17)
        iota(A("WR", 8, 12), [[8, 4]], 8)
        ts(A("KW", 12, 16), A("WR", 8, 12), kc, Op.mult)
        k8, k16, k32 = A("KW", 12, 13), A("KW", 13, 14), A("KW", 15, 16)
        act(A("P6"), A("TA"), Act.Identity, bias=k32, scale=0.125)
        fill(A("C1"), 775.5)
        ts(A("C1", 0, 256, 16), A("TC"), 0.5, Op.mult, k16, Op.add)
        tt(A("C1"), A("C1"), A("P6"), Op.mult)
        act(A("CF", 0, 256), A("C1"), bias=37.0 * 767 - 15.0 / 32)
        ts(A("CF", 256, 512), A("C1"), 37.0 * 767 - 15.0 / 32, Op.add)
        fill(A("T1"), 0.0)
        iota(A("TL", 0, 16), [[1, 8], [128, 2]], 0)
        ts(A("LO"), A("TL", 0, 16), k8, Op.add)
        ts(A("OP"), IND(A("OCN"), A("LO")), -1.0, Op.mult, 767.0, Op.add)
        turn(M(T.O16[:], "O16"), A("OP"))
        iota(A("TL", 96, 128), [[-16, 32]], 511)
        ts(A("LR"), A("TL", 96, 128), kc, Op.subtract)
        gather(A("WT", 16, 528), A("WI"), A("LR"), "s")
        for b in range(2):
            mms(A("P1", 128 * b, 128 * b + 128), [(A("IN%d%d" % (h, b)), M(T.O16[:, :, h, :], "O16")) for h in range(2)], more=b < 1)
        cp(A("O"), A("P1", 0, 256))
        const(A("WT", 0, 16), 0.0)
        cp(A("WL"), A("QW"))

        row(A("TI", 0, 8), A("ZF", 0, 8), 0, 1.0)
        row(A("RS"), A("ZF", 0, 8), 0, 1.0)
        for t in range(3):
            row(A("RS%d" % t), A("TI", 0, 8), 5 + t, 1.0)
        act(A("WD", 0, 128), A("ZF"))
        for lo in (128, 256, 512, 1024, 2048):
            act(A("WD", lo, 2 * lo), A("WD", 0, lo))
        iota(A("WR", 1, 4), [[1, 3]], 5)
        ts(A("WR", 5, 8), A("WR", 1, 4), kc, Op.is_equal, -8192.0, Op.mult)
        for t in range(3):
            act(A("WD", 16 * t, 4096, 128), A("ZF", 0, 32), Act.Identity, bias=A("WR", 5 + t, 6 + t))
        iota(A("WD", 4096, 4112), [[0, 16]], -4096)
        act(A("WE", 0, 1028), A("XT", 0, 1028))
        for lo in range(1028, 4112, 1028):
            iota(A("WE", lo, lo + 1028), [[0, 1028]], 0)
        iota(A("RMN"), [[0, 512]], -1000000)
        const(A("RMN", 0, 512, 16), 1.0e6)
        act(A("RMX"), A("RMN"), scale=-1.0)
        act(A("R01"), A("RMX", 0, 256), Act.Relu, scale=1.0e-6)
        iota(A("YC"), [[1, 16], [0, 32]], 0)
        act(A("XC"), A("YC"), bias=part + 4096.0, scale=1.0 / 128)
        iota(A("Q1"), [[0, 256]], 1)
        iota(A("K1K"), [[0, 16], [-1024, 16]], 15360)
        iota(A("TC2"), [[-16, 16]], 1279)
        iota(A("BIG"), [[0, 16]], 65536)
        act(A("RW"), ones, scale=k16)
        for o in (A("AH", 0, 512), A("AH", 1024, 1536), A("PT", 0, 512), A("TT")):
            iota(o, [[0, 512]], 0)
        iota(A("PT", 512, 768), [[0, 256]], 0)
        iota(A("MT", 0, 16), [[0, 16]], 32768)
        iota(A("CMP", 0, 16), [[0, 16]], 1)
        iota(A("THP", 32, 48), [[0, 16]], 32768)
        iota(A("Q16"), [[0, 256]], 16)
        const(A("Y", 256, 272), 2.0 ** 25)
        iota(A("TL", 16, 48), [[1, 32]], 0)
        ts(A("KW", 3, 4), kc, 14.5, Op.is_lt)
        ts(A("KW", 4, 5), kc, 14.5, Op.is_gt, 32.0, Op.mult)
        ts(A("LC2"), A("TL", 16, 48), A("KW", 3, 4), Op.mult, A("KW", 4, 5), Op.add)
        ts(A("KW", 5, 6), A("KW", 3, 4), -8192.0, Op.mult)
        ts(A("KW", 10, 11), A("KW", 3, 4), 8192.0, Op.mult, 2048.0, Op.add)
        iota(A("TL", 48, 80), [[0, 16], [16, 2]], 0)
        ts(A("LX"), A("TL", 48, 80), kc, Op.add)
        ts(A("KW", 9, 10), kc, 7.5, Op.is_gt, -255.0, Op.mult)
        iota(A("TL", 80, 96), [[2, 16]], 0)
        ts(A("LY"), A("TL", 80, 96), k32, Op.add, A("KW", 9, 10), Op.add)
        iota(PART("VV", 0, 16), [[16, 16], [256, 16]], -4096)
        aff(PART("TE", 0, 16), PART("VV", 0, 16), [[0, 16], [1, 16]], Op.is_equal, 0.0, 1, -1)
        aff(PART("TE", 0, 16), PART("TE", 0, 16), [[0, 16], [1, 16]], Op.not_equal, 64.0, 0, -1)
        aff(PART("TH", 0, 16), PART("VV", 0, 16), [[0, 16], [1, 16]], Op.is_equal, 0.0, -15, -1)
        aff(PART("REP", 0, 16), PART("ZF", 0, 16), [[0, 8], [1, 16]], Op.not_equal, 1.0, 0, -1)
        mms(A("P7", 0, 256), [(PART("REP", 0, 16), PART(n, 0, 16)) for n in ("TE", "TH")])
        act(A("CAT"), A("P7", 0, 256))
        const(A("BC", 0, 1), 2.0 ** -63.2)
        act(A("BC", 1, 2), A("BC", 0, 1), Act.Ln)
        act(A("BC", 2, 3), A("BC", 1, 2), scale=2000.0)
        ts(A("JC"), A("TC2"), kc, Op.subtract)
        const(A("TI", 64, 128), 0.25)
        scan(A("TJ", 0, 64), A("TI", 64, 128), A("ZF", 0, 64), 2.0 ** 65, Op.mult, Op.max)
        tt(A("TK", 0, 64), A("IF", 0, 64), A("IF", 64, 128), Op.add)
        tt(A("TJ", 64, 128), A("TJ", 0, 64), A("TK", 0, 64), Op.mult)
        total(A("JW", 0, 1), A("TJ", 64, 128))
        const(A("RK"), 128.0 * 2 * LN2)
        const(A("RK", 4, 128, 8), -320.0 * 2 * LN2)
        const(A("RK", 0, 128, 8), -1.0e6)
        cp(A("LIM", 0, 1), A("THI", 0, 1))
        ts(A("LIM", 1, 2), A("THI", 0, 1), 0.5, Op.add)
        act(A("G0"), A("TI", 0, 8), scale=A("LIM", 0, 1))
        for c in range(4):
            mm(A("P7", 256 + 8 * c, 264 + 8 * c), one, A("G0"), more=True)
            mm(A("P7", 288 + 8 * c, 296 + 8 * c), A("WI", 128 * c, 128 + 128 * c), A("RW"), more=c < 3)
        act(A("THP", 0, 32), A("P7", 256, 288), bias=-MID)
        gather(A("THB"), A("THP"), A("LC2"), "s")
        act(A("W2"), A("P7", 288, 320), bias=MID + 8192.0)

    def later_constants():
        act(A("NPL", 0, 256), A("P6"), bias=-2048.0, scale=8.0)
        for b in range(2):
            act(A("NPL", 256 + 128 * b, 384 + 128 * b), A("NPL", 128 - 128 * b, 256 - 128 * b), scale=-1.0)

    def lists(t):
        o = A("O")
        ts(A("OU"), o, -240.0, Op.add)
        mm(whole(A("P0", 0, 512)), A("IF"), A("CF"), True, False, cut=True)
        if t < 2:
            act(A("CF"), A("CF"), bias=77.0)
        mm(whole(A("P0", 0, 256)), A("IN37"), o, False, False)
        for b in range(2):
            mm(whole(A("P0", 256 + 128 * b, 384 + 128 * b)), A("IN37"), A("O", 128 - 128 * b, 256 - 128 * b), False, b == 1)
        tt((T.T1[:, :, 1:16], [("T1", 0, 256, 1)]), (T.O[:, :, 0:15], o[1]), (T.P6[:, 0:16, 1:16], [("P6", 0, 256, 1)]), Op.mult)
        for b in range(2):
            tt(A("H", 256 * b, 256 * b + 256), A("P0", 256 * b, 256 * b + 256), A("T1"), Op.subtract)
        ts(A("HA"), A("H"), 4095, Op.bitwise_and)
        cp(A("HU"), A("HA"))
        ts(A("EM"), o, 255.5, Op.is_lt)

    def wants(c):
        gather(A("WG", 1024 * c, 1024 * c + 1024), A("WT"), A("OU", 64 * c, 64 * c + 64), "s")

    def minima(c, shared):
        w, lo, bank = A("WG", 1024 * c, 1024 * c + 1024), 1024 * c, "P3" if c & 2 else "P2"
        mate = A("HU", 256 + 64 * (c ^ 2), 320 + 64 * (c ^ 2))

        def d(x):
            return whole(A(bank, 64 * (x & 1), 64 * (x & 1) + 64))
        if not c & 1:
            mm(whole(A(bank, 0, 128)), A("IPEN"), A("EM", 64 * c, 64 * c + 128), True, False, cut=True)
        tt(A("D0", lo, lo + 1024), IND(A("XT"), A("HU", 64 * c, 64 * c + 64)), w, Op.min)
        mms(A("P1", 64 * c, 64 * c + 64), [(A("I16"), A("CADD"))] + rows("EZ1", "D0", lo, 1024), more=True)
        mms(d(c), rows("EZM", "D0", lo, 1024), False, False, cut=True)
        if c in shared:
            gather(A("D1", lo, lo + 1024), A("XT"), mate, "s")
            mms(d(c), rows("EZ1", "WG", lo, 1024), False, False, cut=True)
            for b, stage in enumerate(("P4", "P5")):
                piece = (lo + 512 * b, lo + 512 * b + 512)
                mms(A(stage), [(A("I16"), A("WG", *piece)), (A("IN16"), A("D1", *piece))])
                act(A("D1", *piece), A(stage), Act.Relu)
        else:
            tt(A("D1", lo, lo + 1024), IND(A("XT"), mate), w, Op.min)
        if c & 1:
            late = [x for x in (c - 1, c) if x in shared] + [x for x in (c,) if x not in shared]
            for x in late:
                mms(d(x), rows("EZM" if x in shared else "EZ1", "D1", 1024 * x, 1024), False, x == late[-1], cut=True)
        elif c not in shared:
            mms(d(c), rows("EZ1", "D1", lo, 1024), False, False, cut=True)
        if c == 3:
            act(A("E1"), A("P3", 0, 128), scale=-1.0)

    def decide():
        tt(A("SW"), A("P2", 0, 128), A("E1"), Op.is_gt)
        tt(A("EE", 0, 128), A("P2", 0, 128), A("SW"), Op.mult)
        tt(A("EE", 128, 256), A("P3", 0, 128), A("SW"), Op.mult)
        tt(A("F"), A("EE"), A("P1", 0, 256), Op.add)
        to_window("WD", 0, A("F"))

    def exchanged(more):
        mm(whole(A("P0", 256, 512)), A("I16"), A("O"), True, False)
        mm(whole(A("P0", 256, 384)), A("IN16"), A("ZS"), False, False)
        mm(whole(A("P0", 384, 512)), A("I16"), A("ZS"), False, not more, cut=True)
        if more:
            mms(whole(A("P0", 256, 512)), more, False, True)

    def exchange():
        mms(A("P0", 0, 128), [(A("I16"), A("O", 0, 128)), (A("IN16"), A("O", 128, 256))], more=True)
        mms(A("P0", 128, 256), [(A("IF"), A("F", 0, 128)), (A("INF"), A("F", 128, 256))])
        tt(A("ZS"), A("P0", 0, 128), A("SW"), Op.mult)
        tt(A("FS"), A("P0", 128, 256), A("SW"), Op.mult)
        exchanged([])
        ts(A("OU2"), A("P0", 256, 512), -240.0, Op.add)

    def by_slot(n, win, m, q, plus=0.0):
        w = 64 // len(q)
        for i, on in enumerate(q):
            lo = 64 * m + w * i
            gather(A(n, 16 * lo, 16 * lo + 16 * w), A(win), A("WL", lo, lo + w), on, plus)

    def read(bank, at, sel, c):
        for s in range(16):
            mm(A(bank, at + s, at + 128 - 15 + s, 16), A("GS", 2048 * c + s, 2048 * c + 2048 - 15 + s, 16), A(sel), more=s < 15)

    used, plan = [], []
    for d in sorted([d for d in T.cores if d != core], key=lambda d: len(topo.engines(core, d))):
        es = [e for e in topo.engines(core, d) if e not in used][:4]
        used += es
        plan.append((d, sum(1 << e for e in es), len(es)))

    best = A("SMX", 15, 512, 16)

    def largest(bank, at, lo, hi):
        scan(A("SMX", lo, hi), A("RMX", 0, hi - lo), A(bank, at, at + hi - lo), 0.0, Op.min, Op.max)

    def roll(t, lo, hi):
        land = "LAND%d" % t
        own = A(land, 32 * rank + lo, 32 * rank + hi)
        ts(own, A("SMX", 16 * lo + 15, 16 * hi, 16), part, Op.add, -3000.0, Op.max)
        others = [(land, 32 * r + lo, 32 * r + hi, 1) for r in range(4) if r != rank]

        def go(on):
            deps(on, own[1], [])
            tr = []
            tok = ("arr%d" % (t if hi == 32 else 3), sum([p[2] for p in plan]))
            for d, mask, ne in plan:
                rid, pid = topo.addr(d, core)
                tr.append(RemoteDMATransfer(dst_ids=[DstId(rid=rid, pnc=pid)], dma_engine_mask=mask, remote_sem=T.sem[tok[0]], src=own[0], dst=own[0]))
            g.remote_dma_fused(tr, local_sem=T.sem.sent)
            cnt["sent"] = cnt.get("sent", 0) + tok[1]
            cnt[tok[0]] = tok[1]
            snap[tok] = {tok[0]: tok[1]}
            note(hist, "net", [], others, tok)
        step("g", SEND, own[1], others, go, REMOTE)

    def as_holder():
        scan(A("PMN"), A("RMN"), A("P3"), 0.0, Op.max, Op.min)
        tt(A("TM"), best, A("W2"), Op.add)
        ts(A("UU", 0, 32), A("TM"), 0xF0, Op.bitwise_and)
        ts(A("UU", 32, 64), A("TM"), 15, Op.bitwise_and)
        cp(A("UF"), A("UU"))
        mms(A("P2", 416, 448), [(A("I16"), A("THB", 0, 512, 16)), (A("IN16"), best), (A("I16"), A("PMN", 15, 512, 16))])
        act(A("NE"), A("P2", 416, 448), Act.Sign, bias=MID + 0.5)
        mms(A("P2", 384, 416), [(A("I16"), best), (A("IM2K"), A("UF", 0, 32)), (A("I4K"), A("NE"))])
        mm(A("P7"), A("IN16"), A("YC"), True, False)
        for y in range(16):
            mm(A("P7", 32 * y, 32 * y + 32), A("I16"), A("UF", 32, 64), False, y == 15)
        ts(A("BL"), A("P7"), 0.0, Op.is_equal, A("JW", 0, 1), Op.mult)

    def staying():
        mms(A("P5"), [(A("I16"), A("THB")), (A("I16"), A("PMN"))], True, False)
        for s in range(15):
            mm(A("P5", s, 512, 16), A("IN16"), best, False, s == 14)
        act(A("CMP", 16, 528), A("P5"), Act.Sign, bias=MID + 0.5)

    def thresholds(t):
        land = "LAND%d" % t
        tt(A("KK"), A(land, 0, 64), A(land, 64, 128), Op.max)
        tt(A("TT", 0, 512, 16), A("KK", 0, 32), A("KK", 32, 64), Op.max)
        for c in range(4):
            mm(A("P1", 384 - 128 * c, 512 - 128 * c), A("TT", 128 * c, 128 * c + 128), A("J16"), more=c < 3)
        act(A("MT", 16, 528), A("P1"))
        tt(A("K"), A("KK", 0, 32), A("KK", 32, 64), Op.max)
        tt(A("KQ"), A("K"), A("P2", 384, 416), Op.subtract)
        tt(A("AH", 512, 1024), IND(A("KQ"), A("LX")), A("XC"), Op.is_equal)

    def limits(t, c):
        w = LIMITS[c:c + 2]
        gather(A("MG", 16 * w[0], 16 * w[1]), A("MT"), A("OU2", *w), "sv"[c & 1])
        if c == 0:
            mm(whole(A("P4", 0, 256)), A("INF"), A("F"), True, False)
            for b, l in enumerate(("IF", "INF")):
                mm(whole(A("P4", 128 * b, 128 * b + 128)), A(l), A("FS"), False, False)
            mm(whole(A("P4", 16 * t, 256, 128)), A("I16"), A("BIG", 0, 2), False, False, cut=True)
        mms(whole(A("P4", *w)), rows("EZ1", "MG", 16 * w[0], 16 * (w[1] - w[0])), False, c == 3, cut=c < 3)

    def logs():
        for j in range(2):
            for c in range(4):
                for x in range(8):
                    w0, a, col = 512 - 512 * (x & 1) + 8 * c + x, 32 * (x >> 1), 4 * j + c
                    reg = ("P3", 512, 640, 1) if (j, c, x) == (1, 0, 0) else ("P3", 512 + 128 * j + a + col, 513 + 128 * j + a + col, 1)
                    mm((PART("P3", a, a + 32, 1, col, 128 - 7 + col, 8)[0], [reg]),
                       PART("AH", 64 * j, 64 * j + 64, 1, w0, w0 + 1024 - 31, 32), PART("BL", 64 * j, 64 * j + 64, 1, 8 * c + x, 512, 32),
                       not x & 1, bool(x & 1), 8 * c + x < 31)
        act(A("LT"), A("P3", 0, 128), Act.Ln, bias=2.0 ** -64)
        act(A("PEN"), A("LT"), Act.Relu, bias=A("BC", 2, 3), scale=-2000.0)
        tt(A("K2"), A("LT"), A("PEN"), Op.subtract)
        scan(A("KM"), A("RK"), A("K2"), 0.0, Op.add, Op.max)

    def leave():
        ts(A("GO"), A("P4", 0, 256), A("LIM", 1, 2), Op.is_gt, 1024.0, Op.mult)
        exchanged([(A("I14"), A("GO"))])
        scan(A("CN"), A("R01"), A("GO"), 0.0, Op.mult, Op.add)
        ts(A("BT"), A("CN"), float(2 ** 13 + 2 ** 9 + 2 ** 5 + 2), Op.mult)
        ts(A("BT2"), A("BT"), 2 ** 23 + 2 ** 20 + 2 ** 17 + 2 ** 14, Op.bitwise_and)
        tt(A("Y", 0, 256), A("BT2"), A("P0", 256, 512), Op.add)

    def new_places():
        mm(whole(A("P2")), A("I16"), A("NPL"), True, False)
        for l in ("IN8K", "I2K"):
            mm(whole(A("P2", 256, 512)), A(l), A("Q1", 0, 256), False, False)
        for b in range(4):
            mm(whole(A("P2", 128 * b, 128 * b + 128)), A("I8K"), A("SW"), False, False, cut=b == 3)
        for l, m, n in (("I37", "IN37", "GO"), ("IM1K", "IP1K", "CN")):
            mm(whole(A("P2", 0, 256)), A(l), A(n), False, False)
            for b in range(2):
                mm(whole(A("P2", 256 + 128 * b, 384 + 128 * b)), A(m), A(n, 128 - 128 * b, 256 - 128 * b), False, n == "CN" and b == 1, cut=b == 1)
        act(A("EA"), A("P2", 0, 256), Act.Relu, bias=2048.0, scale=-1.0)
        tt(A("EH"), A("EA"), A("P2", 256, 512), Op.max)
        to_window(MOVES, move_row, A("EH"))

    def close_up(j):
        act(A("P1", 0, 272), A("Y"), Act.Abs, bias=-2.0 ** (23 - 3 * j))
        if j == 3:
            tt(A("XK"), A("Y", 0, 256), A("P3", 0, 256), Op.min)
        tt(A("O") if j == 3 else A("Y", 0, 256), A("XK") if j == 3 else A("Y", 0, 256), A("P1", 1 << j, 256 + (1 << j)), Op.min)

    def winners():
        left = A("CN", 15, 256, 16)
        ts(A("PF"), left, 0.5, Op.is_lt, 1.0e4, Op.mult)
        tt(A("PM"), A("KM", 7, 128, 8), A("PF"), Op.subtract)
        ts(A("PN"), A("PM"), 0.5 / LN2, Op.mult, 1280.0 + 31.4, Op.add)
        tt(A("SUI"), A("PN"), A("JC"), Op.max)
        mm(whole(A("P3", 0, 256)), A("I16"), A("K1K"), True, False)
        for k in range(16):
            mm(whole(A("P3", k, 256, 16)), A("IN16"), left, False, False, cut=k == 15)
        for k in range(16):
            mm(whole(A("P3", k, 256, 16)), A("I16"), A("SUI"), False, k == 15)

    def new_entries():
        ts(A("SU"), A("SUI"), -1.0, Op.mult, 1280.0 + 511.0, Op.add)
        mm(A("P5", 0, 256), A("I16"), A("Q16"), True, False)
        for k in range(16):
            mm(A("P5", k, 256, 16), A("IM1K"), A("CN", 15, 256, 16), False, k == 15)
        tt(A("AT"), A("P5", 0, 256), A("CAT"), Op.min)
        scatter(A("PT"), A("SU"), A("AT"))
        mm(whole(A("P7")), A("I16"), A("AH", 0, 512), True, False)
        for c in range(4):
            o = whole(A("P7", 128 * c, 128 * c + 128))
            mm(o, A("CMP", 16 + 128 * c, 144 + 128 * c), A("I4K"), False, False)
            mm(o, A("CMP", 15 + 128 * c, 143 + 128 * c), A("IN4K"), False, False, cut=c == 3)
        mm(whole(A("P7")), A("BO"), A("PT", 0, 512), False, True)
        ts(A("XS"), A("P7"), A("KW", 5, 6), Op.min, A("KW", 10, 11), Op.add)

    def move(m, q, last):
        bank, lo, hi, news = [x for x in last if x[1] <= m < x[2]][0]
        o, new = whole(A(bank, 0, 64 * (hi - lo))), (A("I16"), A("XS", 64 * lo, 64 * hi))
        by_slot("GE", MOVES, m, q, -2048.0)
        if m == lo:
            mm(o, *(new if news == lo else (A("I16"), A("AH", 0, 64 * (hi - lo)))), True, False, cut=news == lo)
        elif m == news:
            mm(o, *new, False, False, cut=True)
        mms(whole(A(bank, 64 * (m - lo), 64 * (m - lo) + 64)), rows("EZR", "GE", 1024 * m, 1024), False, m == hi - 1 and news < hi, cut=True)
        if m == hi - 1 and news == hi:
            mm(o, *new, False, True)

    def new_slots(out, piece, copy):
        bank, lo, hi, _ = piece
        copy(A(out, 64 * lo, 64 * hi), A(bank, 0, 64 * (hi - lo)))

    constants()
    for t in range(3):
        now[0] = t
        lists(t)
        for c in ORDER:
            wants(c)
            minima(c, SHARED[t])
        decide()
        exchange()
        for piece in PIECES[t - 1] if t else ():
            new_slots("WL", piece, cp)
        for c in range(4):
            for m in (2 * c, 2 * c + 1):
                by_slot("GS", "WD", m, "sv"[m & 1])
            if t == 0 and EARLY:
                read(("P1", "P1", "P5", "P2")[c], 128 * (c == 1), "RS", c)
            else:
                read("P1" if c < 3 else "P2", 128 * (c % 3), "RS", c)
            read("P3", 128 * c, "RS%d" % t, c)
            if t == 0 and EARLY and c == 1:
                largest("P1", 0, 0, 256)
                roll(t, 0, 16)
        if t == 0 and EARLY:
            largest("P5", 0, 256, 384)
        else:
            largest("P1", 0, 0, 384)
        largest("P2", 0, 384, 512)
        roll(t, 16 if t == 0 and EARLY else 0, 32)
        as_holder()
        if t == 0:
            later_constants()
        thresholds(t)
        for c in range(4):
            limits(t, c)
        staying()
        logs()
        leave()
        new_places()
        winners()
        for j in range(4):
            close_up(j)
        new_entries()
        if t < 2:
            iota(A("PT", 0, 512), [[0, 512]], 0)
        for m in range(8):
            move(m, MOVERS[t][m], PIECES[t])

    ts(A("YA"), A("O"), 255.0, Op.max, 767.0, Op.subtract)
    for h in range(2):
        mms((T.P0[:, h:16:2, :], [("P0", 0, 256, 1)]),
            [(A("OUT%d%d" % (h, b)), A("YA", 128 * b, 128 * b + 128)) for b in range(2)], more=h < 1)
    turn(A("YP"), A("P0", 0, 256))
    gather(A("YO"), A("YP"), A("LY"), "v")
    dmas("y", [(ext(T.yoc[:]), A("YO"))])
    for piece, copy in zip(PIECES[2], COPIES):
        new_slots("YQ", piece, act if copy == "s" else cp)
        dmas("y", [(ext(T.yq[:, 64 * piece[1]:64 * piece[2]]), A("YQ", 64 * piece[1], 64 * piece[2]))])
    issue_all()
    for s in sorted(cnt):
        if known["g"].get(s, 0) < cnt[s]:
            g.wait_ge(T.sem[s], cnt[s])
